import numpy as np, ml_dtypes
CORES = [1,5,17,21,33,37,49,53]
N = 8
BF = ml_dtypes.bfloat16
W, M, TV, S, B = 2560, 256, 4, 3, 1
QN = W // 16
def parts(rng):
    X = rng.integers(0, 256, (N, 8, 16, W)); z = rng.integers(0, 256, (N, 8, 16, M))
    o = np.argsort(rng.random((8, W)), axis=1); A, H, Q = o[:, :8], o[:, 8:40], o[:, 40:40 + QN]; gi = np.arange(8)[None, :, None, None]
    e = rng.integers(0, W, (N, 8, 16, W)); l = rng.integers(0, W, (N, 8, 16, M))
    e = np.where(rng.random(e.shape) < 0.2, H[gi, rng.integers(0, 32, e.shape)], e)
    l[:, :, 0] = H[gi[..., 0], rng.integers(0, 32, (N, 8, M))]
    for q in range(N):
        for g in range(8):
            lanes = rng.permutation(16)[:8]; sub = e[q, g]; sub[lanes[:, None], Q[g][None, :]] = A[g][:, None]
    barred = rng.random((N, 8, M)) < 0.06; barred[:, :, 5] = True
    lb = Q[gi, rng.integers(0, QN, (N, 8, 16, M))]; lb[:, :, 0] = A[gi[..., 0], rng.integers(0, 8, (N, 8, M))]
    keep = (rng.random((N, 8, 1, M)) < 0.5) & (np.arange(16)[None, None, :, None] == rng.integers(1, 16, (N, 8, 1, M)))
    l = np.where(barred[:, :, None, :] & ~keep, lb, l)
    return X, e, l, z, rng.integers(800, 1501, (N, 8))
def pack(X, e, l, z, th):
    return {"xt": np.ascontiguousarray(X.reshape(N, 128, W)).astype(np.float32).astype(BF), "ex": np.ascontiguousarray(e.reshape(N, 128, W)).astype(np.int32),
            "l0": np.ascontiguousarray(l.reshape(N, 128, M)).astype(np.int32), "z0": np.ascontiguousarray(z.reshape(N, 128, M)).astype(np.float32).astype(BF),
            "th": np.ascontiguousarray(th.reshape(N, 8, 1)).astype(np.int32)}
def setup_inputs(rng):
    return pack(*parts(rng))
def setup_inputs_spread(rng):
    def skew(top, rows, n):
        return np.minimum((top * rng.random((N, 8, rows, n)) ** np.exp2(rng.integers(-3, 4, (N, 8, 1, n)))).astype(np.int64), top - 1)
    return pack(skew(256, 16, W), skew(W, 16, W), skew(W, 16, M), skew(256, 16, M), rng.integers(0, 4081, (N, 8)))
def setup_inputs_ends(rng):
    ends = np.array([0, W - 1])
    def bits(n):
        u = rng.random((N, 8, 1, n)); return np.where(u < 0.3, 0, np.where(u < 0.6, 255, 255 * rng.integers(0, 2, (N, 8, 16, n))))
    X = bits(W); z = bits(M); sw = (np.arange(N)[:, None, None] + np.arange(8)[None, :, None]) % 2
    X[..., 0] = 255 * sw; X[..., W - 1] = 255 * (1 - sw); z[..., M - 1] = 0; z[..., 0] = 255
    u = rng.random((N, 8, 1, W)); u[..., 0] *= 0.7; u[..., W - 1] *= 0.7
    e = np.where(u < 0.25, 0, np.where(u < 0.5, W - 1, np.where(u < 0.7, ends[rng.integers(0, 2, (N, 8, 16, W))], rng.integers(0, W, (N, 8, 16, W)))))
    l = np.where(rng.random((N, 8, 16, M)) < 0.7, ends[rng.integers(0, 2, (N, 8, 16, M))], rng.integers(0, W, (N, 8, 16, M)))
    l[:, :, [2, 7, 15], M - 1] = W - 1; l[:, :, 0, M - 1] = 0
    th = np.stack([rng.permutation(np.array([0, 4080] * 4)) for q in range(N)]); th[N - 1] = np.array([0, 4080] * 4)
    return pack(X, e, l, z, th)
def setup_inputs_corners(rng):
    X, e, l, z, th = parts(rng); v = [int(a) for a in rng.permutation(8)]; i = np.arange(M); c = np.arange(W)
    e[:, v[0]] = np.where(rng.random((N, 16, W)) < 0.5, c, e[:, v[0]])
    l[:, v[0]] = np.where(rng.random((N, 16, M)) < 0.4, l[:, v[0], :1], l[:, v[0]]); l[:, v[0], :, ::8] = l[:, v[0], :1, ::8].copy()
    th[:, v[0]] = 4080
    o = rng.permutation(W); A, full, free = o[:8], o[8:8 + W // 2], o[8 + W // 2:]
    for g in (v[1], v[2]):
        e[:, g] = rng.choice(free, (N, 16, W))
        for q in range(N):
            lanes = rng.permutation(16)[:8]; sub = e[q, g]; sub[lanes[:, None], full[None, :]] = A[:, None]
        l[:, g] = rng.choice(full, (N, 16, M)); l[:, g, 0] = rng.choice(A, (N, M))
    l[:, v[2], 1 + i % 15, i] = rng.choice(free, (N, M)); j = i[1::2]
    l[:, v[2], 1 + (j + 7) % 15, j] = rng.choice(free, (N, len(j)))
    th[:, v[1]] = rng.choice(np.array([1, 4079]), N)
    l[:, v[3], 1:] = rng.integers(0, W, (N, 1, M)); th[:, v[3]] = 0
    X[:, v[4]] = X[:, v[4], :, :4].copy()[:, :, rng.integers(0, 4, W)]
    tips = np.array([0, 1, W - 2, W - 1]); e[:, v[5]] = rng.choice(tips, (N, 16, W)); l[:, v[5]] = rng.choice(tips, (N, 16, M))
    l[:, v[6], 1:] = rng.choice(o[-3:], (N, 15, M)); th[:, v[6]] = 4080
    e[:, v[7]] = (c[None, :] + 1 + np.arange(16)[:, None]) % W; l[:, v[7]] = rng.integers(W - 20, W, (N, 16, M))
    return pack(X, e, l, z, th)
def setup_inputs_crowd(rng):
    X, e, l, z, th = parts(rng); X = np.minimum(np.maximum(X, 1), 254)
    sizes = rng.permutation(np.array([1, 2, 3, 16, 64, 256, W, W]))
    for g in range(8):
        pool = rng.permutation(W)[:int(sizes[g])]
        e[:, g] = rng.choice(pool, (N, 16, W)); l[:, g, 1:] = rng.choice(pool, (N, 15, M))
    th[::2] = 4080; th[1::2] = 0
    return pack(X, e, l, z, th)
def setup_inputs_lull(rng):
    X = np.zeros((N, 8, 16, W), np.int64); e = np.zeros((N, 8, 16, W), np.int64); l = rng.integers(0, W, (N, 8, 16, M)); z = rng.integers(107, 149, (N, 8, 16, M))
    for g in range(8):
        o = rng.permutation(W); bar, grey = int(o[0]), int(o[1]); dl, dh, bl, bh = [o[2 + j::4] for j in range(4)]
        dark = np.concatenate([dl, dh]); bright = np.concatenate([bl, bh]); low = np.concatenate([dl, bl]); high = np.concatenate([dh, bh, o[:2]])
        x = X[:, g]; s = e[:, g]; m = l[:, g]; v = z[:, g]
        x[:, :, dark] = rng.integers(60, 101, (N, 16, len(dark))); x[:, :, bright] = rng.integers(155, 196, (N, 16, len(bright)))
        x[:, :, bar] = 255 * rng.integers(0, 2, (N, 16)); x[:, :, grey] = rng.integers(107, 149, (N, 16))
        s[:, :, low] = rng.choice(dark, (N, 16, len(low))); s[:, :, high] = rng.choice(bright, (N, 16, len(high)))
        s[:, 1, high] = rng.choice(bl, (N, len(high))); s[:, 2, high] = rng.choice(bh, (N, len(high)))
        np.put_along_axis(s, rng.integers(3, 15, (N, 1, W)), bar, 1)
        m[:, 0] = bar; m[:, 1] = np.stack([rng.permutation(low)[:M] for q in range(N)]); m[:, 2] = rng.choice(high[:-2], (N, M))
        m[:, 3:, 3::16] = grey; m[:, 4:, 11::16] = grey
        v[:, :, 3::16] = x[:, :, grey][:, :, None]; v[:, :, 11::16] = x[:, :, grey][:, :, None]
    th = np.zeros((N, 8), np.int64); th[::2] = rng.integers(1310, 1361, th[::2].shape); th[::2, rng.permutation(8)[:3]] = 4080
    return pack(X, e, l, z, th)
def check_inputs(d):
    bad = []
    for k, lo, hi in (("xt", 0, 255), ("ex", 0, W - 1), ("l0", 0, W - 1), ("z0", 0, 255), ("th", 0, 4080)):
        v = np.asarray(d[k]).astype(np.float64)
        if not (np.min(v) >= lo and np.max(v) <= hi): bad.append("range of " + k)
        elif not np.all(v == np.floor(v)): bad.append("whole numbers of " + k)
    return bad
def pick(w, ix):
    return np.take_along_axis(w, ix.reshape(8, 1, -1), 2).reshape((8, 16) + ix.shape[1:])
def at(l, k):
    return np.take_along_axis(l, k[:, None, :], 1)[:, 0]
def reference(xt, ex, l0, z0, th):
    X = xt.astype(np.float32).astype(np.int32).reshape(N, 8, 16, W); R = ex.astype(np.int64).reshape(N, 8, 16, W)
    L = l0.astype(np.int64).reshape(N, 8, 16, M); Z = z0.astype(np.float32).astype(np.int32).reshape(N, 8, 16, M); limit = th.astype(np.int64).reshape(N, 8, 1)
    count = [0] * N; kk = np.arange(16)[None, :, None]; gg = np.arange(8)[:, None] + np.zeros((8, M), np.int64); ii = np.arange(M)[None, :] + np.zeros((8, M), np.int64)
    for t in range(TV):
        for h in range(N):
            q = (h + S * t) % N; x = X[q]; l = L[h].copy(); z = Z[h].copy()
            d = np.add.reduce(np.abs(pick(x, l) - z[:, :, None, :]), axis=1).astype(np.int64)
            conf = np.any(pick(R[q], l) == l[:, None, :1, :], axis=1)
            key = np.where(conf, 2 ** 16 + kk, 16 * d + kk); key[:, 0] = 2 ** 20
            o = np.argsort(key, axis=1, kind="stable"); ra = o[:, 0]; rb = o[:, 1]
            la = at(l, ra); lb = at(l, rb); e = []
            Ea = pick(R[q], la); Eb = pick(R[q], lb)
            for E in (Ea, Eb):
                de = np.add.reduce(np.abs(pick(x, E) - z[:, :, None, :]), axis=1)
                e.append(at(E, np.argmin(de, axis=1)))
            far = 16 * d + 15 - kk; far[:, 0] = -1
            np.put_along_axis(far, ra[:, None, :], -1, 1); np.put_along_axis(far, rb[:, None, :], -1, 1)
            new = l.copy()
            for v in e:
                p = np.argmax(far, axis=1); np.put_along_axis(far, p[:, None, :], -1, 1); np.put_along_axis(new, p[:, None, :], v[:, None, :], 1)
            xa = pick(x, e[0]); xb = pick(x, e[1])
            acc = np.add.reduce(np.abs(xa - xb), axis=1) < limit[q] + (count[h] & 63)
            new[:, 1:] = np.where(acc[:, None, :], Eb[:, 1:], new[:, 1:])
            first = np.full((8, W), M); np.minimum.at(first, (gg[acc], la[acc]), ii[acc])
            win = acc & (first[gg, la] == ii)
            R[q][gg[win], (ii[win] + t) & 15, la[win]] = l[:, 0][win]
            L[h] = new; Z[h] = (xa + xb) >> 1; count[h] = int(np.count_nonzero(acc))
    home = [(q - S * (TV - 1)) % N for q in range(N)]
    return {"yl": L[home].reshape(N, 128, M).astype(np.float32), "yz": Z[home].reshape(N, 128, M).astype(np.float32).astype(BF),
            "yr": np.add.reduce(R.reshape(N, 128, B, W // B), axis=2).astype(np.float32)}

@@ -1,0 +1,656 @@
+import numpy as np
+from concourse.bass import DstId, RemoteDMATransfer
+from concourse.mybir import dt, AluOpType, AxisListType, ActivationFunctionType
+
+OP = AluOpType
+AF = ActivationFunctionType
+W, M, HM, TV, STEP = 2560, 256, 128, 4, 3
+BIG, FARK, CONF = 4194304.0, 1048576.0, 131072.0
+CEN, TCEN = 1280.0, 2040.0
+MAGIC = 12582912.0
+GC = 1.5
+CYC = 0.83
+HOP = 80.0
+HELP = 200.0
+PIECES = 1
+CUT = {(1, 1): 2, (0, 1): 2}
+EARLY = {'reps_l01': 300, 'count': -1300, 'bits1': 9000, 'sel30': 6400, 'sel21': 100, 'far0': 23300, 'sel20': 6700, 'reps_l00': 100,
+         'phase1x1': -300, 'far1': 400, 'limits': -8000, 'rvals0': -6000, 'phase20': -6000, 'phase21': -2000, 'reps_z0': -300,
+         'phase1r1': 4000, 'sel31': 1900, 'rupd1': 1000, 'sel11': 3300, 'sel10': 9700, 'rupd0': 2000, 'reps_z1': -4600, 'phase1x0': 1000,
+         'bits0': -3300, 'upd0': -300, 'rvals1': -3300, 'upd1': 300}
+BYPE = ((0, 0),)
+
+SCRATCH, BANK, ORDER = {}, {}, {}
+
+
+WHAT, AT = {}, {}
+
+
+def _buf(name, shape, dtype, where="sbuf"):
+    WHAT[name] = (where, shape, dtype)
+    if where == "psum" or len(shape) > 2 or shape[1] > 2048:
+        SCRATCH[name] = WHAT[name]
+        return
+    host = "all_" + dtype
+    at = SCRATCH[host][1][1] if host in SCRATCH else 0
+    AT[name] = (host, at)
+    SCRATCH[host] = ("sbuf", [128, at + -(-shape[1] // 64) * 64], dtype)
+
+
+def _declare():
+    B, F, H, I, U = "bfloat16", "float32", "float16", "int32", "uint16"
+    sq = [128, 128]
+    for n, s, d in (("XW", [128, W], B), ("RI", [128, W], I), ("RW", [128, W + M], F), ("LI", [128, M], I)):
+        _buf(n, s, d)
+    for t in range(TV):
+        for n, d in (("LF", U), ("LC", H), ("ZB", B), ("LFo", U), ("LCo", H), ("ZBo", B), ("L0B", F)):
+            _buf("%s%d" % (n, t), [128, M], d)
+        _buf("CN%d" % t, [128, 1], F)
+        _buf("CNo%d" % t, [128, 1], F)
+    for h in range(2):
+        for n, s, d in (("L0R", [128, 2048], F), ("ZR", [128, 2048], B), ("GX", [128, 2048], B), ("AD", [128, 2048], B), ("CF", [128, 2048], B),
+                        ("DA", [128, 2048], B), ("DB", [128, 2048], B), ("KEY", sq, F), ("LOSE", sq, F), ("KF", sq, F), ("LS", sq, F),
+                        ("M1", sq, F), ("M2", sq, F), ("MF", sq, F), ("MG", sq, F), ("KE", [128, 256], F), ("OAB", [128, 256], B),
+                        ("OL", [128, 256], H), ("LOF", [128, 16], U), ("EU", [128, 256], U), ("EC", [128, 256], H), ("ME", [128, 256], F),
+                        ("OE", [128, 256], B), ("OEE", [128, 256], H), ("LEF", [128, 16], U), ("XE", [128, 256], B), ("AE", sq, B),
+                        ("ACT", sq, B), ("ACN", sq, B), ("FF", [128, 256], B), ("FN", [128, 256], B), ("UU", [128, 256], H),
+                        ("KL", sq, H), ("TT", sq, F), ("BI", sq, I), ("WM", sq, B)):
+            _buf("%s_%d" % (n, h), s, d)
+    for n, s, d in (("FTe", [128, 256], B), ("FTo", [128, 256], B), ("EQ", [128, 3072], B), ("LAD", [128, 16], F), ("SCF", [128, 16], F),
+                    ("SCG", [128, 16], F), ("SCU", [128, 16], U), ("EAM", [128, 256], F), ("L0S", [128, 256], F), ("THT", sq, F),
+                    ("THN", sq, F), ("COLS", [128, 16], F), ("NI", [128, 1], I), ("LY", [128, 256], F), ("IA", sq, I), ("IB", sq, I),
+                    ("IC", sq, I), ("ID", [128, 264], I), ("IP", [128, 16], I), ("IQ", [128, 16], I), ("IG", [8, 128], I), ("IE", [128, 1], I),
+                    ("DELTA", sq, B), ("BOb", sq, B), ("BOh", sq, H), ("Ib", sq, B), ("NIb", sq, B), ("HIb", sq, B), ("Ih", sq, H),
+                    ("NIh", sq, H), ("QB", sq, B), ("TRI", sq, B), ("NDEL", sq, B), ("ONb", sq, B), ("ONh", sq, H), ("SB", [128, 264], F),
+                    ("NSB", [128, 264], F), ("SEL0", sq, H), ("BLK", [128, 16], B), ("BLKC", [128, 8], B), ("CK", [128, 256], B),
+                    ("CKE", [128, 256], B), ("BC", [128, 16], U), ("CC", sq, F), ("RMIN", [128, 256], F), ("RMAX", sq, F),
+                    ("SELA", [128, 16, 128], H), ("PW", [128, 16], F), ("PX", [128, 16], F), ("DUM", [128, 16], F), ("DMC", [128, 16], F),
+                    ("GB8", [8, 128], H), ("THI", [8, 1], I), ("THF", [8, 1], F), ("THH", [8, 1], H), ("THG", [8, 128], H)):
+        _buf(n, s, d)
+    for n, s, k in (("P0", [128, 512], 0), ("P1", [128, 512], 1), ("PB_0", [128, 512], 2), ("PB_1", [128, 512], 3), ("P4", [128, 512], 4), ("P5", [128, 512], 5), ("P6", [128, 512], 6), ("P7", [128, 512], 7)):
+        _buf(n, s, F, "psum")
+        BANK[n] = k
+
+
+_declare()
+SEMAPHORES = ["sV", "sS", "sP", "sG", "snt"] + ["ld%d" % i for i in range(12)]
+for _t in range(1, TV):
+    SEMAPHORES += ["l0%d" % _t, "cn%d" % _t] + ["z%d_%d" % (_t, h) for h in range(2)] + ["l%d_%d" % (_t, h) for h in range(2)]
+SCOL, CME, CCE, CMO, CCO, CP0, CNEG, CTH0, CTH, CNR, CM15 = range(11)
+
+
+def rank_program(g, core, T, topo):
+    rank = T.rank_of(core)
+    if rank is None:
+        return
+    N = len(T.cores)
+    V, S, P = g.vector, g.scalar, g.tensor
+    ops, hist, ndma, stage = [], {}, [0], ["start"]
+    full = slice(None)
+
+    def v(name, *idx):
+        where, shape, dtype = WHAT[name]
+        sl = list(idx) + [full] * (len(shape) - len(idx))
+        lo = hi = 0
+        n, stride, lane = 1, 1, None
+        for d in range(len(shape) - 1, 0, -1):
+            a, b, st = sl[d].indices(shape[d]) if isinstance(sl[d], slice) else (sl[d], sl[d] + 1, 1)
+            c = (b - a + st - 1) // st
+            lo += a * stride
+            hi += (a + (c - 1) * st) * stride
+            n *= c
+            if d == len(shape) - 1 and st == 16:
+                lane = a % 16
+            stride *= shape[d]
+        if name in AT:
+            host, at = AT[name]
+            a, b, st = sl[1].indices(shape[1])
+            p0, p1, _ = sl[0].indices(shape[0])
+            ap = T[host][p0:p1, at + a:at + b:st]
+        else:
+            ap = T[name][tuple(sl)]
+        return {"ap": ap, "name": name, "lo": lo, "hi": hi + 1, "lane": lane, "n": n,
+                "psum": where == "psum", "two": dtype in ("bfloat16", "float16", "uint16")}
+
+    def cols(name, lo, hi, st=1):
+        return v(name, full, slice(lo, hi, st))
+
+    def col(j):
+        return cols("COLS", j, j + 1)
+
+    def ind(win, off):
+        return {"ap": win["ap"].indirect(off["ap"]), "parts": [win, off], "n": 16 * off["n"], "psum": False, "two": False, "ind": True}
+
+    def flat(aps):
+        out = []
+        for a in aps:
+            if isinstance(a, dict):
+                out += a["parts"] if "parts" in a else [a]
+        return out
+
+    def hit(a, b):
+        return a[5] == b[5] and a[2] < b[3] and b[2] < a[3] and (a[4] is None or b[4] is None or a[4] == b[4])
+
+    def op(eng, cost, reads, writes, fns, **kw):
+        i = len(ops)
+        o = {"i": i, "eng": eng, "cost": cost, "stage": stage[0], "fns": fns, "deps": set(), "order": set(kw.pop("after", ()))}
+        o.update(kw)
+        for a, wr in [(a, 0) for a in flat(reads)] + [(a, 1) for a in flat(writes)]:
+            key = BANK.get(a["name"], a["name"])
+            me = (i, wr, a["lo"], a["hi"], a["lane"], a["name"])
+            old = hist.setdefault(key, [])
+            if a["psum"] and eng == "P":
+                for e in old:
+                    if e[0] != i:
+                        o["order" if ops[e[0]]["eng"] == "P" else "deps"].add(e[0])
+                hist[key] = [e for e in old if e[0] == i] + [me]
+                continue
+            keep = []
+            for e in old:
+                if e[0] != i:
+                    if a["psum"] and ops[e[0]]["eng"] != eng:
+                        o["deps"].add(e[0])
+                    elif (wr or e[1]) and hit(me, e):
+                        o["deps"].add(e[0])
+                        if wr and a["lane"] is None and not a["psum"] and a["lo"] <= e[2] and e[3] <= a["hi"]:
+                            continue
+                keep.append(e)
+            keep.append(me)
+            hist[key] = keep
+        ops.append(o)
+        return i
+
+    def cyc(n, half):
+        return max(64, n * (0.5 if half else 1)) * CYC + 60
+
+    def tt(out, a, b, o):
+        if "ind" in out:
+            c = 50 + out["n"] * 3.5 * CYC
+        elif "ind" in a:
+            c = 50 + a["n"] * GC * CYC
+        else:
+            c = cyc(a["n"], False) if (a["psum"] or b["psum"]) else cyc(2 * a["n"], False)
+        return op("V", c, [a, b], [out], [lambda: V.tensor_tensor(out["ap"], a["ap"], b["ap"], o)])
+
+    def ts(out, a, s1, o1, s2=None, o2=None):
+        def f():
+            x1 = s1["ap"] if isinstance(s1, dict) else s1
+            x2 = s2["ap"] if isinstance(s2, dict) else s2
+            if o2 is None:
+                return V.tensor_scalar(out["ap"], a["ap"], x1, None, o1)
+            return V.tensor_scalar(out["ap"], a["ap"], x1, x2, o1, o2)
+        return op("V", cyc(a["n"], a["two"] and out["two"]), [a, s1, s2], [out], [f])
+
+    def cp(out, a):
+        c = 50 + a["n"] * GC * CYC if "ind" in a else cyc(a["n"], a["two"] and out["two"])
+        return op("V", c, [a], [out], [lambda: V.tensor_copy(out["ap"], a["ap"])])
+
+    def fill(out, x):
+        return op("V", cyc(out["n"], out["two"]), [], [out], [lambda: V.memset(out["ap"], x)])
+
+    def scan(out, d0, d1, o0, o1):
+        return op("V", cyc(d0["n"], False), [d0, d1], [out], [lambda: V.tensor_tensor_scan(out["ap"], d0["ap"], d1["ap"], 0.0, o0, o1)])
+
+    def total(out, a):
+        return op("V", cyc(a["n"], False), [a], [out], [lambda: V.tensor_reduce(out["ap"], a["ap"], AxisListType.X, OP.add)])
+
+    def act(out, a, f, **kw):
+        c = (65 + a["n"] * GC * CYC) if "ind" in a else a["n"] * CYC + 100
+        return op("S", c, [a] + list(kw.values()), [out],
+                  [lambda: S.activation(out["ap"], a["ap"], f, **{k: (x["ap"] if isinstance(x, dict) else x) for k, x in kw.items()})])
+
+    def either(out, a):
+        k = "ind" in a
+        cv = 50 + a["n"] * GC * CYC if k else cyc(a["n"], a["two"] and out["two"])
+        cs = 65 + a["n"] * GC * CYC if k else a["n"] * CYC + 100
+        return op("VS", cv, [a], [out], [lambda: S.activation(out["ap"], a["ap"], AF.Copy)], costs={"V": cv, "S": cs},
+                  alt=[lambda: V.tensor_copy(out["ap"], a["ap"])])
+
+    def pe(*mms):
+        c = sum(max(64, m[2]["n"]) * CYC + 5 for m in mms)
+        return op("P", c, [x for m in mms for x in (m[1], m[2])], [m[0] for m in mms],
+                  [(lambda m=m: P.matmul(m[0]["ap"], m[1]["ap"], m[2]["ap"], m[3], m[4])) for m in mms])
+
+    def iota(out, pat, base, cm, small=False):
+        def f():
+            if small:
+                return g.iota(out["ap"], pat, base, cm, allow_small_or_imprecise_dtypes=True)
+            return g.iota(out["ap"], pat, base, cm)
+        return op("G", 130 + 2 * out["n"] * CYC, [], [out], [f])
+
+    def dma(q, out, a, reads=(), writes=(), cost=2500):
+        k = ndma[0]
+        ndma[0] += 1
+        f = {"Y": lambda: g.sync.dma_start(out, a), "S": lambda: S.dma_start(out, a),
+             "G": lambda: g.dma_start(out, a, allow_slow_non_contiguous=True)}[q]
+        return op(q, 60, list(reads), list(writes), [f], dmasem="ld%d" % k, lat=cost)
+
+    def send(items, sem, dsts=None, cost=1200):
+        dsts = dsts or [T.cores[(rank + STEP) % N]] * len(items)
+        at, tr = 0, []
+        for it, d in zip(items, dsts):
+            tr.append((it, topo.addr(d), sum(1 << e for e in topo.engines(core, d)[at:at + it[2]])))
+            at += it[2]
+
+        def f():
+            if len(tr) == 1:
+                it, (rid, pid, _), mk = tr[0]
+                g.remote_dma(it[1]["ap"], it[0]["ap"], T.sem[sem[0]], T.sem["snt"], pid, rid, mk)
+            else:
+                g.remote_dma_fused([RemoteDMATransfer(dst_ids=[DstId(rid=ad[0], pnc=ad[1])], dma_engine_mask=mk, remote_sem=T.sem[sem[j % len(sem)]],
+                                                      src=it[0]["ap"], dst=it[1]["ap"]) for j, (it, ad, mk) in enumerate(tr)], local_sem=T.sem["snt"])
+        s = op("G", cost, [it[0] for it in items], [], [f], remote=at)
+        for j, sm in enumerate(sem):
+            mine = [it for q, it in enumerate(items) if q % len(sem) == j]
+            op("R", 0, [], [it[1] for it in mine], [], arr=(sm, sum(it[2] for it in mine)), after=[s], pre=2500)
+
+    H = [slice(0, HM), slice(HM, M)]
+    def load(q, name, src, cost=2500):
+        dma(q, v(name)["ap"], T[src][:], writes=[v(name)], cost=cost)
+    load("Y", "LI", "l0", 2200)
+    load("Y", "XW", "xt", 4500)
+    load("S", "ZB0", "z0")
+    load("S", "RI", "ex", 8000)
+    load("G", "THI", "th")
+
+    one = slice(0, 1)
+    iota(v("IC"), [[-1, 128]], 0, 1)
+    iota(v("IB"), [[-16, 8], [0, 16]], 0, 1)
+    iota(v("IA"), [[0, 8], [-1, 16]], 16, 1)
+    iota(v("IG"), [[1, 128]], 0, -16)
+    iota(v("CK", one, slice(0, 128)), [[0, 8], [1, 16]], 0, 0, True)
+    iota(v("CK", one, slice(128, 256)), [[0, 8], [-1, 16]], 16, 0, True)
+    iota(v("CC"), [[0, 8], [1, 16]], 65536, 0, True)
+    iota(v("CKE", one), [[0, 16], [1, 16]], 0, 0, True)
+    iota(v("IP"), [[0, 16]], 0, 1)
+    iota(v("IQ"), [[16, 16]], W, 0)
+    iota(v("ID"), [[-1, 264]], 512, 1)
+    cp(v("LF0"), v("LI"))
+    ts(v("LC0"), v("LI"), -CEN, OP.add)
+    ts(v("Ib"), v("IC"), 0, OP.is_equal)
+    ts(v("NIb"), v("IC"), 0, OP.is_equal, -1.0, OP.mult)
+    ts(v("IA"), v("IA"), 15, OP.bitwise_and)
+    ts(v("DELTA"), v("IA"), 0, OP.is_equal)
+    ts(col(CP0), cols("IA", 0, 1), 0, OP.is_equal)
+    ts(v("IB"), v("IB"), 4, OP.arith_shift_right)
+    ts(v("BOb"), v("IB"), 0, OP.is_equal)
+    ts(v("BOh"), v("IB"), 0, OP.is_equal)
+    ts(v("SEL0"), v("BOh"), col(CP0), OP.mult)
+    ts(cols("BLK", 0, 8), cols("BOb", 0, 128, 16), 16.0, OP.mult)
+    ts(cols("BLK", 8, 16), cols("BOb", 0, 128, 16), 16.0, OP.mult)
+    ts(v("BLKC"), cols("BOb", 0, 128, 16), CONF, OP.mult)
+    fill(v("CK", one, slice(0, 128, 16)), FARK)
+    fill(v("CK", one, slice(128, 256, 16)), 0.0)
+    fill(cols("CC", 0, 128, 16), FARK)
+    fill(v("ONb"), 1.0)
+    fill(v("RMIN"), 0.0)
+    fill(cols("RMIN", 0, 256, 16), BIG)
+    fill(v("RMAX"), 1.0)
+    fill(cols("RMAX", 0, 128, 16), 0.0)
+    ts(v("BC"), v("IQ"), 15 - W, OP.add)
+    for h in range(2):
+        fill(cols("LOSE_%d" % h, 0, 1), BIG)
+        fill(cols("LS_%d" % h, 0, 1), 0.0)
+    cp(cols("RW", 0, W), v("RI"))
+    ts(v("Ih"), v("IC"), 0, OP.is_equal)
+    ts(v("NIh"), v("IC"), 0, OP.is_equal, -1.0, OP.mult)
+    fill(v("SELA"), 0.0)
+    for a in range(16):
+        cp(v("SELA", full, a, slice(a, 128, 16)), cols("BOh", a, 128, 16))
+    ts(v("HIb"), v("IC"), 0, OP.is_equal, 0.5, OP.mult)
+    ts(v("NDEL"), v("IA"), 0, OP.not_equal)
+    fill(v("QB"), -1.0 / 512)
+    ts(v("TRI"), v("IC"), 0, OP.is_ge, -2.0, OP.mult)
+    ts(v("ID"), v("ID"), 15, OP.bitwise_and)
+    ts(v("SB"), v("ID"), 0, OP.is_equal)
+    ts(v("NSB"), v("ID"), 0, OP.not_equal)
+    for j in range(12):
+        fill(cols("PW", j, j + 1), float(2 ** (11 - j)))
+    fill(cols("PW", 12, 16), 0.0)
+    tt(v("PX"), v("PW"), cols("DELTA", 0, 16), OP.mult)
+    total(col(SCOL), v("PX"))
+    ts(v("IE"), cols("IP", 0, 1), 4, OP.arith_shift_right, 1, OP.bitwise_and)
+    ts(col(CME), v("IE"), 0, OP.is_equal, 1.0 / 1024, OP.mult)
+    ts(col(CCE), v("IE"), 0, OP.is_equal, -1.0, OP.mult)
+    ts(col(CMO), v("IE"), 1.0 / 1024, OP.mult)
+    ts(col(CCO), v("IE"), -1.0, OP.mult)
+    fill(col(CM15), -15.0)
+    ts(v("IP"), v("IP"), 15, OP.bitwise_and)
+    tt(v("DUM"), v("IP"), v("IQ"), OP.add)
+    ts(v("DMC"), v("DUM"), -1.0, OP.mult, CEN, OP.add)
+    ts(v("IG"), v("IG"), 4, OP.arith_shift_right)
+    ts(v("GB8"), v("IG"), 0, OP.is_equal)
+    ts(v("THF"), v("THI"), -TCEN, OP.add)
+    ts(v("THH"), v("THI"), -TCEN, OP.add)
+    ts(v("THG"), v("GB8"), v("THF"), OP.mult)
+    fill(v("ONh", slice(0, 8)), 1.0)
+    pe((cols("P7", 0, 128), v("ONh", slice(0, 8)), v("THG"), True, True))
+    ts(v("THT"), cols("P7", 0, 128), TCEN, OP.add)
+    pe((cols("P7", 128, 129), v("GB8"), v("THH"), True, True))
+    ts(col(CNEG), col(CP0), -100000.0, OP.mult)
+    ts(col(CTH0), cols("P7", 128, 129), TCEN, OP.add, col(CNEG), OP.add)
+    pe((cols("P6", 0, 256), v("SEL0"), v("LC0"), True, True))
+    act(v("L0B0"), cols("P6", 0, 256), AF.Copy, bias=CEN)
+    send([(v("L0B0"), v("L0B%d" % t), 2) for t in range(1, TV)], ["l0%d" % t for t in range(1, TV)],
+         [T.cores[(rank + STEP * t) % N] for t in range(1, TV)])
+
+    def hc(name, h, lo=0, hi=None):
+        if name == "PU":
+            return cols("PB_%d" % h, 256 + lo, 256 + hi)
+        return cols("%s_%d" % (name, h), lo, hi if hi else WHAT["%s_%d" % (name, h)][1][1])
+
+    def last(name, h, n=128):
+        return ind(hc(name, h), cols("BC", 0, n // 16))
+
+    def reps_l0(t, h):
+        for k in range(1 if t else 0, 16):
+            either(cols("L0R_%d" % h, k, 2048, 16), v("L0B%d" % t, full, H[h]))
+
+    def reps_z(t, h):
+        for k in range(16):
+            either(cols("ZR_%d" % h, k, 2048, 16), v("ZB%d" % t, full, H[h]))
+
+    def far_off(t, h, off, o0, G, AD, k0):
+        for q in range(PIECES):
+            a, b = HM * q // PIECES, HM * (q + 1) // PIECES
+            either(cols(G, 16 * a, 16 * b), ind(v("XW"), cols(off, o0 + a, o0 + b)))
+        for c in range(4):
+            ks = [k for k in range(4 * c, 4 * c + 4) if k >= k0]
+            for k in ks:
+                o = cols("P%d" % (c % 2), 128 * (k % 4), 128 * (k % 4) + 128)
+                pe((o, v("Ib"), cols(G, k, 2048, 16), True, False), (o, v("NIb"), v("ZB%d" % t, full, H[h]), False, True))
+            lo, hi = ks[0], ks[-1] + 1
+            act(cols(AD, 128 * lo, 128 * hi), cols("P%d" % (c % 2), 128 * (lo % 4), 128 * (hi - 4 * c)), AF.Abs)
+
+    def phase1x(t, h):
+        AD, PB = "AD_%d" % h, "PB_%d" % h
+        far_off(t, h, "LF%d" % t, HM * h, "GX_%d" % h, AD, 1)
+        pe((cols(PB, 0, 256), v("ONb", one), v("CK", one), True, False))
+        for k in range(1, 16):
+            pe((cols(PB, k, 256, 16), cols(AD, 128 * k, 128 * k + 128), v("BLK"), False, False))
+
+    def phase1r(t, h):
+        tt(hc("CF", h), ind(cols("RW", 0, W), v("LF%d" % t, full, H[h])), hc("L0R", h), OP.is_equal)
+        pe(*[(cols("PB_%d" % h, k, 128, 16), cols("CF_%d" % h, k, 2048, 16), v("BLKC"), False, k == 15) for k in range(1, 16)])
+
+    def pp(h, lo, hi):
+        return cols("P5" if h else "P6", lo, hi)
+
+    def lists(h, src, out, extra=None):
+        o = pp(h, 256, 272)
+        pe(*[(o, v("SELA", full, a), cols(src, a, 256, 16), a == 0, a == 15) for a in range(16)])
+        ts(v(out), o, CEN, OP.add)
+        if extra:
+            tt(cols("LAD", 8 * h, 8 * h + 8), pp(h, 256, 264), cols("DMC", 8 * h, 8 * h + 8), OP.add)
+
+    def sel1(t, h):
+        tt(hc("KEY", h), cols("PB_%d" % h, 0, 128), v("CC"), OP.min)
+        scan(hc("M1", h), cols("RMIN", 0, 128), hc("KEY", h), OP.max, OP.min)
+        tt(hc("LOSE", h, 1, 128), hc("KEY", h, 1, 128), hc("M1", h, 0, 127), OP.max)
+        tt(hc("OAB", h, 0, 128), last("M1", h), hc("KEY", h), OP.is_equal)
+        scan(hc("M2", h), cols("RMIN", 0, 128), hc("LOSE", h), OP.max, OP.min)
+        tt(hc("OAB", h, 128, 256), last("M2", h), hc("KEY", h), OP.is_equal)
+        for l in range(2):
+            p = pp(h, 128 * l, 128 * l + 128)
+            pe((p, hc("OAB", h, 128 * l, 128 * l + 128), v("Ib"), True, True))
+            tt(hc("OL", h, 128 * l, 128 * l + 128), p, v("LC%d" % t, full, H[h]), OP.mult)
+        lists(h, "OL_%d" % h, "LOF_%d" % h, True)
+        cp(hc("EU", h), ind(cols("RW", 0, W), hc("LOF", h)))
+        ts(hc("EC", h), hc("EU", h), -CEN, OP.add)
+        tt(hc("KF", h), last("M2", h), hc("KEY", h), OP.is_lt)
+
+    def far(t, h):
+        tt(hc("KF", h), cols("PB_%d" % h, 128, 256), hc("KF", h), OP.mult)
+        scan(hc("MF", h), v("RMAX"), hc("KF", h), OP.mult, OP.max)
+        tt(hc("LS", h, 1, 128), hc("KF", h, 1, 128), hc("MF", h, 0, 127), OP.min)
+        tt(hc("FF", h, 0, 128), last("MF", h), hc("KF", h), OP.is_equal)
+        scan(hc("MG", h), v("RMAX"), hc("LS", h), OP.mult, OP.max)
+        tt(hc("FF", h, 128, 256), last("MG", h), hc("KF", h), OP.is_equal)
+        f = [hc("FF", h, 0, 128), hc("FF", h, 128, 256)]
+        pe(*[(cols("P7", 128 * l, 128 * l + 128), f[l], v("Ib"), True, True) for l in range(2)])
+        act(hc("FN", h), cols("P7", 0, 256), AF.Copy)
+        keep = cols("P7", 256, 384)
+        pe((keep, f[0], v("NIb"), True, False), (keep, f[1], v("NIb"), False, False), (keep, v("ONb", one), v("ONb", one), False, True))
+        tt(hc("KL", h), keep, v("LC%d" % t, full, H[h]), OP.mult)
+
+    def bits(t, h):
+        p = cols("P7", 384, 512)
+        pe((p, v("BOh"), hc("OL", h, 0, 128), True, True))
+        BI = hc("BI", h)
+        ts(BI, p, CEN, OP.add, col(SCOL), OP.mult)
+        ts(BI, BI, 2048, OP.bitwise_and)
+        ts(v("FTe", full, H[h]), BI, col(CME), OP.mult, col(CCE), OP.add)
+        ts(v("FTo", full, H[h]), BI, col(CMO), OP.mult, col(CCO), OP.add)
+        for q in range(4):
+            mm, n = [], 0
+            for F in ("FTe", "FTo"):
+                for hp in range(h + 1):
+                    o, ps = cols("P%d" % (q % 2), n, n + 128), slice(32 * q, 32 * q + 32)
+                    if hp == h:
+                        mm.append((o, v("Ib"), v("TRI"), True, False))
+                    mm.append((o, v(F, ps, H[hp]), v(F, ps, H[h]), hp != h, True))
+                    n += 128
+            pe(*mm)
+            c = 1024 * h + n * q
+            act(cols("EQ", c, c + n), cols("P%d" % (q % 2), 0, n), AF.Relu, bias=col(CM15))
+
+    def phase2(t, h):
+        for l, D in enumerate(("DA", "DB")):
+            e = hc("EU", h, 128 * l, 128 * l + 128)
+            if (h, l) in BYPE:
+                far_off(t, h, "EU_%d" % h, 128 * l, "GX_%d" % h, "%s_%d" % (D, h), 0)
+            else:
+                cut = CUT.get((h, l), 1)
+                for q in range(cut):
+                    a, b = HM * q // cut, HM * (q + 1) // cut
+                    d = hc(D, h, 16 * a, 16 * b)
+                    tt(d, ind(v("XW"), hc("EU", h, 128 * l + a, 128 * l + b)), hc("ZR", h, 16 * a, 16 * b), OP.subtract)
+                    act(d, d, AF.Abs)
+        pe((cols("P4", 0, 256), v("ONb", one), v("CKE", one), True, False))
+        for l, D in enumerate(("DA", "DB")):
+            D = "%s_%d" % (D, h)
+            pe(*[(cols("P4", 128 * l + j, 128 * l + 128, 16), cols(D, 128 * j, 128 * j + 128) if (h, l) in BYPE else cols(D, j, 2048, 16),
+                  cols("BLK", 0, 8), False, l == 1 and j == 15) for j in range(16)])
+
+    def sel2(t, h):
+        act(hc("KE", h), cols("P4", 0, 256), AF.Copy)
+        scan(hc("ME", h), v("RMIN"), hc("KE", h), OP.max, OP.min)
+        tt(hc("OE", h), last("ME", h, 256), hc("KE", h), OP.is_equal)
+
+    def sel3(t, h):
+        pe(*[(pp(h, 128 * l, 128 * l + 128), hc("OE", h, 128 * l, 128 * l + 128), v("Ib"), True, True) for l in range(2)])
+        tt(hc("OEE", h), pp(h, 0, 256), hc("EC", h), OP.mult)
+        lists(h, "OEE_%d" % h, "LEF_%d" % h)
+        cp(hc("XE", h), ind(v("XW"), hc("LEF", h)))
+        pe((pp(h, 0, 256), v("BOh"), hc("OEE", h), True, True))
+        tt(hc("UU", h), pp(h, 0, 256), hc("FN", h), OP.mult)
+        xa, xb = hc("XE", h, 0, 128), hc("XE", h, 128, 256)
+        p0, p1 = hc("PU", h, 0, 128), hc("PU", h, 128, 256)
+        pe((p0, v("Ib"), xa, True, False), (p0, v("NIb"), xb, False, True))
+        act(hc("AE", h), p0, AF.Abs)
+        pe((p0, v("BOb"), hc("AE", h), True, True))
+        pe((p1, hc("AE", h), v("BOb"), True, True))
+
+    def upd(t, h):
+        p0, p1 = hc("PU", h, 0, 128), hc("PU", h, 128, 256)
+        xa, xb = hc("XE", h, 0, 128), hc("XE", h, 128, 256)
+        ts(hc("ACN", h), p0, col(CTH), OP.is_lt)
+        u, w = pp(h, 0, 128), pp(h, 128, 256)
+        ua, ub, kl = hc("UU", h, 0, 128), hc("UU", h, 128, 256), hc("KL", h)
+        pe((u, v("Ih"), kl, True, False), (u, v("Ih"), ua, False, False), (u, v("Ih"), ub, False, True),
+           (w, v("Ih"), hc("EC", h, 128, 256), True, False), (w, v("NIh"), kl, False, False), (w, v("NIh"), ua, False, False), (w, v("NIh"), ub, False, True))
+        tt(hc("TT", h), w, hc("ACN", h), OP.mult)
+        lc, lf = v("LCo%d" % t, full, H[h]), v("LFo%d" % t, full, H[h])
+        tt(lc, u, hc("TT", h), OP.add)
+        if t < TV - 1:
+            ts(lf, lc, CEN, OP.add)
+            send([(lf, v("LF%d" % (t + 1), full, H[h]), 4), (lc, v("LC%d" % (t + 1), full, H[h]), 4)], ["l%d_%d" % (t + 1, h)])
+        else:
+            ts(v("LY", full, H[h]), lc, CEN, OP.add)
+        tt(hc("ACT", h), p1, v("THN"), OP.is_lt)
+        p0 = hc("PU", h, 0, 128)
+        pe((p0, v("HIb"), xa, True, False), (p0, v("HIb"), xb, False, False), (p0, v("QB"), v("ONb"), False, True))
+        zo = v("ZBo%d" % t, full, H[h])
+        ts(zo, p0, MAGIC, OP.add, -MAGIC, OP.add)
+        if t < TV - 1:
+            send([(zo, v("ZB%d" % (t + 1), full, H[h]), 8)], ["z%d_%d" % (t + 1, h)])
+
+    def rvals(t, h):
+        i0 = HM * h + t
+        tt(v("EAM", full, H[h]), ind(cols("RW", 0, W), hc("LOF", h, 0, 8)), cols("NSB", i0, i0 + HM), OP.mult)
+        tt(v("L0S", full, H[h]), v("L0B%d" % t, full, H[h]), cols("SB", i0, i0 + HM), OP.mult)
+
+    def rupd(t, h):
+        P_ = "P5" if h else "P7"
+        eq = lambda gg, hp: 1024 * h + 128 * ((h + 1) * gg + hp)
+        pe((cols(P_, 0, 128), v("Ib"), v("NDEL"), True, False),
+           *[(cols(P_, 16 * gg, 16 * gg + 16), cols("EQ", eq(gg, hp), eq(gg, hp) + 128),
+              hc("ACT", hp, 16 * gg, 16 * gg + 16), False, gg == 7 and hp == h) for gg in range(8) for hp in range(h + 1)])
+        tt(hc("WM", h), hc("ACT", h), cols(P_, 0, 128), OP.is_gt)
+        pe((cols(P_, 256, 264), hc("WM", h), cols("BOb", 0, 128, 16), True, True))
+        c = slice(8 * h, 8 * h + 8)
+        tt(v("SCF", full, c), cols(P_, 256, 264), v("LAD", full, c), OP.mult)
+        tt(v("SCG", full, c), v("SCF", full, c), v("DUM", full, c), OP.add)
+        cp(v("SCU", full, c), v("SCG", full, c))
+        tt(ind(v("RW"), v("SCU", full, c)), v("EAM", full, H[h]), v("L0S", full, H[h]), OP.add)
+
+    def count(t):
+        p = cols("P7", 288, 296)
+        pe(*[(p, v("ONb"), cols("ACT_%d" % h, 0, 128, 16), h == 0, h == 1) for h in range(2)])
+        total(col(CNR), p)
+        cp(v("NI"), col(CNR))
+        ts(v("NI"), v("NI"), 63, OP.bitwise_and)
+        cp(v("CNo%d" % t), v("NI"))
+        send([(v("CNo%d" % t), v("CN%d" % (t + 1)), 1)], ["cn%d" % (t + 1)])
+
+    def do(part, name, t, h):
+        stage[0] = name + str(h)
+        part(t, h)
+
+    for h in range(2):
+        do(reps_l0, "reps_l0", 0, h)
+    for t in range(TV):
+        for h in range(2):
+            do(phase1x, "phase1x", t, h)
+        for h in range(2):
+            do(phase1r, "phase1r", t, h)
+            if t + 1 < TV:
+                do(reps_l0, "reps_l0", t + 1, h)
+        for h in range(2):
+            do(reps_z, "reps_z", t, h)
+            do(sel1, "sel1", t, h)
+            if h:
+                do(sel2, "sel2", t, 0)
+            do(phase2, "phase2", t, h)
+            do(far, "far", t, h)
+            do(bits, "bits", t, h)
+            do(rvals, "rvals", t, h)
+        do(sel2, "sel2", t, 1)
+        stage[0] = "limits"
+        if t:
+            ts(v("THN"), v("THT"), v("CN%d" % t), OP.add)
+            ts(col(CTH), col(CTH0), v("CN%d" % t), OP.add)
+        else:
+            cp(v("THN"), v("THT"))
+            cp(col(CTH), col(CTH0))
+        for h in range(2):
+            do(sel3, "sel3", t, h)
+            do(upd, "upd", t, h)
+            do(rupd, "rupd", t, h)
+        if t + 1 < TV:
+            stage[0] = "count"
+            count(t)
+        else:
+            dma("Y", T["yl"][:], v("LY")["ap"], reads=[v("LY")])
+            dma("Y", T["yz"][:], v("ZBo%d" % t)["ap"], reads=[v("ZBo%d" % t)])
+    dma("Y", T["yr"][:], T["RW"][:, 0:W], reads=[cols("RW", 0, W)])
+
+    n = len(ops)
+    if "order" not in ORDER:
+        succ, need, tail, ready = [[] for _ in range(n)], [0] * n, [0.0] * n, [0.0] * n
+        for o in ops:
+            pre = o["deps"] | o["order"]
+            need[o["i"]] = len(pre)
+            for d in pre:
+                succ[d].append(o["i"])
+        for i in range(n - 1, -1, -1):
+            o = ops[i]
+            tail[i] = o["cost"] + o.get("lat", 0) + o.get("pre", 0) + HOP + max([tail[j] for j in succ[i]] + [0.0])
+        pri = [tail[o["i"]] + EARLY.get(o["stage"], 0) for o in ops]
+        avail = {e: [] for o in ops for e in o["eng"]}
+        free = {e: 0.0 for e in avail}
+
+        def put(i):
+            for e in ops[i]["eng"]:
+                avail[e].append(i)
+        for o in ops:
+            if not need[o["i"]]:
+                put(o["i"])
+        order, plan, who = [], [], {}
+        while len(order) < n:
+            best = None
+            for e, lst in avail.items():
+                if e == "V":
+                    lst = [j for j in lst if "costs" not in ops[j] or free["S"] > max(ready[j], free["V"]) + HELP]
+                if lst:
+                    first = min(ready[j] for j in lst)
+                    est = first if e == "R" else max(free[e], first)
+                    if best is None or est < best[0]:
+                        best = (est, e, lst)
+            est, e, lst = best
+            i = max((j for j in lst if ready[j] <= est), key=lambda j: ("costs" not in ops[j] or e != "V", pri[j], -j))
+            order.append(i)
+            o = ops[i]
+            for x in o["eng"]:
+                avail[x].remove(i)
+            who[i] = e
+            fin = est + (o["costs"][e] if "costs" in o else o["cost"]) + o.get("pre", 0)
+            if e != "R":
+                free[e] = fin
+            plan.append((est, fin, e, i))
+            for j in succ[i]:
+                ready[j] = max(ready[j], fin + o.get("lat", 0) + (HOP if i in ops[j]["deps"] or e == "R" else 0.0))
+                need[j] -= 1
+                if not need[j]:
+                    put(j)
+        ORDER["order"], ORDER["plan"], ORDER["who"], ORDER["ops"] = order, plan, who, ops
+    order, who = ORDER["order"], ORDER["who"]
+
+    que = {"V": V, "S": S, "P": P, "G": g, "Y": g.sync}
+    count_, known, clock, place = {}, {}, {}, {}
+    sent = 0
+    for pos, i in enumerate(order):
+        o = ops[i]
+        e = who[i]
+        if o["eng"] == "VS" and e == "V":
+            o["fns"] = o["alt"]
+        place[i] = pos
+        if e == "R":
+            clock[i] = (o["arr"][0], o["arr"][1], {})
+            count_[o["arr"][0]] = o["arr"][1]
+            continue
+        kn = known.setdefault(e, {})
+        for d in sorted(o["deps"], key=lambda j: -place[j]):
+            sem, val, snap = clock[d]
+            if kn.get(sem, 0) >= val:
+                continue
+            que[e].wait_ge(T.sem[sem], val)
+            kn[sem] = val
+            for s, x in snap.items():
+                kn[s] = max(kn.get(s, 0), x)
+        if "remote" in o:
+            o["fns"][0]()
+            sent += o["remote"]
+        elif "dmasem" in o:
+            o["fns"][0]().then_inc(T.sem[o["dmasem"]], 16)
+            clock[i] = (o["dmasem"], 16, dict(kn))
+            count_[o["dmasem"]] = 16
+        else:
+            s = "s" + e
+            for f in o["fns"]:
+                f().then_inc(T.sem[s], 1)
+                count_[s] = count_.get(s, 0) + 1
+            clock[i] = (s, count_[s], dict(kn))
+    for s, x in count_.items():
+        g.wait_ge(T.sem[s], x)
+    g.wait_ge(T.sem["snt"], sent)

@@ -5,24 +5,16 @@ from concourse.mybir import dt, AluOpType, AxisListType, ActivationFunctionType
 OP = AluOpType
 AF = ActivationFunctionType
 W, M, HM, TV, STEP = 2560, 256, 128, 4, 3
-BIG, FARK, CONF = 4194304.0, 1048576.0, 131072.0
-CEN, TCEN = 1280.0, 2040.0
+BIG, GATE, CONF = 4194304.0, 262144.0, 131072.0
+CEN, TCEN = 1280.0, 2041.0
 MAGIC = 12582912.0
-GC = 1.5
+RIV = 3840.0
+CFG = {"GC": 1.56, "SC": 3.8, "PE": 0.42, "PO": 2.0, "VO": 20.0, "SO": 40.0, "INORDER": (), "LD": (4500, 8000, 10000, 13500), "RWBY": "G", "OWN": 0, "MM": 4, "GS": 0, "TL": (0, 0), "XSUB": {}, "WIDE": 1, "KE": 1, "RFIRST": (0, 1), "HOP": 230.0, "HELP": 1000.0, "XP": 4, "RP": 4, "SEND": 1000.0, "LAT": 2400.0, "PASS": 300, "SEED": 2, "AMP": 4800.0,
+       "VSUB": {(0, 1): 1, (1, 1): 1}, "VP": 4, "ZBY": ("GGGGGGGG", "GGGGEEEE")}
 CYC = 0.83
-HOP = 80.0
-HELP = 200.0
-PIECES = 1
-CUT = {(1, 1): 2, (0, 1): 2}
-EARLY = {'reps_l01': 300, 'count': -1300, 'bits1': 9000, 'sel30': 6400, 'sel21': 100, 'far0': 23300, 'sel20': 6700, 'reps_l00': 100,
-         'phase1x1': -300, 'far1': 400, 'limits': -8000, 'rvals0': -6000, 'phase20': -6000, 'phase21': -2000, 'reps_z0': -300,
-         'phase1r1': 4000, 'sel31': 1900, 'rupd1': 1000, 'sel11': 3300, 'sel10': 9700, 'rupd0': 2000, 'reps_z1': -4600, 'phase1x0': 1000,
-         'bits0': -3300, 'upd0': -300, 'rvals1': -3300, 'upd1': 300}
-BYPE = ((0, 0),)
+LW = 136
 
 SCRATCH, BANK, ORDER = {}, {}, {}
-
-
 WHAT, AT = {}, {}
 
 
@@ -40,43 +32,47 @@ def _buf(name, shape, dtype, where="sbuf"):
 def _declare():
     B, F, H, I, U = "bfloat16", "float32", "float16", "int32", "uint16"
     sq = [128, 128]
-    for n, s, d in (("XW", [128, W], B), ("RI", [128, W], I), ("RW", [128, W + M], F), ("LI", [128, M], I)):
+    for h in range(2):
+        for n, s, d in (("XW", [128, W], B), ("RI", [128, W], I), ("RW", [128, W + 16], F)):
+            _buf("%s_%d" % (n, h), s, d)
+    for n, s, d in (("LI", [128, M], I), ("ZI", [128, M], B),
+                    ("L0R0", [128, 4096], F), ("L0R1", [128, 4096], F), ("LY", [128, M], F), ("ZY", [128, M], B)):
         _buf(n, s, d)
     for t in range(TV):
-        for n, d in (("LF", U), ("LC", H), ("ZB", B), ("LFo", U), ("LCo", H), ("ZBo", B), ("L0B", F)):
-            _buf("%s%d" % (n, t), [128, M], d)
-        _buf("CN%d" % t, [128, 1], F)
-        _buf("CNo%d" % t, [128, 1], F)
+        for n, d in (("LF", U), ("ZB", B), ("LFo", U), ("ZBo", B)):
+            _buf("%s%d" % (n, t), [128, 2 * LW], d)
+        _buf("L0B%d" % t, [128, M], F)
     for h in range(2):
-        for n, s, d in (("L0R", [128, 2048], F), ("ZR", [128, 2048], B), ("GX", [128, 2048], B), ("AD", [128, 2048], B), ("CF", [128, 2048], B),
-                        ("DA", [128, 2048], B), ("DB", [128, 2048], B), ("KEY", sq, F), ("LOSE", sq, F), ("KF", sq, F), ("LS", sq, F),
-                        ("M1", sq, F), ("M2", sq, F), ("MF", sq, F), ("MG", sq, F), ("KE", [128, 256], F), ("OAB", [128, 256], B),
-                        ("OL", [128, 256], H), ("LOF", [128, 16], U), ("EU", [128, 256], U), ("EC", [128, 256], H), ("ME", [128, 256], F),
-                        ("OE", [128, 256], B), ("OEE", [128, 256], H), ("LEF", [128, 16], U), ("XE", [128, 256], B), ("AE", sq, B),
-                        ("ACT", sq, B), ("ACN", sq, B), ("FF", [128, 256], B), ("FN", [128, 256], B), ("UU", [128, 256], H),
-                        ("KL", sq, H), ("TT", sq, F), ("BI", sq, I), ("WM", sq, B)):
+        for n, s, d in (("GA", [128, 2048], B), ("GB", [128, 2048], B), ("DA", [128, 2048], B), ("DB", [128, 2048], B), ("CF", [128, 2048], B),
+                        ("LC", sq, H), ("M1", sq, F), ("M2", sq, F), ("KEY", sq, F), ("LOSE", sq, F), ("OAB", [128, 256], B), ("MF", sq, F),
+                        ("MG", sq, F), ("KF", sq, F), ("LS", sq, F), ("FF", [128, 256], B), ("LAC", [128, 8], H), ("ML", [128, 16], F), ("KE", [128, 256], F),
+                        ("ME", [128, 256], F), ("QE", [128, 257], B), ("OL", [128, 256], H), ("LOF", [128, 16], U), ("EU", [128, 256], U),
+                        ("EC", [128, 256], H), ("LTD", [128, 256], H), ("ETD", [128, 256], H), ("NW", [128, 512], F), ("THM", [128, 256], H), ("THG", [8, 128], H),
+                        ("GB8", [8, 128], H), ("SCT", sq, H), ("OEE", [128, 256], H), ("LEF", [128, 16], U),
+                        ("XE", [128, 256], B), ("AE", sq, B), ("SG", [128, 256], B), ("NL", [128, 512], F), ("EQ", sq, H),
+                        ("SCU", [128, 32], U), ("ZR", [128, 2048], B), ("Z4", [128, 512], B)):
             _buf("%s_%d" % (n, h), s, d)
-    for n, s, d in (("FTe", [128, 256], B), ("FTo", [128, 256], B), ("EQ", [128, 3072], B), ("LAD", [128, 16], F), ("SCF", [128, 16], F),
-                    ("SCG", [128, 16], F), ("SCU", [128, 16], U), ("EAM", [128, 256], F), ("L0S", [128, 256], F), ("THT", sq, F),
-                    ("THN", sq, F), ("COLS", [128, 16], F), ("NI", [128, 1], I), ("LY", [128, 256], F), ("IA", sq, I), ("IB", sq, I),
-                    ("IC", sq, I), ("ID", [128, 264], I), ("IP", [128, 16], I), ("IQ", [128, 16], I), ("IG", [8, 128], I), ("IE", [128, 1], I),
-                    ("DELTA", sq, B), ("BOb", sq, B), ("BOh", sq, H), ("Ib", sq, B), ("NIb", sq, B), ("HIb", sq, B), ("Ih", sq, H),
-                    ("NIh", sq, H), ("QB", sq, B), ("TRI", sq, B), ("NDEL", sq, B), ("ONb", sq, B), ("ONh", sq, H), ("SB", [128, 264], F),
-                    ("NSB", [128, 264], F), ("SEL0", sq, H), ("BLK", [128, 16], B), ("BLKC", [128, 8], B), ("CK", [128, 256], B),
-                    ("CKE", [128, 256], B), ("BC", [128, 16], U), ("CC", sq, F), ("RMIN", [128, 256], F), ("RMAX", sq, F),
-                    ("SELA", [128, 16, 128], H), ("PW", [128, 16], F), ("PX", [128, 16], F), ("DUM", [128, 16], F), ("DMC", [128, 16], F),
-                    ("GB8", [8, 128], H), ("THI", [8, 1], I), ("THF", [8, 1], F), ("THH", [8, 1], H), ("THG", [8, 128], H)):
+    for n, s, d in (("COLS", [128, 16], F), ("AC", [128, 2], F), ("IA", sq, I), ("IB", sq, I), ("IC", sq, I), ("ID", [128, 132], I),
+                    ("IQ", [128, 16], F), ("IP", [128, 1], I), ("IG", [8, 128], I), ("GI", sq, F), ("KI", sq, F),
+                    ("DELTA", sq, B), ("BOb", sq, B), ("BOh", sq, H), ("NBOh", sq, H), ("NBR", sq, B), ("Ib", sq, B), ("NIb", sq, B),
+                    ("HIb", sq, B), ("Ih", sq, H), ("PI", sq, B), ("NI", sq, B), ("TRI", sq, B), ("TRF", sq, F), ("ONb", sq, B),
+                    ("SB", [128, 132], B), ("NSB", [128, 132], B), ("SEL0", sq, H), ("SELA", [128, 144], H), ("BLK", [128, 8], B), ("CN", [128, 4], F), ("BLK2", [128, 16], B),
+                    ("BLKC", [128, 8], B), ("CK", [128, 408], B), ("CKE", [128, 256], B), ("EO", sq, B), ("RP", [128, 512], B),
+                    ("BC", [128, 16], U), ("BS", [128, 16], U), ("CC1", sq, F), ("CC2", sq, F), ("RMIN", [128, 256], B), ("RMAX", sq, B),
+                    ("R4", [128, 512], B), ("TMK", sq, F), ("ONh", sq, H), ("O32", sq, F),
+                    ("DEL2", [128, 256], B), ("DUP0", sq, H), ("DUP1", sq, H), ("SD0", sq, H), ("SD1", sq, H),
+                    ("THI", [8, 1], I), ("THF", [8, 1], F), ("THH", [8, 1], H)):
         _buf(n, s, d)
-    for n, s, k in (("P0", [128, 512], 0), ("P1", [128, 512], 1), ("PB_0", [128, 512], 2), ("PB_1", [128, 512], 3), ("P4", [128, 512], 4), ("P5", [128, 512], 5), ("P6", [128, 512], 6), ("P7", [128, 512], 7)):
-        _buf(n, s, F, "psum")
+    for k, n in enumerate(("D0", "D1", "K_0", "K_1", "U_0", "U_1", "W_0", "W_1")):
+        _buf(n, [128, 512], F, "psum")
         BANK[n] = k
 
 
 _declare()
-SEMAPHORES = ["sV", "sS", "sP", "sG", "snt"] + ["ld%d" % i for i in range(12)]
+SEMAPHORES = ["sV", "sS", "sP", "sG", "snt"] + ["ld%d" % i for i in range(28)]
 for _t in range(1, TV):
-    SEMAPHORES += ["l0%d" % _t, "cn%d" % _t] + ["z%d_%d" % (_t, h) for h in range(2)] + ["l%d_%d" % (_t, h) for h in range(2)]
-SCOL, CME, CCE, CMO, CCO, CP0, CNEG, CTH0, CTH, CNR, CM15 = range(11)
+    SEMAPHORES += ["l0%d" % _t] + ["l%d_%d" % (_t, h) for h in range(2)]
+CP0, CN0, CD0, CTM, CDUM, CN, CRN = range(7)
 
 
 def rank_program(g, core, T, topo):
@@ -85,32 +81,19 @@ def rank_program(g, core, T, topo):
         return
     N = len(T.cores)
     V, S, P = g.vector, g.scalar, g.tensor
-    ops, hist, ndma, stage = [], {}, [0], ["start"]
+    ops, hist, ndma, stage, latest = [], {}, [0], ["start", 0], {}
     full = slice(None)
+    GC = CFG["GC"]
 
     def v(name, *idx):
         where, shape, dtype = WHAT[name]
         sl = list(idx) + [full] * (len(shape) - len(idx))
-        lo = hi = 0
-        n, stride, lane = 1, 1, None
-        for d in range(len(shape) - 1, 0, -1):
-            a, b, st = sl[d].indices(shape[d]) if isinstance(sl[d], slice) else (sl[d], sl[d] + 1, 1)
-            c = (b - a + st - 1) // st
-            lo += a * stride
-            hi += (a + (c - 1) * st) * stride
-            n *= c
-            if d == len(shape) - 1 and st == 16:
-                lane = a % 16
-            stride *= shape[d]
-        if name in AT:
-            host, at = AT[name]
-            a, b, st = sl[1].indices(shape[1])
-            p0, p1, _ = sl[0].indices(shape[0])
-            ap = T[host][p0:p1, at + a:at + b:st]
-        else:
-            ap = T[name][tuple(sl)]
-        return {"ap": ap, "name": name, "lo": lo, "hi": hi + 1, "lane": lane, "n": n,
-                "psum": where == "psum", "two": dtype in ("bfloat16", "float16", "uint16")}
+        a, b, st = sl[1].indices(shape[1])
+        n = (b - a + st - 1) // st
+        p0, p1, _ = sl[0].indices(shape[0])
+        host, at = AT.get(name, (name, 0))
+        return {"ap": T[host][p0:p1, at + a:at + b:st], "name": name, "lo": a, "hi": a + (n - 1) * st + 1, "lane": a % 16 if st == 16 else None,
+                "n": n, "psum": where == "psum", "two": dtype in ("bfloat16", "float16", "uint16")}
 
     def cols(name, lo, hi, st=1):
         return v(name, full, slice(lo, hi, st))
@@ -133,9 +116,10 @@ def rank_program(g, core, T, topo):
 
     def op(eng, cost, reads, writes, fns, **kw):
         i = len(ops)
-        o = {"i": i, "eng": eng, "cost": cost, "stage": stage[0], "fns": fns, "deps": set(), "order": set(kw.pop("after", ()))}
+        o = {"i": i, "eng": eng, "cost": cost, "stage": stage[0], "t": stage[1], "fns": fns, "deps": set(), "order": set(kw.pop("after", ()))}
         o.update(kw)
-        for a, wr in [(a, 0) for a in flat(reads)] + [(a, 1) for a in flat(writes)]:
+        writes = [a for w in writes for a in (w["parts"][:1] if "parts" in w else [w])]
+        for a, wr in [(a, 0) for a in flat(reads)] + [(a, 1) for a in writes]:
             key = BANK.get(a["name"], a["name"])
             me = (i, wr, a["lo"], a["hi"], a["lane"], a["name"])
             old = hist.setdefault(key, [])
@@ -148,10 +132,11 @@ def rank_program(g, core, T, topo):
             keep = []
             for e in old:
                 if e[0] != i:
-                    if a["psum"] and ops[e[0]]["eng"] != eng:
+                    if a["psum"] and (ops[e[0]]["eng"] != eng or eng == "VS"):
                         o["deps"].add(e[0])
                     elif (wr or e[1]) and hit(me, e):
-                        o["deps"].add(e[0])
+                        same = wr and eng in CFG["INORDER"] and ops[e[0]]["eng"] == eng
+                        o["order" if same else "deps"].add(e[0])
                         if wr and a["lane"] is None and not a["psum"] and a["lo"] <= e[2] and e[3] <= a["hi"]:
                             continue
                 keep.append(e)
@@ -161,25 +146,30 @@ def rank_program(g, core, T, topo):
         return i
 
     def cyc(n, half):
-        return max(64, n * (0.5 if half else 1)) * CYC + 60
+        return max(64, n * (0.5 if half else 1)) * CYC + CFG["VO"]
 
     def tt(out, a, b, o):
+        rd = [a, b]
         if "ind" in out:
-            c = 50 + out["n"] * 3.5 * CYC
+            c = 50 + out["n"] * CFG["SC"] * CYC
+            rd.append(out["parts"][1])
         elif "ind" in a:
             c = 50 + a["n"] * GC * CYC
         else:
             c = cyc(a["n"], False) if (a["psum"] or b["psum"]) else cyc(2 * a["n"], False)
-        return op("V", c, [a, b], [out], [lambda: V.tensor_tensor(out["ap"], a["ap"], b["ap"], o)])
+        return op("V", c, rd, [out], [lambda: V.tensor_tensor(out["ap"], a["ap"], b["ap"], o)])
 
-    def ts(out, a, s1, o1, s2=None, o2=None):
+    def tsf(out, a, s1, o1, s2=None, o2=None):
         def f():
             x1 = s1["ap"] if isinstance(s1, dict) else s1
             x2 = s2["ap"] if isinstance(s2, dict) else s2
             if o2 is None:
                 return V.tensor_scalar(out["ap"], a["ap"], x1, None, o1)
             return V.tensor_scalar(out["ap"], a["ap"], x1, x2, o1, o2)
-        return op("V", cyc(a["n"], a["two"] and out["two"]), [a, s1, s2], [out], [f])
+        return f
+
+    def ts(out, a, s1, o1, s2=None, o2=None):
+        return op("V", cyc(a["n"], a["two"] and out["two"]), [a, s1, s2], [out], [tsf(out, a, s1, o1, s2, o2)])
 
     def cp(out, a):
         c = 50 + a["n"] * GC * CYC if "ind" in a else cyc(a["n"], a["two"] and out["two"])
@@ -188,28 +178,38 @@ def rank_program(g, core, T, topo):
     def fill(out, x):
         return op("V", cyc(out["n"], out["two"]), [], [out], [lambda: V.memset(out["ap"], x)])
 
-    def scan(out, d0, d1, o0, o1):
-        return op("V", cyc(d0["n"], False), [d0, d1], [out], [lambda: V.tensor_tensor_scan(out["ap"], d0["ap"], d1["ap"], 0.0, o0, o1)])
-
-    def total(out, a):
-        return op("V", cyc(a["n"], False), [a], [out], [lambda: V.tensor_reduce(out["ap"], a["ap"], AxisListType.X, OP.add)])
+    def scan(out, d0, d1, o0, o1, first=0.0):
+        return op("V", cyc(d0["n"], False), [d0, d1], [out], [lambda: V.tensor_tensor_scan(out["ap"], d0["ap"], d1["ap"], first, o0, o1)])
 
     def act(out, a, f, **kw):
-        c = (65 + a["n"] * GC * CYC) if "ind" in a else a["n"] * CYC + 100
-        return op("S", c, [a] + list(kw.values()), [out],
+        c = (65 + a["n"] * GC * CYC) if "ind" in a else a["n"] * CYC + CFG["SO"]
+        wr = [out] + ([kw["accum_out"]] if "accum_out" in kw else [])
+        return op("S", c, [a] + [x for k, x in kw.items() if k != "accum_out"], wr,
                   [lambda: S.activation(out["ap"], a["ap"], f, **{k: (x["ap"] if isinstance(x, dict) else x) for k, x in kw.items()})])
 
-    def either(out, a):
+    def either(out, a, add=None):
         k = "ind" in a
         cv = 50 + a["n"] * GC * CYC if k else cyc(a["n"], a["two"] and out["two"])
-        cs = 65 + a["n"] * GC * CYC if k else a["n"] * CYC + 100
-        return op("VS", cv, [a], [out], [lambda: S.activation(out["ap"], a["ap"], AF.Copy)], costs={"V": cv, "S": cs},
-                  alt=[lambda: V.tensor_copy(out["ap"], a["ap"])])
+        cs = 65 + a["n"] * GC * CYC if k else a["n"] * CYC + CFG["SO"]
+        if add is None:
+            fs, fv = (lambda: S.activation(out["ap"], a["ap"], AF.Copy)), (lambda: V.tensor_copy(out["ap"], a["ap"]))
+        else:
+            fs, fv = (lambda: S.activation(out["ap"], a["ap"], AF.Copy, bias=add)), tsf(out, a, add, OP.add)
+        return op("VS", cv, [a], [out], [fs], costs={"V": cv, "S": cs}, alt=[fv])
 
     def pe(*mms):
-        c = sum(max(64, m[2]["n"]) * CYC + 5 for m in mms)
+        c = sum(max(64, m[2]["n"]) * CFG["PE"] * (1 if m[1]["two"] else 4) + CFG["PO"] for m in mms)
         return op("P", c, [x for m in mms for x in (m[1], m[2])], [m[0] for m in mms],
                   [(lambda m=m: P.matmul(m[0]["ap"], m[1]["ap"], m[2]["ap"], m[3], m[4])) for m in mms])
+
+    def acc(*mms, new=False):
+        mms = [list(m) + [new and j == 0, True] for j, m in enumerate(mms)]
+        for m in mms:
+            if not m[3]:
+                latest[m[0]["name"]][4] = False
+            latest[m[0]["name"]] = m
+        for j in range(0, len(mms), CFG["MM"]):
+            pe(*mms[j:j + CFG["MM"]])
 
     def iota(out, pat, base, cm, small=False):
         def f():
@@ -218,6 +218,10 @@ def rank_program(g, core, T, topo):
             return g.iota(out["ap"], pat, base, cm)
         return op("G", 130 + 2 * out["n"] * CYC, [], [out], [f])
 
+    def gcopy(out, a):
+        return op("G", 170 + 2 * out["n"] * CYC, [a], [out],
+                  [lambda: g.affine_select(out["ap"], a["ap"], [[0, out["n"]]], OP.is_ge, 0.0, 0, 0)])
+
     def dma(q, out, a, reads=(), writes=(), cost=2500):
         k = ndma[0]
         ndma[0] += 1
@@ -225,7 +229,7 @@ def rank_program(g, core, T, topo):
              "G": lambda: g.dma_start(out, a, allow_slow_non_contiguous=True)}[q]
         return op(q, 60, list(reads), list(writes), [f], dmasem="ld%d" % k, lat=cost)
 
-    def send(items, sem, dsts=None, cost=1200):
+    def send(items, sem, dsts=None):
         dsts = dsts or [T.cores[(rank + STEP) % N]] * len(items)
         at, tr = 0, []
         for it, d in zip(items, dsts):
@@ -233,387 +237,427 @@ def rank_program(g, core, T, topo):
             at += it[2]
 
         def f():
-            if len(tr) == 1:
-                it, (rid, pid, _), mk = tr[0]
-                g.remote_dma(it[1]["ap"], it[0]["ap"], T.sem[sem[0]], T.sem["snt"], pid, rid, mk)
-            else:
-                g.remote_dma_fused([RemoteDMATransfer(dst_ids=[DstId(rid=ad[0], pnc=ad[1])], dma_engine_mask=mk, remote_sem=T.sem[sem[j % len(sem)]],
-                                                      src=it[0]["ap"], dst=it[1]["ap"]) for j, (it, ad, mk) in enumerate(tr)], local_sem=T.sem["snt"])
-        s = op("G", cost, [it[0] for it in items], [], [f], remote=at)
+            g.remote_dma_fused([RemoteDMATransfer(dst_ids=[DstId(rid=ad[0], pnc=ad[1])], dma_engine_mask=mk, remote_sem=T.sem[sem[j % len(sem)]],
+                                                  src=it[0]["ap"], dst=it[1]["ap"]) for j, (it, ad, mk) in enumerate(tr)], local_sem=T.sem["snt"])
+        s = op("G", CFG["SEND"], [it[0] for it in items], [], [f], remote=at)
         for j, sm in enumerate(sem):
             mine = [it for q, it in enumerate(items) if q % len(sem) == j]
-            op("R", 0, [], [it[1] for it in mine], [], arr=(sm, sum(it[2] for it in mine)), after=[s], pre=2500)
+            op("R", 0, [], [it[1] for it in mine], [], arr=(sm, sum(it[2] for it in mine)), after=[s], pre=CFG["LAT"])
 
-    H = [slice(0, HM), slice(HM, M)]
-    def load(q, name, src, cost=2500):
-        dma(q, v(name)["ap"], T[src][:], writes=[v(name)], cost=cost)
-    load("Y", "LI", "l0", 2200)
-    load("Y", "XW", "xt", 4500)
-    load("S", "ZB0", "z0")
-    load("S", "RI", "ex", 8000)
-    load("G", "THI", "th")
+    IN = [slice(0, HM), slice(HM, M)]
+    SIDE = [slice(0, 64), slice(64, 128)]
 
-    one = slice(0, 1)
+    def load(q, name, cs, src, h, both, cost):
+        for s in range(2):
+            x = dict(v(name, SIDE[s], cs), lane=s)
+            dma(q, x["ap"], T[src][SIDE[h], full if both else IN[s]], writes=[x], cost=cost)
+    GS = CFG["GS"]
+    if not GS:
+        IN = IN[::-1]
+        for q, name, src, c in (("Y", "LI", "l0", 2200), ("Y", "XW_0", "xt", 4500), ("S", "ZI", "z0", 2500), ("S", "THI", "th", 2500),
+                                ("Y", "RI_0", "ex", 8000)):
+            dma(q, v(name)["ap"], T[src][:], writes=[v(name)], cost=c)
+    for h in range(2 * GS):
+        load("Y", "LI", IN[h], "l0", h, False, 2200)
+        load("S", "ZI", IN[h], "z0", h, False, 2500)
+        if h:
+            dma("S", v("THI")["ap"], T["th"][:], writes=[v("THI")])
+        load("Y", "XW_%d" % h, full, "xt", h, True, CFG["LD"][2 * h])
+        load("Y", "RI_%d" % h, slice(0, W), "ex", h, True, CFG["LD"][2 * h + 1])
+
+    def hc(name, h, lo=0, hi=None, st=1):
+        n = "%s_%d" % (name, h if GS or name not in ("XW", "RI", "RW", "THM") else 0)
+        return cols(n, lo, hi if hi else WHAT[n][1][1], st)
+
+    def lf(t, h, lo=0, hi=HM):
+        return cols("LF%d" % t, LW * h + lo, LW * h + hi)
+
+    def zb(t, h):
+        return cols("ZB%d" % t, LW * h, LW * h + HM) if t else v("ZI", full, IN[h])
+
+    one, two, row = slice(0, 1), slice(0, 33), slice(32, 33)
     iota(v("IC"), [[-1, 128]], 0, 1)
     iota(v("IB"), [[-16, 8], [0, 16]], 0, 1)
     iota(v("IA"), [[0, 8], [-1, 16]], 16, 1)
-    iota(v("IG"), [[1, 128]], 0, -16)
-    iota(v("CK", one, slice(0, 128)), [[0, 8], [1, 16]], 0, 0, True)
-    iota(v("CK", one, slice(128, 256)), [[0, 8], [-1, 16]], 16, 0, True)
-    iota(v("CC"), [[0, 8], [1, 16]], 65536, 0, True)
-    iota(v("CKE", one), [[0, 16], [1, 16]], 0, 0, True)
-    iota(v("IP"), [[0, 16]], 0, 1)
-    iota(v("IQ"), [[16, 16]], W, 0)
-    iota(v("ID"), [[-1, 264]], 512, 1)
-    cp(v("LF0"), v("LI"))
-    ts(v("LC0"), v("LI"), -CEN, OP.add)
+    for h in range(2):
+        cp(lf(0, h), v("LI", full, IN[h]))
+        ts(hc("LC", h), v("LI", full, IN[h]), -CEN, OP.add)
     ts(v("Ib"), v("IC"), 0, OP.is_equal)
-    ts(v("NIb"), v("IC"), 0, OP.is_equal, -1.0, OP.mult)
+    for n, x in (("NIb", -1.0), ("PI", GATE), ("NI", -GATE), ("HIb", 0.5), ("Ih", 1.0)):
+        ts(v(n), v("Ib"), x, OP.mult)
     ts(v("IA"), v("IA"), 15, OP.bitwise_and)
     ts(v("DELTA"), v("IA"), 0, OP.is_equal)
     ts(col(CP0), cols("IA", 0, 1), 0, OP.is_equal)
     ts(v("IB"), v("IB"), 4, OP.arith_shift_right)
     ts(v("BOb"), v("IB"), 0, OP.is_equal)
-    ts(v("BOh"), v("IB"), 0, OP.is_equal)
-    ts(v("SEL0"), v("BOh"), col(CP0), OP.mult)
-    ts(cols("BLK", 0, 8), cols("BOb", 0, 128, 16), 16.0, OP.mult)
-    ts(cols("BLK", 8, 16), cols("BOb", 0, 128, 16), 16.0, OP.mult)
+    for n, x in (("BOh", 1.0), ("NBOh", -1.0), ("NBR", -RIV / 2)):
+        ts(v(n), v("BOb"), x, OP.mult)
+    ts(v("SEL0"), v("BOb"), col(CP0), OP.mult)
+    ts(v("BLK"), cols("BOb", 0, 128, 16), 16.0, OP.mult)
     ts(v("BLKC"), cols("BOb", 0, 128, 16), CONF, OP.mult)
-    fill(v("CK", one, slice(0, 128, 16)), FARK)
-    fill(v("CK", one, slice(128, 256, 16)), 0.0)
-    fill(cols("CC", 0, 128, 16), FARK)
+    if any(CFG["VSUB"].values()):
+        ts(cols("BLK2", 0, 8), cols("BOb", 0, 128, 16), 32.0, OP.mult)
+        ts(cols("BLK2", 8, 16), cols("BOb", 0, 128, 16), -16.0, OP.mult)
+    fill(v("SELA"), 0.0)
+    cp(cols("SELA", 15, 143, 16), cols("BOb", 0, 128, 16))
     fill(v("ONb"), 1.0)
-    fill(v("RMIN"), 0.0)
-    fill(cols("RMIN", 0, 256, 16), BIG)
+    for h in range(2):
+        acc((cols("U_0", HM * h, HM * h + HM), v("SEL0"), hc("LC", h)), new=True)
+    act(v("L0B0"), cols("U_0", 0, M), AF.Copy, bias=CEN)
+    send([(v("L0B0"), v("L0B%d" % t), 2) for t in range(1, TV)], ["l0%d" % t for t in range(1, TV)],
+         [T.cores[(rank + STEP * t) % N] for t in range(1, TV)])
+    for k in range(16):
+        either(cols("L0R0", k, 4096, 16), v("L0B0"))
+    gcopy(cols("L0R1", 0, 4096, 16), v("L0B0"))
+    iota(v("GI"), [[-32768, 8], [0, 16]], 0, 0, True)
+    iota(v("KI"), [[0, 8], [1, 16]], 65536, 0, True)
+    fill(v("CK", slice(0, 64)), 0.0)
+    ts(v("CK", one, slice(0, 128)), v("KI", one), -65536.0, OP.add)
+    ts(v("CK", one, slice(128, 256)), v("KI", one), -1.0, OP.mult, 65552.0, OP.add)
+    fill(v("CK", one, slice(0, 128, 16)), GATE)
+    fill(v("CK", one, slice(128, 256, 16)), 0.0)
+    fill(v("CK", one, slice(256, 384)), -0.25)
+    fill(v("CK", one, slice(384, 385)), -31.5)
+    ts(v("CK", row, slice(0, 128)), v("GI", row), 4.0, OP.mult)
+    ts(v("GI"), v("GI"), 4.0, OP.mult)
+    tt(v("CC1"), v("GI"), v("KI"), OP.add)
+    ts(cols("CC1", 0, 128, 16), cols("CC1", 0, 128, 16), 65536.0, OP.add)
+    cp(v("CC2"), v("CC1"))
+    ts(cols("CC2", 1, 128, 16), cols("CC2", 1, 128, 16), 65536.0, OP.add)
+    iota(v("IQ"), [[16, 16]], 15, 0, True)
+    cp(v("BC"), v("IQ"))
+    ts(v("BS"), v("IQ"), -15.0, OP.add, 1.0 / 16, OP.mult)
+    for h in range(2):
+        fill(hc("LOSE", h, 0, 1), BIG)
+        fill(hc("LS", h, 0, 1), 0.0)
+        fill(hc("QE", h, 0, 1), 1.0)
+    fill(v("EO", one), 0.0)
+    fill(v("EO", one, slice(0, 128, 16)), 1.0)
+    iota(v("CKE", one), [[0, 16], [1, 16]], 0, 0, True)
     fill(v("RMAX"), 1.0)
     fill(cols("RMAX", 0, 128, 16), 0.0)
-    ts(v("BC"), v("IQ"), 15 - W, OP.add)
-    for h in range(2):
-        fill(cols("LOSE_%d" % h, 0, 1), BIG)
-        fill(cols("LS_%d" % h, 0, 1), 0.0)
-    cp(cols("RW", 0, W), v("RI"))
-    ts(v("Ih"), v("IC"), 0, OP.is_equal)
-    ts(v("NIh"), v("IC"), 0, OP.is_equal, -1.0, OP.mult)
-    fill(v("SELA"), 0.0)
-    for a in range(16):
-        cp(v("SELA", full, a, slice(a, 128, 16)), cols("BOh", a, 128, 16))
-    ts(v("HIb"), v("IC"), 0, OP.is_equal, 0.5, OP.mult)
-    ts(v("NDEL"), v("IA"), 0, OP.not_equal)
-    fill(v("QB"), -1.0 / 512)
-    ts(v("TRI"), v("IC"), 0, OP.is_ge, -2.0, OP.mult)
+    fill(v("RMIN"), 0.0)
+    fill(cols("RMIN", 0, 256, 16), BIG)
+    fill(v("R4"), -BIG)
+    fill(cols("R4", 0, 512, 4), BIG)
+    fill(v("RP", one), 0.0)
+    fill(v("RP", one, slice(0, 512, 4)), GATE)
+    fill(v("RP", one, slice(1, 512, 4)), GATE)
+    iota(v("IP"), [[0, 1]], 0, 1)
+    ts(v("IP"), v("IP"), 15, OP.bitwise_and)
+    ts(col(CDUM), v("IP"), float(W), OP.add)
+    ts(col(CRN), v("IP"), 65536.0, OP.add)
+    ts(v("TRF"), v("KI"), col(CRN), OP.is_ge, -7 * RIV, OP.mult)
+    ts(v("TRI"), v("DELTA"), -RIV, OP.mult)
+    tt(v("TRI"), v("TRI"), v("TRF"), OP.add)
+    iota(v("ID"), [[-1, 132]], 512, 1)
     ts(v("ID"), v("ID"), 15, OP.bitwise_and)
     ts(v("SB"), v("ID"), 0, OP.is_equal)
     ts(v("NSB"), v("ID"), 0, OP.not_equal)
-    for j in range(12):
-        fill(cols("PW", j, j + 1), float(2 ** (11 - j)))
-    fill(cols("PW", 12, 16), 0.0)
-    tt(v("PX"), v("PW"), cols("DELTA", 0, 16), OP.mult)
-    total(col(SCOL), v("PX"))
-    ts(v("IE"), cols("IP", 0, 1), 4, OP.arith_shift_right, 1, OP.bitwise_and)
-    ts(col(CME), v("IE"), 0, OP.is_equal, 1.0 / 1024, OP.mult)
-    ts(col(CCE), v("IE"), 0, OP.is_equal, -1.0, OP.mult)
-    ts(col(CMO), v("IE"), 1.0 / 1024, OP.mult)
-    ts(col(CCO), v("IE"), -1.0, OP.mult)
-    fill(col(CM15), -15.0)
-    ts(v("IP"), v("IP"), 15, OP.bitwise_and)
-    tt(v("DUM"), v("IP"), v("IQ"), OP.add)
-    ts(v("DMC"), v("DUM"), -1.0, OP.mult, CEN, OP.add)
-    ts(v("IG"), v("IG"), 4, OP.arith_shift_right)
-    ts(v("GB8"), v("IG"), 0, OP.is_equal)
-    ts(v("THF"), v("THI"), -TCEN, OP.add)
-    ts(v("THH"), v("THI"), -TCEN, OP.add)
-    ts(v("THG"), v("GB8"), v("THF"), OP.mult)
+    fill(v("O32"), 1.0 / 32)
+    fill(cols("CN", 0, 1), TCEN - 0.5)
+    iota(v("IG"), [[0, 2], [1, 4], [0, 16]] if GS else [[1, 8], [0, 16]], 0, -1)
+    ts(v("THF"), v("THI"), -1.0, OP.mult, TCEN, OP.add)
+    cp(v("THH"), v("THF"))
     fill(v("ONh", slice(0, 8)), 1.0)
-    pe((cols("P7", 0, 128), v("ONh", slice(0, 8)), v("THG"), True, True))
-    ts(v("THT"), cols("P7", 0, 128), TCEN, OP.add)
-    pe((cols("P7", 128, 129), v("GB8"), v("THH"), True, True))
-    ts(col(CNEG), col(CP0), -100000.0, OP.mult)
-    ts(col(CTH0), cols("P7", 128, 129), TCEN, OP.add, col(CNEG), OP.add)
-    pe((cols("P6", 0, 256), v("SEL0"), v("LC0"), True, True))
-    act(v("L0B0"), cols("P6", 0, 256), AF.Copy, bias=CEN)
-    send([(v("L0B0"), v("L0B%d" % t), 2) for t in range(1, TV)], ["l0%d" % t for t in range(1, TV)],
-         [T.cores[(rank + STEP * t) % N] for t in range(1, TV)])
+    ts(v("TMK"), v("DELTA"), -60000.0, OP.mult, 30000.0, OP.add)
+    ts(col(CTM), col(CP0), 60000.0, OP.mult, -30000.0, OP.add)
+    for h in range(1 + GS):
+        gb, tg = v("GB8_%d" % h), v("THG_%d" % h)
+        ts(gb, v("IG"), -4 * h, OP.is_equal)
+        ts(tg, gb, v("THF"), OP.mult)
+        acc((hc("U", 1, 0, 128), v("ONh", slice(0, 8)), tg), new=True)
+        acc((hc("U", 1, 128, 129), gb, v("THH")), new=True)
+        ts(hc("THM", h, 0, 128), v("ONb"), hc("U", 1, 128, 129), OP.mult, col(CTM), OP.max)
+        tt(hc("THM", h, 128, 256), hc("U", 1, 0, 128), v("TMK"), OP.max)
+        for n, x in (("DUP", "Ih"), ("SD", "SEL0")):
+            for s in range(2 * GS):
+                cp(v(n + str(h), full, SIDE[s]), v(x, full, SIDE[h]))
+    cp(cols("DEL2", 0, 128), v("DELTA"))
+    cp(cols("DEL2", 128, 256), v("DELTA"))
+    for h in range(1 + GS):
+        stage[0] = "rw%d" % h
+        for q in range(4):
+            {"V": cp, "G": gcopy}[CFG["RWBY"]](hc("RW", h, 640 * q, 640 * q + 640), hc("RI", h, 640 * q, 640 * q + 640))
 
-    def hc(name, h, lo=0, hi=None):
-        if name == "PU":
-            return cols("PB_%d" % h, 256 + lo, 256 + hi)
-        return cols("%s_%d" % (name, h), lo, hi if hi else WHAT["%s_%d" % (name, h)][1][1])
+    def table(t, h):
+        return hc("RW", h, 0, W) if t else hc("RI", h)
 
-    def last(name, h, n=128):
-        return ind(hc(name, h), cols("BC", 0, n // 16))
+    def reps(t):
+        for k in range(1, 16):
+            gcopy(cols("L0R%d" % (t % 2), k, 4096, 16), v("L0B%d" % t))
 
-    def reps_l0(t, h):
-        for k in range(1 if t else 0, 16):
-            either(cols("L0R_%d" % h, k, 2048, 16), v("L0B%d" % t, full, H[h]))
+    def gather(h, off, G):
+        for q in range(CFG["XP"]):
+            a, b = HM * q // CFG["XP"], HM * (q + 1) // CFG["XP"]
+            either(hc(G, h, 16 * a, 16 * b), ind(hc("XW", h), off(a, b)))
 
-    def reps_z(t, h):
-        for k in range(16):
-            either(cols("ZR_%d" % h, k, 2048, 16), v("ZB%d" % t, full, H[h]))
-
-    def far_off(t, h, off, o0, G, AD, k0):
-        for q in range(PIECES):
-            a, b = HM * q // PIECES, HM * (q + 1) // PIECES
-            either(cols(G, 16 * a, 16 * b), ind(v("XW"), cols(off, o0 + a, o0 + b)))
+    def sizes(t, h, G, D, k0, out, blk):
         for c in range(4):
+            bank = "D%d" % (h if CFG["OWN"] else c % 2)
             ks = [k for k in range(4 * c, 4 * c + 4) if k >= k0]
             for k in ks:
-                o = cols("P%d" % (c % 2), 128 * (k % 4), 128 * (k % 4) + 128)
-                pe((o, v("Ib"), cols(G, k, 2048, 16), True, False), (o, v("NIb"), v("ZB%d" % t, full, H[h]), False, True))
+                o = cols(bank, 128 * (k % 4), 128 * (k % 4) + 128)
+                acc((o, v("Ib"), hc(G, h, k, 2048, 16)), (o, v("NIb"), zb(t, h)), new=True)
             lo, hi = ks[0], ks[-1] + 1
-            act(cols(AD, 128 * lo, 128 * hi), cols("P%d" % (c % 2), 128 * (lo % 4), 128 * (hi - 4 * c)), AF.Abs)
+            act(hc(D, h, 128 * lo, 128 * hi), cols(bank, 128 * (lo % 4), 128 * (hi - 4 * c)), AF.Abs)
+            for j in range(len(out(0))):
+                acc(*[(out(k)[j], hc(D, h, 128 * k, 128 * k + 128), blk) for k in ks])
 
     def phase1x(t, h):
-        AD, PB = "AD_%d" % h, "PB_%d" % h
-        far_off(t, h, "LF%d" % t, HM * h, "GX_%d" % h, AD, 1)
-        pe((cols(PB, 0, 256), v("ONb", one), v("CK", one), True, False))
-        for k in range(1, 16):
-            pe((cols(PB, k, 256, 16), cols(AD, 128 * k, 128 * k + 128), v("BLK"), False, False))
+        if t:
+            ts(hc("LC", h), lf(t, h), -CEN, OP.add)
+        acc((hc("W", h, 256, 384), v("ONb", one), v("CK", one, slice(128, 256))), new=True)
+        if h in CFG["XSUB"] and t:
+            for q in range(CFG["VP"]):
+                a, b = HM * q // CFG["VP"], HM * (q + 1) // CFG["VP"]
+                x, y = hc("GA", h, 16 * a, 16 * b), hc("DA", h, 16 * a, 16 * b)
+                tt(x, ind(hc("XW", h), lf(t, h, a, b)), hc("ZR", h, 16 * a, 16 * b), OP.subtract)
+                act(y, x, AF.Abs)
+            for o, at in (("K", 0), ("W", 256)):
+                acc(*[(hc(o, h, at + k, at + 128, 16), hc("DA", h, k, 2048, 16), v("BLK")) for k in range(1, 16)])
+            return
+        gather(h, lambda a, b: lf(t, h, a, b), "GA")
+        sizes(t, h, "GA", "DA", 1, lambda k: [hc("K", h, k, 128, 16), hc("W", h, 256 + k, 384, 16)], v("BLK"))
 
     def phase1r(t, h):
-        tt(hc("CF", h), ind(cols("RW", 0, W), v("LF%d" % t, full, H[h])), hc("L0R", h), OP.is_equal)
-        pe(*[(cols("PB_%d" % h, k, 128, 16), cols("CF_%d" % h, k, 2048, 16), v("BLKC"), False, k == 15) for k in range(1, 16)])
+        for q in range(CFG["RP"]):
+            a, b = HM * q // CFG["RP"], HM * (q + 1) // CFG["RP"]
+            tt(hc("CF", h, 16 * a, 16 * b), ind(table(t, h), lf(t, h, a, b)),
+               cols("L0R%d" % (t % 2), 2048 * h + 16 * a, 2048 * h + 16 * b), OP.is_equal)
+        acc(*[(hc("K", h, k, 128, 16), hc("CF", h, k, 2048, 16), v("BLKC")) for k in range(1, 16)])
 
-    def pp(h, lo, hi):
-        return cols("P5" if h else "P6", lo, hi)
+    def last(h, name):
+        return ind(hc(name, h), cols("BC", 0, 8))
 
-    def lists(h, src, out, extra=None):
-        o = pp(h, 256, 272)
-        pe(*[(o, v("SELA", full, a), cols(src, a, 256, 16), a == 0, a == 15) for a in range(16)])
-        ts(v(out), o, CEN, OP.add)
-        if extra:
-            tt(cols("LAD", 8 * h, 8 * h + 8), pp(h, 256, 264), cols("DMC", 8 * h, 8 * h + 8), OP.add)
+    def step(h, Q, l, Mn, n, bc):
+        either(hc("ML", h), hc(Mn, h, 15, n, 16))
+        tt(hc(Q, h, 1 + 128 * l, 1 + 128 * l + n), ind(hc("ML", h), cols(bc, 0, n // 16)), hc(Mn, h, 0, n), OP.is_equal)
 
-    def sel1(t, h):
-        tt(hc("KEY", h), cols("PB_%d" % h, 0, 128), v("CC"), OP.min)
-        scan(hc("M1", h), cols("RMIN", 0, 128), hc("KEY", h), OP.max, OP.min)
-        tt(hc("LOSE", h, 1, 128), hc("KEY", h, 1, 128), hc("M1", h, 0, 127), OP.max)
-        tt(hc("OAB", h, 0, 128), last("M1", h), hc("KEY", h), OP.is_equal)
-        scan(hc("M2", h), cols("RMIN", 0, 128), hc("LOSE", h), OP.max, OP.min)
-        tt(hc("OAB", h, 128, 256), last("M2", h), hc("KEY", h), OP.is_equal)
+    def qq(h, Q, l):
+        return hc(Q, h, 1 + 128 * l, 129 + 128 * l), hc(Q, h, 128 * l, 128 + 128 * l)
+
+    def turn(h, Q, l):
+        o, (q, s) = hc("U", h, 128 * l, 128 * l + 128), qq(h, Q, l)
+        acc((o, v("EO", one), v("ONb", one)), (o, q, v("Ib")), (o, s, v("NIb")), new=True)
+        return o
+
+    def lists(o, src, a0, a1, new=False):
+        acc(*[(o, cols("SELA", 15 - a, 143 - a), cols(src, a0 + a, a1, 16)) for a in range(16)], new=new)
+
+    def tlists(h, bank, src, mid):
         for l in range(2):
-            p = pp(h, 128 * l, 128 * l + 128)
-            pe((p, hc("OAB", h, 128 * l, 128 * l + 128), v("Ib"), True, True))
-            tt(hc("OL", h, 128 * l, 128 * l + 128), p, v("LC%d" % t, full, H[h]), OP.mult)
-        lists(h, "OL_%d" % h, "LOF_%d" % h, True)
-        cp(hc("EU", h), ind(cols("RW", 0, W), hc("LOF", h)))
+            acc((hc(bank, h, 128 * l, 128 * l + 128), hc(src, h, 128 * l, 128 * l + 128), v("BOh")), new=True)
+        tt(hc(mid, h), hc(bank, h, 0, 256), v("DEL2"), OP.mult)
+        for l in range(2):
+            acc((hc(bank, h, 256 + 8 * l, 264 + 8 * l), hc(mid, h, 128 * l, 128 * l + 128), cols("BOh", 0, 128, 16)), new=True)
+
+    def near(t, h):
+        key = hc("K", h, 0, 128)
+        scan(hc("M1", h), v("CC1"), key, OP.min, OP.min, BIG)
+        tt(hc("LOSE", h, 1, 128), hc("K", h, 1, 128), hc("M1", h, 0, 127), OP.max)
+        tt(hc("KEY", h), key, v("CC1"), OP.min)
+        scan(hc("M2", h), v("CC2"), hc("LOSE", h), OP.min, OP.min, BIG)
+        for l in range(2):
+            o, u = hc("OAB", h, 128 * l, 128 * l + 128), hc("U", h, 128 * l, 128 * l + 128)
+            tt(o, last(h, "M%d" % (l + 1)), hc("KEY", h), OP.is_equal)
+            acc((u, o, v("Ib")), new=True)
+            tt(hc("OL", h, 128 * l, 128 * l + 128), u, hc("LC", h), OP.mult)
+        if CFG["TL"][0]:
+            tlists(h, "K", "OL", "LTD")
+        else:
+            lists(hc("K", h, 256, 272), "OL_%d" % h, 0, 256, True)
+        ts(hc("LOF", h), hc("K", h, 256, 272), CEN, OP.add)
+        cp(hc("EU", h), ind(table(t, h), hc("LOF", h)))
         ts(hc("EC", h), hc("EU", h), -CEN, OP.add)
-        tt(hc("KF", h), last("M2", h), hc("KEY", h), OP.is_lt)
 
     def far(t, h):
-        tt(hc("KF", h), cols("PB_%d" % h, 128, 256), hc("KF", h), OP.mult)
-        scan(hc("MF", h), v("RMAX"), hc("KF", h), OP.mult, OP.max)
-        tt(hc("LS", h, 1, 128), hc("KF", h, 1, 128), hc("MF", h, 0, 127), OP.min)
-        tt(hc("FF", h, 0, 128), last("MF", h), hc("KF", h), OP.is_equal)
+        key = hc("W", h, 256, 384)
+        acc(*[(key, v("NI"), hc("OAB", h, 128 * l, 128 * l + 128)) for l in range(2)])
+        scan(hc("MF", h), v("RMAX"), key, OP.mult, OP.max)
+        tt(hc("LS", h, 1, 128), hc("W", h, 257, 384), hc("MF", h, 0, 127), OP.min)
+        either(hc("KF", h), key)
+        tt(hc("FF", h, 0, 128), last(h, "MF"), hc("KF", h), OP.is_equal)
         scan(hc("MG", h), v("RMAX"), hc("LS", h), OP.mult, OP.max)
-        tt(hc("FF", h, 128, 256), last("MG", h), hc("KF", h), OP.is_equal)
-        f = [hc("FF", h, 0, 128), hc("FF", h, 128, 256)]
-        pe(*[(cols("P7", 128 * l, 128 * l + 128), f[l], v("Ib"), True, True) for l in range(2)])
-        act(hc("FN", h), cols("P7", 0, 256), AF.Copy)
-        keep = cols("P7", 256, 384)
-        pe((keep, f[0], v("NIb"), True, False), (keep, f[1], v("NIb"), False, False), (keep, v("ONb", one), v("ONb", one), False, True))
-        tt(hc("KL", h), keep, v("LC%d" % t, full, H[h]), OP.mult)
+        tt(hc("FF", h, 128, 256), last(h, "MG"), hc("KF", h), OP.is_equal)
 
-    def bits(t, h):
-        p = cols("P7", 384, 512)
-        pe((p, v("BOh"), hc("OL", h, 0, 128), True, True))
-        BI = hc("BI", h)
-        ts(BI, p, CEN, OP.add, col(SCOL), OP.mult)
-        ts(BI, BI, 2048, OP.bitwise_and)
-        ts(v("FTe", full, H[h]), BI, col(CME), OP.mult, col(CCE), OP.add)
-        ts(v("FTo", full, H[h]), BI, col(CMO), OP.mult, col(CCO), OP.add)
-        for q in range(4):
-            mm, n = [], 0
-            for F in ("FTe", "FTo"):
-                for hp in range(h + 1):
-                    o, ps = cols("P%d" % (q % 2), n, n + 128), slice(32 * q, 32 * q + 32)
-                    if hp == h:
-                        mm.append((o, v("Ib"), v("TRI"), True, False))
-                    mm.append((o, v(F, ps, H[hp]), v(F, ps, H[h]), hp != h, True))
-                    n += 128
-            pe(*mm)
-            c = 1024 * h + n * q
-            act(cols("EQ", c, c + n), cols("P%d" % (q % 2), 0, n), AF.Relu, bias=col(CM15))
+    def rivals(t, h):
+        ola, o, d = hc("OL", h, 0, 128), hc("U", h, 256, 384), hc("K", h, 272, 400)
+        if not CFG["TL"][0]:
+            acc((o, ola, v("BOh")), new=True)
+            tt(hc("LTD", h, 0, 128), o, v("DELTA"), OP.mult)
+        acc((d, v("Ib"), v("TRI")), (d, v("NBOh"), ola), (d, hc("LTD", h, 0, 128), v("BOh")), new=True)
+        if not GS:
+            acc((o, v("Ih"), hc("EC", h, 0, 128)), (o, v("NI"), cols("SB", t, t + 128)), new=True)
+            o = hc("U", h, 384, 512)
+            acc((o, v("SEL0"), hc("LC", h)), (o, v("NI"), cols("NSB", t, t + 128)), new=True)
+            either(hc("NW", h, 0, 256), hc("U", h, 256, 512), CEN)
+            return
+        for s in range(2):
+            o = hc("U", h, 128 * s, 128 * s + 128)
+            acc((o, v("DUP%d" % s), hc("EC", h, 0, 128)), (o, v("NI"), cols("SB", t, t + 128)), new=True)
+            o = hc("U", h, 256 + 128 * s, 384 + 128 * s)
+            acc((o, v("SD%d" % s), hc("LC", h)), (o, v("NI"), cols("NSB", t, t + 128)), new=True)
+        either(hc("NW", h), hc("U", h), CEN)
+
+    def phase2g(t, h):
+        for l, G in enumerate(("GA", "GB")):
+            if (h, l) not in CFG["VSUB"]:
+                gather(h, lambda a, b: hc("EU", h, 128 * l + a, 128 * l + b), G)
+
+    def spread(t, h):
+        if not any(x[0] == h for x in CFG["VSUB"]):
+            return
+        how = {"G": gcopy, "V": cp, "E": either}
+        by = CFG["ZBY"][h]
+        for k, e in enumerate(by[:4]):
+            how[e](dict(hc("Z4", h, k, 512, 4), lane=k), zb(t, h))
+        for k, e in enumerate(by[4:]):
+            how[e](dict(hc("ZR", h, k, 2048, 4), lane=k), hc("Z4", h))
 
     def phase2(t, h):
-        for l, D in enumerate(("DA", "DB")):
-            e = hc("EU", h, 128 * l, 128 * l + 128)
-            if (h, l) in BYPE:
-                far_off(t, h, "EU_%d" % h, 128 * l, "GX_%d" % h, "%s_%d" % (D, h), 0)
-            else:
-                cut = CUT.get((h, l), 1)
-                for q in range(cut):
-                    a, b = HM * q // cut, HM * (q + 1) // cut
-                    d = hc(D, h, 16 * a, 16 * b)
-                    tt(d, ind(v("XW"), hc("EU", h, 128 * l + a, 128 * l + b)), hc("ZR", h, 16 * a, 16 * b), OP.subtract)
-                    act(d, d, AF.Abs)
-        pe((cols("P4", 0, 256), v("ONb", one), v("CKE", one), True, False))
-        for l, D in enumerate(("DA", "DB")):
-            D = "%s_%d" % (D, h)
-            pe(*[(cols("P4", 128 * l + j, 128 * l + 128, 16), cols(D, 128 * j, 128 * j + 128) if (h, l) in BYPE else cols(D, j, 2048, 16),
-                  cols("BLK", 0, 8), False, l == 1 and j == 15) for j in range(16)])
+        acc((hc("W", h, 0, 256), v("ONb", one), v("CKE", one)), new=True)
+        for l, (G, D) in enumerate((("GA", "DA"), ("GB", "DB"))):
+            out = lambda k: hc("W", h, 128 * l + k, 128 * l + 128, 16)
+            if (h, l) not in CFG["VSUB"]:
+                if not CFG["WIDE"]:
+                    sizes(t, h, G, D, 0, lambda k: [out(k)], v("BLK"))
+                    continue
+                for c in range(4):
+                    o = v("D%d" % (h if CFG["OWN"] else c % 2))
+                    acc((o, v("NIb"), hc("ZR", h, 512 * c, 512 * c + 512)), new=True)
+                    acc((o, v("Ib"), hc(G, h, 512 * c, 512 * c + 512)))
+                    act(hc(D, h, 512 * c, 512 * c + 512), o, AF.Abs)
+                acc(*[(out(k), hc(D, h, k, 2048, 16), v("BLK")) for k in range(16)])
+                continue
+            relu = CFG["VSUB"][(h, l)]
+            for q in range(CFG["VP"]):
+                a, b = HM * q // CFG["VP"], HM * (q + 1) // CFG["VP"]
+                x, y = hc(G, h, 16 * a, 16 * b), hc(D, h, 16 * a, 16 * b)
+                tt(x, ind(hc("XW", h), hc("EU", h, 128 * l + a, 128 * l + b)), hc("ZR", h, 16 * a, 16 * b), OP.subtract)
+                if relu:
+                    op("VS", cyc(x["n"], True), [x], [y], [lambda x=x, y=y: S.activation(y["ap"], x["ap"], AF.Relu)],
+                       costs={"V": cyc(x["n"], True), "S": x["n"] * CYC + CFG["SO"]}, alt=[tsf(y, x, 0.0, OP.max)])
+                else:
+                    act(y, x, AF.Abs)
+            if relu:
+                acc(*[(out(k), hc(G, h, k, 2048, 16), cols("BLK2", 8, 16)) for k in range(16)])
+            acc(*[(out(k), hc(D, h, k, 2048, 16), cols("BLK2" if relu else "BLK", 0, 8)) for k in range(16)])
 
-    def sel2(t, h):
-        act(hc("KE", h), cols("P4", 0, 256), AF.Copy)
-        scan(hc("ME", h), v("RMIN"), hc("KE", h), OP.max, OP.min)
-        tt(hc("OE", h), last("ME", h, 256), hc("KE", h), OP.is_equal)
-
-    def sel3(t, h):
-        pe(*[(pp(h, 128 * l, 128 * l + 128), hc("OE", h, 128 * l, 128 * l + 128), v("Ib"), True, True) for l in range(2)])
-        tt(hc("OEE", h), pp(h, 0, 256), hc("EC", h), OP.mult)
-        lists(h, "OEE_%d" % h, "LEF_%d" % h)
-        cp(hc("XE", h), ind(v("XW"), hc("LEF", h)))
-        pe((pp(h, 0, 256), v("BOh"), hc("OEE", h), True, True))
-        tt(hc("UU", h), pp(h, 0, 256), hc("FN", h), OP.mult)
-        xa, xb = hc("XE", h, 0, 128), hc("XE", h, 128, 256)
-        p0, p1 = hc("PU", h, 0, 128), hc("PU", h, 128, 256)
-        pe((p0, v("Ib"), xa, True, False), (p0, v("NIb"), xb, False, True))
-        act(hc("AE", h), p0, AF.Abs)
-        pe((p0, v("BOb"), hc("AE", h), True, True))
-        pe((p1, hc("AE", h), v("BOb"), True, True))
-
-    def upd(t, h):
-        p0, p1 = hc("PU", h, 0, 128), hc("PU", h, 128, 256)
-        xa, xb = hc("XE", h, 0, 128), hc("XE", h, 128, 256)
-        ts(hc("ACN", h), p0, col(CTH), OP.is_lt)
-        u, w = pp(h, 0, 128), pp(h, 128, 256)
-        ua, ub, kl = hc("UU", h, 0, 128), hc("UU", h, 128, 256), hc("KL", h)
-        pe((u, v("Ih"), kl, True, False), (u, v("Ih"), ua, False, False), (u, v("Ih"), ub, False, True),
-           (w, v("Ih"), hc("EC", h, 128, 256), True, False), (w, v("NIh"), kl, False, False), (w, v("NIh"), ua, False, False), (w, v("NIh"), ub, False, True))
-        tt(hc("TT", h), w, hc("ACN", h), OP.mult)
-        lc, lf = v("LCo%d" % t, full, H[h]), v("LFo%d" % t, full, H[h])
-        tt(lc, u, hc("TT", h), OP.add)
-        if t < TV - 1:
-            ts(lf, lc, CEN, OP.add)
-            send([(lf, v("LF%d" % (t + 1), full, H[h]), 4), (lc, v("LC%d" % (t + 1), full, H[h]), 4)], ["l%d_%d" % (t + 1, h)])
+    def pick(t, h):
+        scan(hc("ME", h), v("RMIN"), hc("W", h, 0, 256), OP.max, OP.min)
+        if CFG["KE"]:
+            either(hc("KE", h), hc("W", h, 0, 256))
+            tt(hc("QE", h, 0, 256), ind(hc("ME", h), v("BC")), hc("KE", h), OP.is_equal)
+            for l in range(2):
+                acc((hc("U", h, 128 * l, 128 * l + 128), hc("QE", h, 128 * l, 128 * l + 128), v("Ib")), new=True)
         else:
-            ts(v("LY", full, H[h]), lc, CEN, OP.add)
-        tt(hc("ACT", h), p1, v("THN"), OP.is_lt)
-        p0 = hc("PU", h, 0, 128)
-        pe((p0, v("HIb"), xa, True, False), (p0, v("HIb"), xb, False, False), (p0, v("QB"), v("ONb"), False, True))
-        zo = v("ZBo%d" % t, full, H[h])
-        ts(zo, p0, MAGIC, OP.add, -MAGIC, OP.add)
-        if t < TV - 1:
-            send([(zo, v("ZB%d" % (t + 1), full, H[h]), 8)], ["z%d_%d" % (t + 1, h)])
-
-    def rvals(t, h):
-        i0 = HM * h + t
-        tt(v("EAM", full, H[h]), ind(cols("RW", 0, W), hc("LOF", h, 0, 8)), cols("NSB", i0, i0 + HM), OP.mult)
-        tt(v("L0S", full, H[h]), v("L0B%d" % t, full, H[h]), cols("SB", i0, i0 + HM), OP.mult)
-
-    def rupd(t, h):
-        P_ = "P5" if h else "P7"
-        eq = lambda gg, hp: 1024 * h + 128 * ((h + 1) * gg + hp)
-        pe((cols(P_, 0, 128), v("Ib"), v("NDEL"), True, False),
-           *[(cols(P_, 16 * gg, 16 * gg + 16), cols("EQ", eq(gg, hp), eq(gg, hp) + 128),
-              hc("ACT", hp, 16 * gg, 16 * gg + 16), False, gg == 7 and hp == h) for gg in range(8) for hp in range(h + 1)])
-        tt(hc("WM", h), hc("ACT", h), cols(P_, 0, 128), OP.is_gt)
-        pe((cols(P_, 256, 264), hc("WM", h), cols("BOb", 0, 128, 16), True, True))
-        c = slice(8 * h, 8 * h + 8)
-        tt(v("SCF", full, c), cols(P_, 256, 264), v("LAD", full, c), OP.mult)
-        tt(v("SCG", full, c), v("SCF", full, c), v("DUM", full, c), OP.add)
-        cp(v("SCU", full, c), v("SCG", full, c))
-        tt(ind(v("RW"), v("SCU", full, c)), v("EAM", full, H[h]), v("L0S", full, H[h]), OP.add)
-
-    def count(t):
-        p = cols("P7", 288, 296)
-        pe(*[(p, v("ONb"), cols("ACT_%d" % h, 0, 128, 16), h == 0, h == 1) for h in range(2)])
-        total(col(CNR), p)
-        cp(v("NI"), col(CNR))
-        ts(v("NI"), v("NI"), 63, OP.bitwise_and)
-        cp(v("CNo%d" % t), v("NI"))
-        send([(v("CNo%d" % t), v("CN%d" % (t + 1)), 1)], ["cn%d" % (t + 1)])
-
-    def do(part, name, t, h):
-        stage[0] = name + str(h)
-        part(t, h)
-
-    for h in range(2):
-        do(reps_l0, "reps_l0", 0, h)
-    for t in range(TV):
-        for h in range(2):
-            do(phase1x, "phase1x", t, h)
-        for h in range(2):
-            do(phase1r, "phase1r", t, h)
-            if t + 1 < TV:
-                do(reps_l0, "reps_l0", t + 1, h)
-        for h in range(2):
-            do(reps_z, "reps_z", t, h)
-            do(sel1, "sel1", t, h)
-            if h:
-                do(sel2, "sel2", t, 0)
-            do(phase2, "phase2", t, h)
-            do(far, "far", t, h)
-            do(bits, "bits", t, h)
-            do(rvals, "rvals", t, h)
-        do(sel2, "sel2", t, 1)
-        stage[0] = "limits"
-        if t:
-            ts(v("THN"), v("THT"), v("CN%d" % t), OP.add)
-            ts(col(CTH), col(CTH0), v("CN%d" % t), OP.add)
+            step(h, "QE", 0, "ME", 256, "BS")
+            for l in range(2):
+                turn(h, "QE", l)
+        tt(hc("OEE", h), hc("U", h, 0, 256), hc("EC", h), OP.mult)
+        if CFG["TL"][1]:
+            tlists(h, "U", "OEE", "ETD")
         else:
-            cp(v("THN"), v("THT"))
-            cp(col(CTH), col(CTH0))
-        for h in range(2):
-            do(sel3, "sel3", t, h)
-            do(upd, "upd", t, h)
-            do(rupd, "rupd", t, h)
+            lists(hc("U", h, 256, 272), "OEE_%d" % h, 0, 256, True)
+        ts(hc("LEF", h), hc("U", h, 256, 272), CEN, OP.add)
+        either(hc("XE", h), ind(hc("XW", h), hc("LEF", h)))
+        xa, xb = hc("XE", h, 0, 128), hc("XE", h, 128, 256)
+        o = hc("W", h, 0, 128)
+        acc((o, v("Ib"), xa), (o, v("NIb"), xb), new=True)
+        act(hc("AE", h), o, AF.Abs)
+        acc((hc("W", h, 128, 384), v("Ih"), hc("THM", h)), (hc("W", h, 128, 256), v("BOb"), hc("AE", h)),
+            (hc("W", h, 256, 384), hc("AE", h), v("BOb")), new=True)
+        if t and not h:
+            ts(cols("CN", t, t + 1), cols("ZB%d" % t, LW + HM, LW + HM + 1), TCEN + 31.0, OP.add)
+        act(hc("SG", h), hc("W", h, 128, 384), AF.Sign, scale=-1.0, bias=cols("CN", t, t + 1), accum_out=cols("AC", h, h + 1))
+        o = hc("W", h, 384, 512)
+        acc((o, v("ONb", one), v("CK", one, slice(256, 384))), (o, v("HIb"), xa), (o, v("HIb"), xb), new=True)
+        zo = cols("ZBo%d" % t, LW * (1 - h), LW * (1 - h) + HM) if t < TV - 1 else v("ZY", full, IN[h])
+        ts(zo, o, MAGIC, OP.add, -MAGIC, OP.add)
+
+    def rows(t, h):
+        c = [hc("U", h, j, 512, 4) for j in range(4)]
+        mm = [(hc("U", h), v("ONb", one), v("RP", one)), (c[2], v("Ih"), hc("LC", h)), (c[3], v("Ih"), hc("EC", h, 128, 256))]
+        for l in range(2):
+            q = hc("FF", h, 128 * l, 128 * l + 128)
+            mm += [(c[l], q, v("NI")), (c[2], q, v("PI")), (c[l], v("BOh"), hc("OEE", h, 128 * l, 128 * l + 128))]
+        acc(*mm, new=True)
+        acc(*[(c[j], v("NI" if j == 3 else "PI"), hc("SG", h, 0, 128)) for j in range(4)])
+        scan(hc("NL", h), v("R4"), hc("U", h), OP.max, OP.min)
+        lo = cols("LFo%d" % t, HM * (1 - h), HM * (2 - h)) if t < TV - 1 else v("LY", full, IN[h])
+        ts(lo, hc("NL", h, 3, 512, 4), GATE + CEN, OP.add)
+
+    def leave(t, h):
+        wide = HM + h
+        if h:
+            p = cols("W_1", 0, 1)
+            acc((p, v("ONb", one), v("CK", one, slice(384, 385))), *[(p, v("O32"), cols("AC", j, j + 1)) for j in range(2)], new=True)
+            ts(col(CRN), p, 64 * MAGIC, OP.add, -64 * MAGIC, OP.add)
+            tt(cols("ZBo%d" % t, HM, HM + 1), p, col(CRN), OP.subtract)
+        send([(cols("LFo%d" % t, HM * (1 - h), HM * (1 - h) + wide), lf(t + 1, h, 0, wide), 4),
+              (cols("ZBo%d" % t, LW * (1 - h), LW * (1 - h) + wide), cols("ZB%d" % (t + 1), LW * h, LW * h + wide), 4)], ["l%d_%d" % (t + 1, h)])
+
+    def winners(t, h):
+        d = hc("K", h, 272, 400)
+        acc((d, hc("SG", h, 128, 256), v("NBR")))
+        ts(hc("EQ", h), d, 0.0, OP.is_equal, RIV, OP.mult)
+        o = hc("K", h, 0, 128)
+        acc((o, hc("OL", h, 0, 128), v("BOh")), (o, hc("EQ", h), v("BOh")), new=True)
+        tt(hc("SCT", h), o, v("DELTA"), OP.mult)
+        if GS:
+            for s in range(2):
+                for r in range(2):
+                    acc((v("K_%d" % h, SIDE[r], slice(128 + 8 * s, 136 + 8 * s)), hc("SCT", h, 64 * s, 64 * s + 64), cols("BOh", 0, 128, 16)), new=True)
+        else:
+            acc((hc("K", h, 128, 136), hc("SCT", h), cols("BOh", 0, 128, 16)), new=True)
+        n = 8 + 8 * GS
+        ts(hc("SCU", h, 0, 2 * n, 2), hc("K", h, 128, 128 + n), CEN, OP.add, col(CDUM), OP.min)
+
+    def write(t, h):
+        n = 128 + 128 * GS
+        for b in range(n // 16 - 1, -1, -1):
+            tt(ind(hc("RW", h), hc("SCU", h, 2 * b, 2 * b + 1)), hc("NW", h, 16 * b, 16 * b + 16), hc("NW", h, n + 16 * b, n + 16 + 16 * b), OP.max)
+        if t == TV - 1 and h and not GS:
+            dma("S", T["yl"][:], v("LY")["ap"], reads=[v("LY")])
+            dma("S", T["yz"][:], v("ZY")["ap"], reads=[v("ZY")])
+            dma("Y", T["yr"][:], hc("RW", h, 0, W)["ap"], reads=[hc("RW", h, 0, W)], cost=6000)
+        if t == TV - 1 and GS:
+            for s in range(2):
+                for n, x in (("yl", "LY"), ("yz", "ZY")):
+                    dma("Y", T[n][SIDE[h], IN[s]], v(x, SIDE[s], IN[h])["ap"], reads=[v(x, full, IN[h])])
+            dma("Y", T["yr"][SIDE[h], full], v("RW_%d" % h, SIDE[0], slice(0, W))["ap"], reads=[hc("RW", h, 0, W)], cost=4500)
+
+    def do(t, h, *parts):
+        for name, part in parts:
+            stage[0] = name + str(h)
+            part(t, h)
+
+    def first(t, h):
+        stage[0] = "phase1x%d" % h
+        acc((hc("K", h, 0, 128), v("ONb", two), v("CK", two, slice(0, 128))), new=True)
+        do(t, h, ("spread", spread), *[("phase1x", phase1x), ("phase1r", phase1r)][::-1 if CFG["RFIRST"][h] and t else 1])
+        if t + 1 < TV and h == 0:
+            stage[0] = "reps"
+            reps(t + 1)
+
+    def second(t, h):
+        do(t, h, ("near", near), ("phase2g", phase2g), ("far", far), ("rivals", rivals))
+
+    def third(t, h):
+        do(t, h, ("phase2", phase2), ("pick", pick), ("winners", winners), ("rows", rows))
         if t + 1 < TV:
-            stage[0] = "count"
-            count(t)
-        else:
-            dma("Y", T["yl"][:], v("LY")["ap"], reads=[v("LY")])
-            dma("Y", T["yz"][:], v("ZBo%d" % t)["ap"], reads=[v("ZBo%d" % t)])
-    dma("Y", T["yr"][:], T["RW"][:, 0:W], reads=[cols("RW", 0, W)])
+            do(t, h, ("leave", leave))
+        do(t, h, ("write", write))
 
-    n = len(ops)
+    for t in range(TV):
+        for part, h in ([(p, h) for h in range(2) for p in (first, second, third)] if GS else
+                        [(p, h) for p in (first, second, third) for h in range(2)]):
+            stage[1] = t
+            part(t, h)
+
     if "order" not in ORDER:
-        succ, need, tail, ready = [[] for _ in range(n)], [0] * n, [0.0] * n, [0.0] * n
-        for o in ops:
-            pre = o["deps"] | o["order"]
-            need[o["i"]] = len(pre)
-            for d in pre:
-                succ[d].append(o["i"])
-        for i in range(n - 1, -1, -1):
-            o = ops[i]
-            tail[i] = o["cost"] + o.get("lat", 0) + o.get("pre", 0) + HOP + max([tail[j] for j in succ[i]] + [0.0])
-        pri = [tail[o["i"]] + EARLY.get(o["stage"], 0) for o in ops]
-        avail = {e: [] for o in ops for e in o["eng"]}
-        free = {e: 0.0 for e in avail}
-
-        def put(i):
-            for e in ops[i]["eng"]:
-                avail[e].append(i)
-        for o in ops:
-            if not need[o["i"]]:
-                put(o["i"])
-        order, plan, who = [], [], {}
-        while len(order) < n:
-            best = None
-            for e, lst in avail.items():
-                if e == "V":
-                    lst = [j for j in lst if "costs" not in ops[j] or free["S"] > max(ready[j], free["V"]) + HELP]
-                if lst:
-                    first = min(ready[j] for j in lst)
-                    est = first if e == "R" else max(free[e], first)
-                    if best is None or est < best[0]:
-                        best = (est, e, lst)
-            est, e, lst = best
-            i = max((j for j in lst if ready[j] <= est), key=lambda j: ("costs" not in ops[j] or e != "V", pri[j], -j))
-            order.append(i)
-            o = ops[i]
-            for x in o["eng"]:
-                avail[x].remove(i)
-            who[i] = e
-            fin = est + (o["costs"][e] if "costs" in o else o["cost"]) + o.get("pre", 0)
-            if e != "R":
-                free[e] = fin
-            plan.append((est, fin, e, i))
-            for j in succ[i]:
-                ready[j] = max(ready[j], fin + o.get("lat", 0) + (HOP if i in ops[j]["deps"] or e == "R" else 0.0))
-                need[j] -= 1
-                if not need[j]:
-                    put(j)
-        ORDER["order"], ORDER["plan"], ORDER["who"], ORDER["ops"] = order, plan, who, ops
+        ORDER.update(_plan(ops))
     order, who = ORDER["order"], ORDER["who"]
 
     que = {"V": V, "S": S, "P": P, "G": g, "Y": g.sync}
@@ -654,3 +698,131 @@ def rank_program(g, core, T, topo):
     for s, x in count_.items():
         g.wait_ge(T.sem[s], x)
     g.wait_ge(T.sem["snt"], sent)
+
+
+def _after(xs, x):
+    lo, hi = 0, len(xs)
+    while lo < hi:
+        mid = (lo + hi) // 2
+        if xs[mid] > x:
+            hi = mid
+        else:
+            lo = mid + 1
+    return lo
+
+
+def _lay(ops, nxt, need, key, who):
+    n, need = len(ops), list(need)
+    ready, start, fin, new = [0.0] * n, [0.0] * n, [0.0] * n, [None] * n
+    slots = {e: ([], []) for e in "VSPGY"}
+    free = sorted((-key[i], i) for i in range(n) if not need[i])
+    while free:
+        i = free.pop()[1]
+        o, best = ops[i], None
+        for e in (who[i] if who else o["eng"]):
+            c = o["costs"][e] if "costs" in o else o["cost"]
+            at, q = ready[i], 0
+            if e != "R":
+                a, b = slots[e]
+                q = _after(b, at)
+                while q < len(a) and a[q] < at + c:
+                    at = max(at, b[q])
+                    q += 1
+            late = at + c + (CFG["HELP"] if "costs" in o and e == "V" else 0)
+            if best is None or late < best[0]:
+                best = (late, e, at, c, q)
+        _, e, at, c, q = best
+        if e != "R":
+            slots[e][0].insert(q, at)
+            slots[e][1].insert(q, at + c)
+        new[i], start[i], fin[i] = e, at, at + c
+        for j, lag in nxt[i]:
+            ready[j] = max(ready[j], fin[i] + lag)
+            need[j] -= 1
+            if not need[j]:
+                free.insert(_after(free, (-key[j], j)), (-key[j], j))
+    return max(fin[i] + ops[i].get("lat", 0) for i in range(n)), start, fin, new
+
+
+def _plan(ops):
+    n = len(ops)
+    fw, bw = [[] for _ in range(n)], [[] for _ in range(n)]
+    for j, o in enumerate(ops):
+        for i in sorted(o["deps"] | o["order"]):
+            lag = ops[i].get("lat", 0) + o.get("pre", 0) + (CFG["HOP"] if i in o["deps"] else 0.0)
+            fw[i].append((j, lag))
+            bw[j].append((i, lag))
+    nf, nb = [len(x) for x in bw], [len(x) for x in fw]
+    tail = [0.0] * n
+    for i in range(n - 1, -1, -1):
+        tail[i] = ops[i]["cost"] + max([tail[j] + lag for j, lag in fw[i]] + [ops[i].get("lat", 0)])
+    key, best, cur, seed = [-x for x in tail], None, None, [CFG["SEED"]]
+    parts = sorted({o["stage"] for o in ops})
+
+    def draw():
+        seed[0] = (seed[0] * 6364136223846793005 + 1442695040888963407) % 2 ** 64
+        return (seed[0] >> 11) / 2.0 ** 53
+    for _ in range(CFG["PASS"]):
+        r = _lay(ops, fw, nf, key, None)
+        back = _lay(ops, bw, nb, [-r[2][i] - ops[i].get("lat", 0) for i in range(n)], r[3])[2]
+        r = min(r, _lay(ops, fw, nf, [-x for x in back], None), key=lambda x: x[0])
+        if cur is None or r[0] < cur[0] + 300:
+            cur = r
+        if best is None or r[0] < best[0]:
+            best = r
+        move = {parts[int(draw() * len(parts))]: (draw() + draw() + draw() - 1.5) * CFG["AMP"] for _ in range(1 + int(draw() * 3))}
+        key = [cur[1][i] + move.get(ops[i]["stage"], 0.0) + (draw() - 0.5) * CFG["AMP"] / 20 for i in range(n)]
+    end, start, fin, who = best
+    order = sorted(range(n), key=lambda i: (start[i], i))
+    return {"order": order, "who": who, "plan": [(start[i], fin[i], who[i], i) for i in order], "ops": ops, "end": end}
+
+
+def _plan0(ops):
+    n, HOP = len(ops), CFG["HOP"]
+    succ, need, tail, ready = [[] for _ in range(n)], [0] * n, [0.0] * n, [0.0] * n
+    for o in ops:
+        pre = o["deps"] | o["order"]
+        need[o["i"]] = len(pre)
+        for d in pre:
+            succ[d].append(o["i"])
+    for i in range(n - 1, -1, -1):
+        o = ops[i]
+        tail[i] = o["cost"] + o.get("lat", 0) + o.get("pre", 0) + HOP + max([tail[j] for j in succ[i]] + [0.0])
+    pri = [tail[o["i"]] + CFG["EARLY"].get(o["stage"], 0) for o in ops]
+    avail = {e: [] for o in ops for e in o["eng"]}
+    free = {e: 0.0 for e in avail}
+
+    def put(i):
+        for e in ops[i]["eng"]:
+            avail[e].append(i)
+    for o in ops:
+        if not need[o["i"]]:
+            put(o["i"])
+    order, plan, who = [], [], {}
+    while len(order) < n:
+        best = None
+        for e, lst in avail.items():
+            if e == "V":
+                lst = [j for j in lst if "costs" not in ops[j] or free["S"] > max(ready[j], free["V"]) + CFG["HELP"]]
+            if lst:
+                first = min(ready[j] for j in lst)
+                est = first if e == "R" else max(free[e], first)
+                if best is None or est < best[0]:
+                    best = (est, e, lst)
+        est, e, lst = best
+        i = max((j for j in lst if ready[j] <= est), key=lambda j: (pri[j], -j))
+        order.append(i)
+        o = ops[i]
+        for x in o["eng"]:
+            avail[x].remove(i)
+        who[i] = e
+        fin = est + (o["costs"][e] if "costs" in o else o["cost"]) + o.get("pre", 0)
+        if e != "R":
+            free[e] = fin
+        plan.append((est, fin, e, i))
+        for j in succ[i]:
+            ready[j] = max(ready[j], fin + o.get("lat", 0) + (HOP if i in ops[j]["deps"] or e == "R" else 0.0))
+            need[j] -= 1
+            if not need[j]:
+                put(j)
+    return {"order": order, "plan": plan, "who": who, "ops": ops}

@@ -9,7 +9,10 @@ BIG, GATE, CONF = 4194304.0, 262144.0, 131072.0
 CEN, TCEN = 1280.0, 2041.0
 MAGIC = 12582912.0
 RIV = 3840.0
-CFG = {"GC": 1.56, "SC": 3.8, "PE": 0.42, "PO": 2.0, "VO": 20.0, "SO": 40.0, "INORDER": (), "LD": (4500, 8000, 10000, 13500), "RWBY": "G", "OWN": 0, "MM": 4, "GS": 0, "TL": (0, 0), "XSUB": {}, "WIDE": 1, "KE": 1, "RFIRST": (0, 1), "HOP": 230.0, "HELP": 1000.0, "XP": 4, "RP": 4, "SEND": 1000.0, "LAT": 2400.0, "PASS": 300, "SEED": 2, "AMP": 4800.0,
+CFG = {"GC": 1.4, "SC": 3.8, "PE": 0.42, "PO": 2.0, "VO": 20.0, "SO": 40.0, "INORDER": (), "LD": (3600, 6200, 7600, 10200), "WT": 3,
+       "XD": (1, 1), "G0": (2, 2), "SELF": 150.0, "RWBY": "GGGG", "OWN": 1, "MM": 8, "GS": 0, "TL": (0, 0), "XSUB": {}, "WIDE": 1,
+       "KE": (2, 2), "RFIRST": (0, 1), "HOP": 260.0, "HELP": 2500.0, "XP": 4, "RP": 4, "SEND": 600.0, "LAT": 1800.0, "PASS": 20,
+       "FINE": 5000, "TEMP": 500.0, "SEED": 2, "AMP": 4800.0,
        "VSUB": {(0, 1): 1, (1, 1): 1}, "VP": 4, "ZBY": ("GGGGGGGG", "GGGGEEEE")}
 CYC = 0.83
 LW = 136
@@ -33,7 +36,7 @@ def _declare():
     B, F, H, I, U = "bfloat16", "float32", "float16", "int32", "uint16"
     sq = [128, 128]
     for h in range(2):
-        for n, s, d in (("XW", [128, W], B), ("RI", [128, W], I), ("RW", [128, W + 16], F)):
+        for n, s, d in (("XW", [128, W], B), ("RI", [128, W], I), ("RW", [128, W + 32], F)):
             _buf("%s_%d" % (n, h), s, d)
     for n, s, d in (("LI", [128, M], I), ("ZI", [128, M], B),
                     ("L0R0", [128, 4096], F), ("L0R1", [128, 4096], F), ("LY", [128, M], F), ("ZY", [128, M], B)):
@@ -49,15 +52,17 @@ def _declare():
                         ("ME", [128, 256], F), ("QE", [128, 257], B), ("OL", [128, 256], H), ("LOF", [128, 16], U), ("EU", [128, 256], U),
                         ("EC", [128, 256], H), ("LTD", [128, 256], H), ("ETD", [128, 256], H), ("NW", [128, 512], F), ("THM", [128, 256], H), ("THG", [8, 128], H),
                         ("GB8", [8, 128], H), ("SCT", sq, H), ("OEE", [128, 256], H), ("LEF", [128, 16], U),
-                        ("XE", [128, 256], B), ("AE", sq, B), ("SG", [128, 256], B), ("NL", [128, 512], F), ("EQ", sq, H),
+                        ("XE", [128, 256], B), ("AE", sq, B), ("SG", [128, 256], B), ("NL", [128, 512], F), ("EQ", [128, 256 if CFG["WT"] >= 2 else 128], H), ("LIM", [128, 256], F),
+                        ("CNT", [128, 256], F), ("SCF", [128, 8], F), ("LAF", [128, 8], F),
                         ("SCU", [128, 32], U), ("ZR", [128, 2048], B), ("Z4", [128, 512], B)):
             _buf("%s_%d" % (n, h), s, d)
     for n, s, d in (("COLS", [128, 16], F), ("AC", [128, 2], F), ("IA", sq, I), ("IB", sq, I), ("IC", sq, I), ("ID", [128, 132], I),
                     ("IQ", [128, 16], F), ("IP", [128, 1], I), ("IG", [8, 128], I), ("GI", sq, F), ("KI", sq, F),
-                    ("DELTA", sq, B), ("BOb", sq, B), ("BOh", sq, H), ("NBOh", sq, H), ("NBR", sq, B), ("Ib", sq, B), ("NIb", sq, B),
+                    ("DELTA", sq, B), ("BOb", sq, B), ("BOh", sq, H), ("NBOh", sq, H), ("NBR", sq, B), ("NBOb", sq, B), ("ROW1", sq, B), ("J2", [128, 256], B), ("J3", [128, 256], B),
+                    ("LOW", [128, 512], B), ("TR3", [128, 256], B), ("TR2", [128, 256], B), ("NB2", [128, 256], H), ("R32", [128, 256], B), ("Ib", sq, B), ("NIb", sq, B),
                     ("HIb", sq, B), ("Ih", sq, H), ("PI", sq, B), ("NI", sq, B), ("TRI", sq, B), ("TRF", sq, F), ("ONb", sq, B),
                     ("SB", [128, 132], B), ("NSB", [128, 132], B), ("SEL0", sq, H), ("SELA", [128, 144], H), ("BLK", [128, 8], B), ("CN", [128, 4], F), ("BLK2", [128, 16], B),
-                    ("BLKC", [128, 8], B), ("CK", [128, 408], B), ("CKE", [128, 256], B), ("EO", sq, B), ("RP", [128, 512], B),
+                    ("BLKC", [128, 8], B), ("CK", [128, 520], B), ("CKE", [128, 256], B), ("EO", sq, B), ("RP", [128, 512], B),
                     ("BC", [128, 16], U), ("BS", [128, 16], U), ("CC1", sq, F), ("CC2", sq, F), ("RMIN", [128, 256], B), ("RMAX", sq, B),
                     ("R4", [128, 512], B), ("TMK", sq, F), ("ONh", sq, H), ("O32", sq, F),
                     ("DEL2", [128, 256], B), ("DUP0", sq, H), ("DUP1", sq, H), ("SD0", sq, H), ("SD1", sq, H),
@@ -72,7 +77,7 @@ _declare()
 SEMAPHORES = ["sV", "sS", "sP", "sG", "snt"] + ["ld%d" % i for i in range(28)]
 for _t in range(1, TV):
     SEMAPHORES += ["l0%d" % _t] + ["l%d_%d" % (_t, h) for h in range(2)]
-CP0, CN0, CD0, CTM, CDUM, CN, CRN = range(7)
+CP0, CP1, CTM, CRN, CDUM = range(5)
 
 
 def rank_program(g, core, T, topo):
@@ -218,6 +223,9 @@ def rank_program(g, core, T, topo):
             return g.iota(out["ap"], pat, base, cm)
         return op("G", 130 + 2 * out["n"] * CYC, [], [out], [f])
 
+    def select(out, a, pat, o, x, base, cm):
+        return op("G", 170 + 2 * out["n"] * CYC, [a], [out], [lambda: g.affine_select(out["ap"], a["ap"], pat, o, x, base, cm)])
+
     def gcopy(out, a):
         return op("G", 170 + 2 * out["n"] * CYC, [a], [out],
                   [lambda: g.affine_select(out["ap"], a["ap"], [[0, out["n"]]], OP.is_ge, 0.0, 0, 0)])
@@ -254,8 +262,8 @@ def rank_program(g, core, T, topo):
     GS = CFG["GS"]
     if not GS:
         IN = IN[::-1]
-        for q, name, src, c in (("Y", "LI", "l0", 2200), ("Y", "XW_0", "xt", 4500), ("S", "ZI", "z0", 2500), ("S", "THI", "th", 2500),
-                                ("Y", "RI_0", "ex", 8000)):
+        for q, name, src, c in (("Y", "LI", "l0", 2200), ("Y", "XW_0", "xt", CFG["LD"][0]), ("S", "ZI", "z0", 2500), ("S", "THI", "th", 2500),
+                                ("Y", "RI_0", "ex", CFG["LD"][1])):
             dma(q, v(name)["ap"], T[src][:], writes=[v(name)], cost=c)
     for h in range(2 * GS):
         load("Y", "LI", IN[h], "l0", h, False, 2200)
@@ -290,7 +298,7 @@ def rank_program(g, core, T, topo):
     ts(col(CP0), cols("IA", 0, 1), 0, OP.is_equal)
     ts(v("IB"), v("IB"), 4, OP.arith_shift_right)
     ts(v("BOb"), v("IB"), 0, OP.is_equal)
-    for n, x in (("BOh", 1.0), ("NBOh", -1.0), ("NBR", -RIV / 2)):
+    for n, x in (("BOh", 1.0), ("NBOh", -1.0), ("NBOb", -1.0), ("NBR", -RIV / 2)):
         ts(v(n), v("BOb"), x, OP.mult)
     ts(v("SEL0"), v("BOb"), col(CP0), OP.mult)
     ts(v("BLK"), cols("BOb", 0, 128, 16), 16.0, OP.mult)
@@ -306,8 +314,9 @@ def rank_program(g, core, T, topo):
     act(v("L0B0"), cols("U_0", 0, M), AF.Copy, bias=CEN)
     send([(v("L0B0"), v("L0B%d" % t), 2) for t in range(1, TV)], ["l0%d" % t for t in range(1, TV)],
          [T.cores[(rank + STEP * t) % N] for t in range(1, TV)])
-    for k in range(16):
-        either(cols("L0R0", k, 4096, 16), v("L0B0"))
+    for h in range(2):
+        for k in range(16):
+            (gcopy if k < CFG["G0"][h] else either)(cols("L0R0", 2048 * h + k, 2048 * h + 2048, 16), cols("L0B0", HM * h, HM * h + HM))
     gcopy(cols("L0R1", 0, 4096, 16), v("L0B0"))
     iota(v("GI"), [[-32768, 8], [0, 16]], 0, 0, True)
     iota(v("KI"), [[0, 8], [1, 16]], 65536, 0, True)
@@ -336,49 +345,76 @@ def rank_program(g, core, T, topo):
     iota(v("CKE", one), [[0, 16], [1, 16]], 0, 0, True)
     fill(v("RMAX"), 1.0)
     fill(cols("RMAX", 0, 128, 16), 0.0)
-    fill(v("RMIN"), 0.0)
-    fill(cols("RMIN", 0, 256, 16), BIG)
-    fill(v("R4"), -BIG)
-    fill(cols("R4", 0, 512, 4), BIG)
+    iota(v("LOW"), [[0, 512]], -int(BIG), 0, True)
+    select(v("RMIN"), cols("LOW", 0, 256), [[0, 16], [1, 16]], OP.not_equal, BIG, 0, 0)
+    select(v("R4"), v("LOW"), [[0, 128], [1, 4]], OP.not_equal, BIG, 0, 0)
     fill(v("RP", one), 0.0)
     fill(v("RP", one, slice(0, 512, 4)), GATE)
     fill(v("RP", one, slice(1, 512, 4)), GATE)
     iota(v("IP"), [[0, 1]], 0, 1)
     ts(v("IP"), v("IP"), 15, OP.bitwise_and)
     ts(col(CDUM), v("IP"), float(W), OP.add)
-    ts(col(CRN), v("IP"), 65536.0, OP.add)
-    ts(v("TRF"), v("KI"), col(CRN), OP.is_ge, -7 * RIV, OP.mult)
-    ts(v("TRI"), v("DELTA"), -RIV, OP.mult)
-    tt(v("TRI"), v("TRI"), v("TRF"), OP.add)
+    if CFG["WT"] < 2:
+        ts(col(CRN), v("IP"), 65536.0, OP.add)
+    if CFG["WT"] >= 2:
+        ts(col(CDUM + 1), v("IP"), W + 16.0, OP.add)
+        cp(col(CRN), v("IP"))
+        iota(v("J2"), [[-16, 2], [0, 4], [1, 32]], 0, 0, True)
+        ts(v("TR2"), v("J2"), col(CRN), OP.is_gt, RIV, OP.mult)
+        ts(v("TR3"), v("J2"), col(CRN), OP.is_equal, -RIV if CFG["WT"] == 2 else -2.0, OP.mult)
+        iota(v("J3"), [[0, 256]], -1, 0, True)
+        select(v("NB2"), v("J3"), [[-16, 2], [-32, 4], [0, 32]], OP.is_ge, 0.0, 0, 1)
+        select(v("NB2"), v("NB2"), [[16, 2], [32, 4], [0, 32]], OP.is_ge, 0.0, 15, -1)
+        ts(col(CP1), v("IP"), 1, OP.is_equal)
+        if CFG["WT"] == 2:
+            ts(col(CDUM + 2), v("IP"), 1, OP.is_le)
+            ts(v("ROW1"), v("BOb"), col(CDUM + 2), OP.mult, -RIV / 2, OP.mult)
+        ts(v("O32"), v("ONb"), col(CP1), OP.mult, 0.5, OP.mult)
+        if CFG["WT"] == 2:
+            fill(v("R32"), 1.0)
+        else:
+            ts(v("R32"), v("TR3"), 1.0, OP.add)
+            fill(v("CK", one, slice(392, 520)), 2048.0)
+        fill(cols("R32", 0, 256, 32), 0.0)
+    else:
+        fill(v("O32"), 1.0 / 32)
+        ts(v("TRF"), v("KI"), col(CRN), OP.is_ge, -7 * RIV, OP.mult)
+        ts(v("TRI"), v("DELTA"), -RIV, OP.mult)
+        tt(v("TRI"), v("TRI"), v("TRF"), OP.add)
     iota(v("ID"), [[-1, 132]], 512, 1)
     ts(v("ID"), v("ID"), 15, OP.bitwise_and)
     ts(v("SB"), v("ID"), 0, OP.is_equal)
     ts(v("NSB"), v("ID"), 0, OP.not_equal)
-    fill(v("O32"), 1.0 / 32)
-    fill(cols("CN", 0, 1), TCEN - 0.5)
+    fill(cols("CN", 0, 1), TCEN - 0.5 + (2048.0 if CFG["WT"] == 3 else 0.0))
     iota(v("IG"), [[0, 2], [1, 4], [0, 16]] if GS else [[1, 8], [0, 16]], 0, -1)
     ts(v("THF"), v("THI"), -1.0, OP.mult, TCEN, OP.add)
     cp(v("THH"), v("THF"))
-    fill(v("ONh", slice(0, 8)), 1.0)
-    ts(v("TMK"), v("DELTA"), -60000.0, OP.mult, 30000.0, OP.add)
+    if CFG["WT"] < 2:
+        fill(v("ONh", slice(0, 8)), 1.0)
+        ts(v("TMK"), v("DELTA"), -60000.0, OP.mult, 30000.0, OP.add)
     ts(col(CTM), col(CP0), 60000.0, OP.mult, -30000.0, OP.add)
     for h in range(1 + GS):
         gb, tg = v("GB8_%d" % h), v("THG_%d" % h)
         ts(gb, v("IG"), -4 * h, OP.is_equal)
-        ts(tg, gb, v("THF"), OP.mult)
-        acc((hc("U", 1, 0, 128), v("ONh", slice(0, 8)), tg), new=True)
+        if CFG["WT"] < 2:
+            ts(tg, gb, v("THF"), OP.mult)
+            acc((hc("U", 1, 0, 128), v("ONh", slice(0, 8)), tg), new=True)
         acc((hc("U", 1, 128, 129), gb, v("THH")), new=True)
         ts(hc("THM", h, 0, 128), v("ONb"), hc("U", 1, 128, 129), OP.mult, col(CTM), OP.max)
-        tt(hc("THM", h, 128, 256), hc("U", 1, 0, 128), v("TMK"), OP.max)
+        if CFG["WT"] == 3:
+            ts(hc("THM", h, 128, 256), v("ONb"), hc("U", 1, 128, 129), OP.mult)
+        if CFG["WT"] < 2:
+            tt(hc("THM", h, 128, 256), hc("U", 1, 0, 128), v("TMK"), OP.max)
         for n, x in (("DUP", "Ih"), ("SD", "SEL0")):
             for s in range(2 * GS):
                 cp(v(n + str(h), full, SIDE[s]), v(x, full, SIDE[h]))
-    cp(cols("DEL2", 0, 128), v("DELTA"))
-    cp(cols("DEL2", 128, 256), v("DELTA"))
+    if any(CFG["TL"]):
+        cp(cols("DEL2", 0, 128), v("DELTA"))
+        cp(cols("DEL2", 128, 256), v("DELTA"))
     for h in range(1 + GS):
         stage[0] = "rw%d" % h
         for q in range(4):
-            {"V": cp, "G": gcopy}[CFG["RWBY"]](hc("RW", h, 640 * q, 640 * q + 640), hc("RI", h, 640 * q, 640 * q + 640))
+            {"V": cp, "G": gcopy}[CFG["RWBY"][q]](hc("RW", h, 640 * q, 640 * q + 640), hc("RI", h, 640 * q, 640 * q + 640))
 
     def table(t, h):
         return hc("RW", h, 0, W) if t else hc("RI", h)
@@ -394,7 +430,7 @@ def rank_program(g, core, T, topo):
 
     def sizes(t, h, G, D, k0, out, blk):
         for c in range(4):
-            bank = "D%d" % (h if CFG["OWN"] else c % 2)
+            bank = ("D0", "D1", "U_%d" % h if CFG["OWN"] & 1 else "D0", "D0" if CFG["OWN"] & 1 else "D1")[c]
             ks = [k for k in range(4 * c, 4 * c + 4) if k >= k0]
             for k in ks:
                 o = cols(bank, 128 * (k % 4), 128 * (k % 4) + 128)
@@ -470,6 +506,8 @@ def rank_program(g, core, T, topo):
         ts(hc("LOF", h), hc("K", h, 256, 272), CEN, OP.add)
         cp(hc("EU", h), ind(table(t, h), hc("LOF", h)))
         ts(hc("EC", h), hc("EU", h), -CEN, OP.add)
+        if not CFG["WT"]:
+            ts(hc("LAC", h), hc("LOF", h, 0, 8), -CEN, OP.add)
 
     def far(t, h):
         key = hc("W", h, 256, 384)
@@ -486,7 +524,23 @@ def rank_program(g, core, T, topo):
         if not CFG["TL"][0]:
             acc((o, ola, v("BOh")), new=True)
             tt(hc("LTD", h, 0, 128), o, v("DELTA"), OP.mult)
-        acc((d, v("Ib"), v("TRI")), (d, v("NBOh"), ola), (d, hc("LTD", h, 0, 128), v("BOh")), new=True)
+        if CFG["WT"] == 3:
+            for r in range(2):
+                ts(hc("LAF", h, 4 * r, 4 * r + 4), hc("LOF", h, r, 8, 2), 1.0 / 4096, OP.mult, 1.0, OP.add)
+            d = hc("K", h, 0, 256)
+            acc((d, v("Ib"), v("TR2")), (d, hc("LTD", h, 0, 128), v("NB2")),
+                *[(hc("K", h, 128 * r, 128 * r + 128), v("BOh"), ola) for r in range(2)], new=True)
+            if t and not h:
+                ts(cols("CN", t, t + 1), cols("ZB%d" % t, LW + HM, LW + HM + 1), TCEN + 31.0 + 2048.0, OP.add)
+            ts(hc("LIM", h), d, 0.0, OP.is_equal, cols("CN", t, t + 1), OP.mult)
+        elif CFG["WT"] == 2:
+            for r in range(2):
+                cp(hc("LAF", h, 4 * r, 4 * r + 4), hc("LOF", h, r, 8, 2))
+            d = hc("K", h, 0, 256)
+            acc((d, v("Ib"), v("TR2")), (d, v("Ib"), v("TR3")), (d, hc("LTD", h, 0, 128), v("NB2")),
+                *[(hc("K", h, 128 * r, 128 * r + 128), v("BOh"), ola) for r in range(2)], new=True)
+        else:
+            acc((d, v("Ib"), v("TRI")), (d, v("NBOh"), ola), (d, hc("LTD", h, 0, 128), v("BOh")), new=True)
         if not GS:
             acc((o, v("Ih"), hc("EC", h, 0, 128)), (o, v("NI"), cols("SB", t, t + 128)), new=True)
             o = hc("U", h, 384, 512)
@@ -524,7 +578,7 @@ def rank_program(g, core, T, topo):
                     sizes(t, h, G, D, 0, lambda k: [out(k)], v("BLK"))
                     continue
                 for c in range(4):
-                    o = v("D%d" % (h if CFG["OWN"] else c % 2))
+                    o = v(("D0", "D1", "U_%d" % h if CFG["OWN"] & 2 else "D0", "D0" if CFG["OWN"] & 2 else "D1")[c])
                     acc((o, v("NIb"), hc("ZR", h, 512 * c, 512 * c + 512)), new=True)
                     acc((o, v("Ib"), hc(G, h, 512 * c, 512 * c + 512)))
                     act(hc(D, h, 512 * c, 512 * c + 512), o, AF.Abs)
@@ -546,8 +600,8 @@ def rank_program(g, core, T, topo):
 
     def pick(t, h):
         scan(hc("ME", h), v("RMIN"), hc("W", h, 0, 256), OP.max, OP.min)
-        if CFG["KE"]:
-            either(hc("KE", h), hc("W", h, 0, 256))
+        if CFG["KE"][h]:
+            (cp if CFG["KE"][h] == 2 else either)(hc("KE", h), hc("W", h, 0, 256))
             tt(hc("QE", h, 0, 256), ind(hc("ME", h), v("BC")), hc("KE", h), OP.is_equal)
             for l in range(2):
                 acc((hc("U", h, 128 * l, 128 * l + 128), hc("QE", h, 128 * l, 128 * l + 128), v("Ib")), new=True)
@@ -561,18 +615,42 @@ def rank_program(g, core, T, topo):
         else:
             lists(hc("U", h, 256, 272), "OEE_%d" % h, 0, 256, True)
         ts(hc("LEF", h), hc("U", h, 256, 272), CEN, OP.add)
-        either(hc("XE", h), ind(hc("XW", h), hc("LEF", h)))
         xa, xb = hc("XE", h, 0, 128), hc("XE", h, 128, 256)
-        o = hc("W", h, 0, 128)
-        acc((o, v("Ib"), xa), (o, v("NIb"), xb), new=True)
-        act(hc("AE", h), o, AF.Abs)
-        acc((hc("W", h, 128, 384), v("Ih"), hc("THM", h)), (hc("W", h, 128, 256), v("BOb"), hc("AE", h)),
-            (hc("W", h, 256, 384), hc("AE", h), v("BOb")), new=True)
-        if t and not h:
+        nat, tr = hc("W", h, 128, 256), hc("W", h, 256, 384)
+        if CFG["XD"][h]:
+            cp(xb, ind(hc("XW", h), hc("LEF", h, 8, 16)))
+            tt(xa, ind(hc("XW", h), hc("LEF", h, 0, 8)), xb, OP.subtract)
+            ts(hc("AE", h), xa, 0.0, OP.max, 2.0, OP.mult)
+            if CFG["WT"] == 3:
+                both = ((hc("K", h, 256, 384), 128), (nat, 0))
+                for o, at in both:
+                    acc((o, v("Ih"), hc("THM", h, at, at + 128)), (o, v("ONb", one), v("CK", one, slice(392, 520))), new=True)
+                for x, y in (("NBOb", xa), ("BOb", hc("AE", h))):
+                    for o, at in both:
+                        acc((o, v(x), y))
+            elif CFG["WT"] == 2:
+                acc((nat, v("Ih"), hc("THM", h, 0, 128)), new=True)
+                acc((nat, v("NBOb"), xa))
+                acc((nat, v("BOb"), hc("AE", h)))
+            else:
+                acc((hc("W", h, 128, 384), v("Ih"), hc("THM", h)), new=True)
+                acc((nat, v("NBOb"), xa), (tr, xa, v("NBOb")))
+                acc((nat, v("BOb"), hc("AE", h)), (tr, hc("AE", h), v("BOb")))
+        else:
+            either(hc("XE", h), ind(hc("XW", h), hc("LEF", h)))
+            o = hc("W", h, 0, 128)
+            acc((o, v("Ib"), xa), (o, v("NIb"), xb), new=True)
+            act(hc("AE", h), o, AF.Abs)
+            if CFG["WT"] == 2:
+                acc((nat, v("Ih"), hc("THM", h, 0, 128)), (nat, v("BOb"), hc("AE", h)), new=True)
+            else:
+                acc((hc("W", h, 128, 384), v("Ih"), hc("THM", h)), (nat, v("BOb"), hc("AE", h)), (tr, hc("AE", h), v("BOb")), new=True)
+        if t and not h and CFG["WT"] < 3:
             ts(cols("CN", t, t + 1), cols("ZB%d" % t, LW + HM, LW + HM + 1), TCEN + 31.0, OP.add)
-        act(hc("SG", h), hc("W", h, 128, 384), AF.Sign, scale=-1.0, bias=cols("CN", t, t + 1), accum_out=cols("AC", h, h + 1))
+        wide = 128 if CFG["WT"] >= 2 else 256
+        act(hc("SG", h, 0, wide), hc("W", h, 128, 128 + wide), AF.Sign, scale=-1.0, bias=cols("CN", t, t + 1), accum_out=cols("AC", h, h + 1))
         o = hc("W", h, 384, 512)
-        acc((o, v("ONb", one), v("CK", one, slice(256, 384))), (o, v("HIb"), xa), (o, v("HIb"), xb), new=True)
+        acc((o, v("ONb", one), v("CK", one, slice(256, 384))), (o, v("HIb"), xa), (o, v("Ib" if CFG["XD"][h] else "HIb"), xb), new=True)
         zo = cols("ZBo%d" % t, LW * (1 - h), LW * (1 - h) + HM) if t < TV - 1 else v("ZY", full, IN[h])
         ts(zo, o, MAGIC, OP.add, -MAGIC, OP.add)
 
@@ -599,9 +677,30 @@ def rank_program(g, core, T, topo):
               (cols("ZBo%d" % t, LW * (1 - h), LW * (1 - h) + wide), cols("ZB%d" % (t + 1), LW * h, LW * h + wide), 4)], ["l%d_%d" % (t + 1, h)])
 
     def winners(t, h):
+        if CFG["WT"] == 3:
+            for r in range(2):
+                tt(dict(hc("EQ", h, 128 * r, 128 * r + 128)), hc("K", h, 256, 384), hc("LIM", h, 128 * r, 128 * r + 128), OP.is_lt)
+            scan(hc("CNT", h), v("R32"), hc("EQ", h), OP.mult, OP.add)
+            tt(hc("SCF", h), hc("LAF", h), hc("CNT", h, 31, 256, 32), OP.subtract)
+            for r in range(2):
+                ts(dict(hc("SCU", h, r, 8, 2), lane=r), hc("SCF", h, 4 * r, 4 * r + 4), 4096.0, OP.mult, col(CDUM + r), OP.min)
+            return
+        if CFG["WT"] == 2:
+            acc(*[(hc("K", h, 128 * r, 128 * r + 128), v("ROW1"), hc("SG", h, 0, 128)) for r in range(2)])
+            ts(hc("EQ", h), hc("K", h, 0, 256), 0.0, OP.is_equal, RIV, OP.mult)
+            scan(hc("CNT", h), v("R32"), hc("EQ", h), OP.mult, OP.add)
+            tt(hc("SCF", h), hc("CNT", h, 31, 256, 32), hc("LAF", h), OP.add)
+            for r in range(2):
+                ts(dict(hc("SCU", h, r, 8, 2), lane=r), hc("SCF", h, 4 * r, 4 * r + 4), col(CDUM + r), OP.min)
+            return
         d = hc("K", h, 272, 400)
         acc((d, hc("SG", h, 128, 256), v("NBR")))
         ts(hc("EQ", h), d, 0.0, OP.is_equal, RIV, OP.mult)
+        if not CFG["WT"]:
+            acc((hc("K", h, 128, 136), v("Ih"), hc("LAC", h)), new=True)
+            lists(hc("K", h, 128, 136), "EQ_%d" % h, 0, 128)
+            ts(hc("SCU", h, 0, 16, 2), hc("K", h, 128, 136), CEN, OP.add, col(CDUM), OP.min)
+            return
         o = hc("K", h, 0, 128)
         acc((o, hc("OL", h, 0, 128), v("BOh")), (o, hc("EQ", h), v("BOh")), new=True)
         tt(hc("SCT", h), o, v("DELTA"), OP.mult)
@@ -616,7 +715,9 @@ def rank_program(g, core, T, topo):
 
     def write(t, h):
         n = 128 + 128 * GS
-        for b in range(n // 16 - 1, -1, -1):
+        for q in range(3, -1, -1) if CFG["WT"] >= 2 else ():
+            tt(ind(hc("RW", h), hc("SCU", h, 2 * q, 2 * q + 2)), hc("NW", h, 32 * q, 32 * q + 32), hc("NW", h, n + 32 * q, n + 32 + 32 * q), OP.max)
+        for b in range(n // 16 - 1, -1, -1) if CFG["WT"] < 2 else ():
             tt(ind(hc("RW", h), hc("SCU", h, 2 * b, 2 * b + 1)), hc("NW", h, 16 * b, 16 * b + 16), hc("NW", h, n + 16 * b, n + 16 + 16 * b), OP.max)
         if t == TV - 1 and h and not GS:
             dma("S", T["yl"][:], v("LY")["ap"], reads=[v("LY")])
@@ -713,7 +814,7 @@ def _after(xs, x):
 
 def _lay(ops, nxt, need, key, who):
     n, need = len(ops), list(need)
-    ready, start, fin, new = [0.0] * n, [0.0] * n, [0.0] * n, [None] * n
+    ready, start, fin, new = [dict.fromkeys(o["eng"], 0.0) for o in ops], [0.0] * n, [0.0] * n, [None] * n
     slots = {e: ([], []) for e in "VSPGY"}
     free = sorted((-key[i], i) for i in range(n) if not need[i])
     while free:
@@ -721,7 +822,7 @@ def _lay(ops, nxt, need, key, who):
         o, best = ops[i], None
         for e in (who[i] if who else o["eng"]):
             c = o["costs"][e] if "costs" in o else o["cost"]
-            at, q = ready[i], 0
+            at, q = ready[i][e], 0
             if e != "R":
                 a, b = slots[e]
                 q = _after(b, at)
@@ -736,12 +837,42 @@ def _lay(ops, nxt, need, key, who):
             slots[e][0].insert(q, at)
             slots[e][1].insert(q, at + c)
         new[i], start[i], fin[i] = e, at, at + c
-        for j, lag in nxt[i]:
-            ready[j] = max(ready[j], fin[i] + lag)
+        for j, lag, near in nxt[i]:
+            for x in ready[j]:
+                ready[j][x] = max(ready[j][x], fin[i] + (near if x == e else lag))
             need[j] -= 1
             if not need[j]:
                 free.insert(_after(free, (-key[j], j)), (-key[j], j))
     return max(fin[i] + ops[i].get("lat", 0) for i in range(n)), start, fin, new
+
+
+def _relay(prv, turn, key, who, cost, lat):
+    key, start, fin = list(key), [0.0] * len(key), [0.0] * len(key)
+    for i in turn:
+        for j, _, _ in prv[i]:
+            if key[j] >= key[i]:
+                key[i] = key[j] + 0.001
+    slots = {e: ([], []) for e in "VSPGYR"}
+    for i in sorted(turn, key=lambda i: key[i]):
+        e, at = who[i], 0.0
+        c = cost[i][e]
+        for j, lag, near in prv[i]:
+            x = fin[j] + (near if who[j] == e else lag)
+            if x > at:
+                at = x
+        if e != "R":
+            a, b = slots[e]
+            q = m = len(b)
+            while q and b[q - 1] > at:
+                q -= 1
+            while q < m and a[q] < at + c:
+                if b[q] > at:
+                    at = b[q]
+                q += 1
+            a.insert(q, at)
+            b.insert(q, at + c)
+        start[i], fin[i] = at, at + c
+    return max(x + y for x, y in zip(fin, lat)), start, fin, who
 
 
 def _plan(ops):
@@ -749,13 +880,13 @@ def _plan(ops):
     fw, bw = [[] for _ in range(n)], [[] for _ in range(n)]
     for j, o in enumerate(ops):
         for i in sorted(o["deps"] | o["order"]):
-            lag = ops[i].get("lat", 0) + o.get("pre", 0) + (CFG["HOP"] if i in o["deps"] else 0.0)
-            fw[i].append((j, lag))
-            bw[j].append((i, lag))
+            lag = [ops[i].get("lat", 0) + o.get("pre", 0) + (CFG[x] if i in o["deps"] else 0.0) for x in ("HOP", "SELF")]
+            fw[i].append((j, *lag))
+            bw[j].append((i, *lag))
     nf, nb = [len(x) for x in bw], [len(x) for x in fw]
     tail = [0.0] * n
     for i in range(n - 1, -1, -1):
-        tail[i] = ops[i]["cost"] + max([tail[j] + lag for j, lag in fw[i]] + [ops[i].get("lat", 0)])
+        tail[i] = ops[i]["cost"] + max([tail[j] + lag for j, lag, _ in fw[i]] + [ops[i].get("lat", 0)])
     key, best, cur, seed = [-x for x in tail], None, None, [CFG["SEED"]]
     parts = sorted({o["stage"] for o in ops})
 
@@ -772,6 +903,38 @@ def _plan(ops):
             best = r
         move = {parts[int(draw() * len(parts))]: (draw() + draw() + draw() - 1.5) * CFG["AMP"] for _ in range(1 + int(draw() * 3))}
         key = [cur[1][i] + move.get(ops[i]["stage"], 0.0) + (draw() - 0.5) * CFG["AMP"] / 20 for i in range(n)]
+    like, seen, runs = {}, {}, {}
+    for i, o in enumerate(ops):
+        x = (o["stage"], o["t"])
+        seen[x] = seen.get(x, 0) + 1
+        like.setdefault((o["stage"], seen[x]), []).append(i)
+    for x in like:
+        runs.setdefault(x[0], []).append(like[x])
+    both = [x for x in like.values() if all("costs" in ops[i] for i in x)]
+    cur, up, lat = best, list(range(n)), [o.get("lat", 0) for o in ops]
+    cost = [o.get("costs") or {o["eng"]: o["cost"]} for o in ops]
+    for it in range(CFG["FINE"]):
+        key, who, u = list(cur[1]), cur[3], draw()
+        if it % 50 == 49:
+            key = [-x for x in _relay(fw, up[::-1], [-x - y for x, y in zip(cur[2], lat)], who, cost, lat)[2]]
+        elif u < 0.2:
+            x = both[int(draw() * len(both))]
+            who, e = list(who), "V" if who[x[-1]] == "S" else "S"
+            for i in (x if draw() < 0.7 else [x[int(draw() * len(x))]]):
+                who[i] = e
+        else:
+            run = runs[parts[int(draw() * len(parts))]]
+            a = int(draw() * len(run)) if draw() < 0.7 else 0
+            d = (draw() + draw() + draw() - 1.5) * (600, 2000, 6000)[int(draw() * 3)]
+            t = int(draw() * TV) if draw() < 0.4 else None
+            for x in run[a:a + (1, 2, 4, 8, 99)[int(draw() * 5)]]:
+                for i in x:
+                    if t is None or ops[i]["t"] == t:
+                        key[i] += d
+        r = _relay(bw, up, key, who, cost, lat)
+        if r[0] < cur[0] + CFG["TEMP"] * (1 - it / CFG["FINE"]) * draw() ** 2:
+            cur = r
+            best = min(best, r, key=lambda x: x[0])
     end, start, fin, who = best
     order = sorted(range(n), key=lambda i: (start[i], i))
     return {"order": order, "who": who, "plan": [(start[i], fin[i], who[i], i) for i in order], "ops": ops, "end": end}

@@ -8,12 +8,11 @@ W, M, HM, TV, STEP = 2560, 256, 128, 4, 3
 BIG, GATE, CONF = 4194304.0, 262144.0, 131072.0
 CEN, TCEN = 1280.0, 2041.0
 MAGIC = 12582912.0
-RIV = 3840.0
-CFG = {"GC": 1.4, "SC": 3.8, "PE": 0.42, "PO": 2.0, "VO": 20.0, "SO": 40.0, "INORDER": (), "LD": (3600, 6200, 7600, 10200), "WT": 3,
-       "XD": (1, 1), "G0": (2, 2), "SELF": 150.0, "RWBY": "GGGG", "OWN": 1, "MM": 8, "GS": 0, "TL": (0, 0), "XSUB": {}, "WIDE": 1,
-       "KE": (2, 2), "RFIRST": (0, 1), "HOP": 260.0, "HELP": 2500.0, "XP": 4, "RP": 4, "SEND": 600.0, "LAT": 1800.0, "PASS": 20,
-       "FINE": 5000, "TEMP": 500.0, "SEED": 2, "AMP": 4800.0,
-       "VSUB": {(0, 1): 1, (1, 1): 1}, "VP": 4, "ZBY": ("GGGGGGGG", "GGGGEEEE")}
+RIV, APART = 3840.0, 8192.0
+CFG = {"GC": 1.4, "SC": 3.8, "PE": 0.42, "PO": 2.0, "VO": 20.0, "SO": 40.0, "LD": (3600, 6200, 7600, 10400), "GS": 0, "MEAN": 0.0, "SAME": 0.5, "XD": (2, 2), "ZS": (0, 0), "P1": (1, 1),
+       "B1": "oUoU", "B2": "oUoU", "BZ": "o", "BF": "o", "EU2": 1, "HORN": (1, 1), "AFTER": (("phase2g0", "near1"),), "ZSEP": (0, 0), "G0": (2, 2), "SELF": 150.0, "MM": 8, "RFIRST": (0, 1), "HOP": 260.0, "HELP": 1500.0, "XP": 4, "RP": 4,
+       "SEND": 600.0, "LAT": 1800.0, "PASS": 20, "FINE": 7000, "TEMP": 500.0, "CRIT": 0.6, "SEED": 3, "AMP": 4800.0, "VP": 4,
+       "ZBY": ("GSV", "GSV", "GSV")}
 CYC = 0.83
 LW = 136
 
@@ -23,7 +22,7 @@ WHAT, AT = {}, {}
 
 def _buf(name, shape, dtype, where="sbuf"):
     WHAT[name] = (where, shape, dtype)
-    if where == "psum" or len(shape) > 2 or shape[1] > 2048:
+    if where == "psum" or shape[1] > 2048:
         SCRATCH[name] = WHAT[name]
         return
     host = "all_" + dtype
@@ -34,39 +33,37 @@ def _buf(name, shape, dtype, where="sbuf"):
 
 def _declare():
     B, F, H, I, U = "bfloat16", "float32", "float16", "int32", "uint16"
-    sq = [128, 128]
+    sq, dq, wide = [128, 128], [128, 256], [128, 2048]
     for h in range(2):
         for n, s, d in (("XW", [128, W], B), ("RI", [128, W], I), ("RW", [128, W + 32], F)):
             _buf("%s_%d" % (n, h), s, d)
-    for n, s, d in (("LI", [128, M], I), ("ZI", [128, M], B),
-                    ("L0R0", [128, 4096], F), ("L0R1", [128, 4096], F), ("LY", [128, M], F), ("ZY", [128, M], B)):
+        for n, s, d in (("DUP", sq, H), ("SD", sq, H), ("DUN", sq, B), ("GB8", [8, 128], H), ("LAH", [128, 8], H), ("CNB", dq, B)):
+            _buf("%s_%d" % (n, h), s, d)
+    for n, s, d in (("LI", dq, I), ("ZI", dq, B),
+                    ("L0R0", [128, 4096], F), ("L0R1", [128, 4096], F), ("LY", dq, F), ("ZY", dq, B)):
         _buf(n, s, d)
     for t in range(TV):
         for n, d in (("LF", U), ("ZB", B), ("LFo", U), ("ZBo", B)):
             _buf("%s%d" % (n, t), [128, 2 * LW], d)
-        _buf("L0B%d" % t, [128, M], F)
+        _buf("L0B%d" % t, dq, F)
     for h in range(2):
-        for n, s, d in (("GA", [128, 2048], B), ("GB", [128, 2048], B), ("DA", [128, 2048], B), ("DB", [128, 2048], B), ("CF", [128, 2048], B),
-                        ("LC", sq, H), ("M1", sq, F), ("M2", sq, F), ("KEY", sq, F), ("LOSE", sq, F), ("OAB", [128, 256], B), ("MF", sq, F),
-                        ("MG", sq, F), ("KF", sq, F), ("LS", sq, F), ("FF", [128, 256], B), ("LAC", [128, 8], H), ("ML", [128, 16], F), ("KE", [128, 256], F),
-                        ("ME", [128, 256], F), ("QE", [128, 257], B), ("OL", [128, 256], H), ("LOF", [128, 16], U), ("EU", [128, 256], U),
-                        ("EC", [128, 256], H), ("LTD", [128, 256], H), ("ETD", [128, 256], H), ("NW", [128, 512], F), ("THM", [128, 256], H), ("THG", [8, 128], H),
-                        ("GB8", [8, 128], H), ("SCT", sq, H), ("OEE", [128, 256], H), ("LEF", [128, 16], U),
-                        ("XE", [128, 256], B), ("AE", sq, B), ("SG", [128, 256], B), ("NL", [128, 512], F), ("EQ", [128, 256 if CFG["WT"] >= 2 else 128], H), ("LIM", [128, 256], F),
-                        ("CNT", [128, 256], F), ("SCF", [128, 8], F), ("LAF", [128, 8], F),
-                        ("SCU", [128, 32], U), ("ZR", [128, 2048], B), ("Z4", [128, 512], B)):
+        for n, s, d in (("GA", wide, B), ("GB", wide, B), ("DA", wide, B), ("DB", wide, B), ("CF", wide, B), ("ZR", wide, B), ("Z4", [128, 512], B),
+                        ("LC", sq, H), ("M1", sq, F), ("M2", sq, F), ("KEY", sq, F), ("OAB", dq, B), ("MF", sq, F), ("MG", sq, F), ("KF", sq, F),
+                        ("FF", dq, B), ("ME", dq, F), ("QE", [128, 257], B), ("OL", dq, H), ("LOF", [128, 16], U), ("EU", dq, U), ("EC", dq, H),
+                        ("LTD", sq, H), ("NW", [128, 512], F), ("OEE", dq, H), ("LEF", [128, 16], U), ("XE", dq, B), ("AE", sq, B), ("SG", sq, B),
+                        ("NL", [128, 512], F), ("AD", dq, B), ("SN", dq, B), ("CNT", dq, F), ("SCF", [128, 8], F), ("LAF", [128, 8], F),
+                        ("SCU", [128, 16], U), ("ZT", sq, F), ("MK", [128, 512], B)):
             _buf("%s_%d" % (n, h), s, d)
     for n, s, d in (("COLS", [128, 16], F), ("AC", [128, 2], F), ("IA", sq, I), ("IB", sq, I), ("IC", sq, I), ("ID", [128, 132], I),
                     ("IQ", [128, 16], F), ("IP", [128, 1], I), ("IG", [8, 128], I), ("GI", sq, F), ("KI", sq, F),
-                    ("DELTA", sq, B), ("BOb", sq, B), ("BOh", sq, H), ("NBOh", sq, H), ("NBR", sq, B), ("NBOb", sq, B), ("ROW1", sq, B), ("J2", [128, 256], B), ("J3", [128, 256], B),
-                    ("LOW", [128, 512], B), ("TR3", [128, 256], B), ("TR2", [128, 256], B), ("NB2", [128, 256], H), ("R32", [128, 256], B), ("Ib", sq, B), ("NIb", sq, B),
-                    ("HIb", sq, B), ("Ih", sq, H), ("PI", sq, B), ("NI", sq, B), ("TRI", sq, B), ("TRF", sq, F), ("ONb", sq, B),
-                    ("SB", [128, 132], B), ("NSB", [128, 132], B), ("SEL0", sq, H), ("SELA", [128, 144], H), ("BLK", [128, 8], B), ("CN", [128, 4], F), ("BLK2", [128, 16], B),
-                    ("BLKC", [128, 8], B), ("CK", [128, 520], B), ("CKE", [128, 256], B), ("EO", sq, B), ("RP", [128, 512], B),
-                    ("BC", [128, 16], U), ("BS", [128, 16], U), ("CC1", sq, F), ("CC2", sq, F), ("RMIN", [128, 256], B), ("RMAX", sq, B),
-                    ("R4", [128, 512], B), ("TMK", sq, F), ("ONh", sq, H), ("O32", sq, F),
-                    ("DEL2", [128, 256], B), ("DUP0", sq, H), ("DUP1", sq, H), ("SD0", sq, H), ("SD1", sq, H),
-                    ("THI", [8, 1], I), ("THF", [8, 1], F), ("THH", [8, 1], H)):
+                    ("DELTA", sq, B), ("BOb", sq, B), ("BOh", sq, H), ("NBOb", sq, B), ("J2", dq, B), ("J3", dq, B),
+                    ("LOW", dq, B), ("TR2", dq, B), ("NB2", dq, H), ("R32", dq, B), ("Ib", sq, B), ("NIb", sq, B), ("NBOh", sq, H), ("BO2", sq, B),
+                    ("HIb", sq, B), ("Ih", sq, H), ("NIh", sq, H), ("NI", sq, B), ("AI", sq, B), ("ONb", sq, B),
+                    ("LO4", [128, 512], B), ("R4", [128, 512], B), ("RP", [128, 512], B), ("PI", sq, B), ("CNo", [128, 16], F), ("CNi", [128, 16], F),
+                    ("SB", [128, 132], B), ("NSB", [128, 132], B), ("SEL0", sq, H), ("SELA", [128, 144], H), ("BLK", [128, 8], B),
+                    ("CN", [128, 16], F), ("BLK2", [128, 16], B), ("BLKC", [128, 8], B), ("CK", [128, 392], B), ("CKE", dq, B), ("EO", sq, B),
+                    ("BC", [128, 16], U), ("BS", [128, 16], U), ("ML_0", [128, 16], F), ("ML_1", [128, 16], F), ("CC1", sq, F), ("RMIN", dq, B), ("RMAX", sq, B),
+                    ("O32", sq, F), ("THI", [8, 1], I), ("THH", [8, 1], H), ("ONN", sq, B)):
         _buf(n, s, d)
     for k, n in enumerate(("D0", "D1", "K_0", "K_1", "U_0", "U_1", "W_0", "W_1")):
         _buf(n, [128, 512], F, "psum")
@@ -76,8 +73,8 @@ def _declare():
 _declare()
 SEMAPHORES = ["sV", "sS", "sP", "sG", "snt"] + ["ld%d" % i for i in range(28)]
 for _t in range(1, TV):
-    SEMAPHORES += ["l0%d" % _t] + ["l%d_%d" % (_t, h) for h in range(2)]
-CP0, CP1, CTM, CRN, CDUM = range(5)
+    SEMAPHORES += ["l0%d" % _t, "n%d" % _t] + ["%s%d_%d" % (x, _t, h) for x in "lz" for h in range(2)]
+CP0, CP1, CTM, CRN, CDUM, CWIN, CTH = 0, 1, 2, 3, 4, 6, 8
 
 
 def rank_program(g, core, T, topo):
@@ -129,19 +126,23 @@ def rank_program(g, core, T, topo):
             me = (i, wr, a["lo"], a["hi"], a["lane"], a["name"])
             old = hist.setdefault(key, [])
             if a["psum"] and eng == "P":
-                for e in old:
-                    if e[0] != i:
-                        o["order" if ops[e[0]]["eng"] == "P" else "deps"].add(e[0])
-                hist[key] = [e for e in old if e[0] == i] + [me]
+                if key in o["opens"]:
+                    for e in old:
+                        if e[0] != i:
+                            o["order" if ops[e[0]]["eng"] == "P" else "deps"].add(e[0])
+                    hist[key] = [me]
+                else:
+                    o["order"].add(old[0][0])
+                    assert all(ops[e[0]]["eng"] == "P" for e in old if e[0] != i)
+                    old.append(me)
                 continue
             keep = []
             for e in old:
                 if e[0] != i:
-                    if a["psum"] and (ops[e[0]]["eng"] != eng or eng == "VS"):
+                    if a["psum"] and (ops[e[0]]["eng"] != eng or len(eng) > 1):
                         o["deps"].add(e[0])
                     elif (wr or e[1]) and hit(me, e):
-                        same = wr and eng in CFG["INORDER"] and ops[e[0]]["eng"] == eng
-                        o["order" if same else "deps"].add(e[0])
+                        o["deps"].add(e[0])
                         if wr and a["lane"] is None and not a["psum"] and a["lo"] <= e[2] and e[3] <= a["hi"]:
                             continue
                 keep.append(e)
@@ -164,13 +165,14 @@ def rank_program(g, core, T, topo):
             c = cyc(a["n"], False) if (a["psum"] or b["psum"]) else cyc(2 * a["n"], False)
         return op("V", c, rd, [out], [lambda: V.tensor_tensor(out["ap"], a["ap"], b["ap"], o)])
 
+    def raw(x):
+        return x["ap"] if isinstance(x, dict) else x
+
     def tsf(out, a, s1, o1, s2=None, o2=None):
         def f():
-            x1 = s1["ap"] if isinstance(s1, dict) else s1
-            x2 = s2["ap"] if isinstance(s2, dict) else s2
             if o2 is None:
-                return V.tensor_scalar(out["ap"], a["ap"], x1, None, o1)
-            return V.tensor_scalar(out["ap"], a["ap"], x1, x2, o1, o2)
+                return V.tensor_scalar(out["ap"], a["ap"], raw(s1), None, o1)
+            return V.tensor_scalar(out["ap"], a["ap"], raw(s1), raw(s2), o1, o2)
         return f
 
     def ts(out, a, s1, o1, s2=None, o2=None):
@@ -190,29 +192,40 @@ def rank_program(g, core, T, topo):
         c = (65 + a["n"] * GC * CYC) if "ind" in a else a["n"] * CYC + CFG["SO"]
         wr = [out] + ([kw["accum_out"]] if "accum_out" in kw else [])
         return op("S", c, [a] + [x for k, x in kw.items() if k != "accum_out"], wr,
-                  [lambda: S.activation(out["ap"], a["ap"], f, **{k: (x["ap"] if isinstance(x, dict) else x) for k, x in kw.items()})])
+                  [lambda: S.activation(out["ap"], a["ap"], f, **{k: raw(x) for k, x in kw.items()})])
 
-    def either(out, a, add=None):
+    def either(out, a, add=None, mul=None, relu=False):
         k = "ind" in a
         cv = 50 + a["n"] * GC * CYC if k else cyc(a["n"], a["two"] and out["two"])
         cs = 65 + a["n"] * GC * CYC if k else a["n"] * CYC + CFG["SO"]
-        if add is None:
-            fs, fv = (lambda: S.activation(out["ap"], a["ap"], AF.Copy)), (lambda: V.tensor_copy(out["ap"], a["ap"]))
+        if relu:
+            fs, fv = (lambda: S.activation(out["ap"], a["ap"], AF.Relu)), tsf(out, a, 0.0, OP.max)
+        elif mul is not None:
+            fs, fv = (lambda: S.activation(out["ap"], a["ap"], AF.Identity, bias=raw(add), scale=mul)), tsf(out, a, mul, OP.mult, add, OP.add)
+        elif add is not None:
+            fs = lambda: S.activation(out["ap"], a["ap"], AF.Identity if isinstance(add, dict) else AF.Copy, bias=raw(add))
+            fv = tsf(out, a, add, OP.add)
         else:
-            fs, fv = (lambda: S.activation(out["ap"], a["ap"], AF.Copy, bias=add)), tsf(out, a, add, OP.add)
-        return op("VS", cv, [a], [out], [fs], costs={"V": cv, "S": cs}, alt=[fv])
+            fs, fv = (lambda: S.activation(out["ap"], a["ap"], AF.Copy)), (lambda: V.tensor_copy(out["ap"], a["ap"]))
+        return op("VS", cv, [a, add], [out], [fs], costs={"V": cv, "S": cs}, alt={"V": fv, "S": fs})
+
+    def anyone(out, a, by):
+        n = a["n"]
+        fn = {"G": lambda: g.affine_select(out["ap"], a["ap"], [[0, n]], OP.is_ge, 0.0, 0, 0),
+              "V": lambda: V.tensor_copy(out["ap"], a["ap"]), "S": lambda: S.activation(out["ap"], a["ap"], AF.Copy)}
+        c = {"G": 170 + 2 * n * CYC, "V": cyc(n, a["two"] and out["two"]), "S": n * CYC + CFG["SO"]}
+        if len(by) == 1:
+            return op(by, c[by], [a], [out], [fn[by]])
+        return op(by, c[by[0]], [a], [out], [fn[by[0]]], costs={e: c[e] for e in by}, alt=fn)
 
     def pe(*mms):
         c = sum(max(64, m[2]["n"]) * CFG["PE"] * (1 if m[1]["two"] else 4) + CFG["PO"] for m in mms)
         return op("P", c, [x for m in mms for x in (m[1], m[2])], [m[0] for m in mms],
-                  [(lambda m=m: P.matmul(m[0]["ap"], m[1]["ap"], m[2]["ap"], m[3], m[4])) for m in mms])
+                  [(lambda m=m: P.matmul(m[0]["ap"], m[1]["ap"], m[2]["ap"], m[3], m[4])) for m in mms],
+                  opens={BANK[m[0]["name"]] for m in mms if m[3]}, mms=mms)
 
     def acc(*mms, new=False):
-        mms = [list(m) + [new and j == 0, True] for j, m in enumerate(mms)]
-        for m in mms:
-            if not m[3]:
-                latest[m[0]["name"]][4] = False
-            latest[m[0]["name"]] = m
+        mms = [list(m) + [new and j == 0, False] for j, m in enumerate(mms)]
         for j in range(0, len(mms), CFG["MM"]):
             pe(*mms[j:j + CFG["MM"]])
 
@@ -227,17 +240,15 @@ def rank_program(g, core, T, topo):
         return op("G", 170 + 2 * out["n"] * CYC, [a], [out], [lambda: g.affine_select(out["ap"], a["ap"], pat, o, x, base, cm)])
 
     def gcopy(out, a):
-        return op("G", 170 + 2 * out["n"] * CYC, [a], [out],
-                  [lambda: g.affine_select(out["ap"], a["ap"], [[0, out["n"]]], OP.is_ge, 0.0, 0, 0)])
+        return select(out, a, [[0, out["n"]]], OP.is_ge, 0.0, 0, 0)
 
     def dma(q, out, a, reads=(), writes=(), cost=2500):
         k = ndma[0]
         ndma[0] += 1
-        f = {"Y": lambda: g.sync.dma_start(out, a), "S": lambda: S.dma_start(out, a),
-             "G": lambda: g.dma_start(out, a, allow_slow_non_contiguous=True)}[q]
-        return op(q, 60, list(reads), list(writes), [f], dmasem="ld%d" % k, lat=cost)
+        f = {"Y": lambda: g.sync.dma_start(out, a), "S": lambda: S.dma_start(out, a)}[q]
+        latest[q] = [op(q, 60, list(reads), list(writes), [f], dmasem="ld%d" % k, lat=cost, after=latest.get(q, ()))]
 
-    def send(items, sem, dsts=None):
+    def send(items, sem, dsts=None, more=0.0):
         dsts = dsts or [T.cores[(rank + STEP) % N]] * len(items)
         at, tr = 0, []
         for it, d in zip(items, dsts):
@@ -250,32 +261,35 @@ def rank_program(g, core, T, topo):
         s = op("G", CFG["SEND"], [it[0] for it in items], [], [f], remote=at)
         for j, sm in enumerate(sem):
             mine = [it for q, it in enumerate(items) if q % len(sem) == j]
-            op("R", 0, [], [it[1] for it in mine], [], arr=(sm, sum(it[2] for it in mine)), after=[s], pre=CFG["LAT"])
+            op("R", 0, [], [it[1] for it in mine], [], arr=(sm, sum(it[2] for it in mine)), after=[s], pre=CFG["LAT"] + more)
 
-    IN = [slice(0, HM), slice(HM, M)]
+    IN = [slice(HM, M), slice(0, HM)]
+    GS = CFG["GS"]
     SIDE = [slice(0, 64), slice(64, 128)]
+    for q, name, src, c in (("Y", "LI", "l0", 2200), ("Y", "XW_0", "xt", CFG["LD"][0]), ("S", "ZI", "z0", 2500), ("S", "THI", "th", 9000),
+                            ("Y", "RI_0", "ex", CFG["LD"][1])) if not GS else ():
+        dma(q, v(name)["ap"], T[src][:], writes=[v(name)], cost=c)
 
     def load(q, name, cs, src, h, both, cost):
         for s in range(2):
             x = dict(v(name, SIDE[s], cs), lane=s)
             dma(q, x["ap"], T[src][SIDE[h], full if both else IN[s]], writes=[x], cost=cost)
-    GS = CFG["GS"]
-    if not GS:
+    if GS:
         IN = IN[::-1]
-        for q, name, src, c in (("Y", "LI", "l0", 2200), ("Y", "XW_0", "xt", CFG["LD"][0]), ("S", "ZI", "z0", 2500), ("S", "THI", "th", 2500),
-                                ("Y", "RI_0", "ex", CFG["LD"][1])):
-            dma(q, v(name)["ap"], T[src][:], writes=[v(name)], cost=c)
-    for h in range(2 * GS):
-        load("Y", "LI", IN[h], "l0", h, False, 2200)
-        load("S", "ZI", IN[h], "z0", h, False, 2500)
-        if h:
-            dma("S", v("THI")["ap"], T["th"][:], writes=[v("THI")])
-        load("Y", "XW_%d" % h, full, "xt", h, True, CFG["LD"][2 * h])
-        load("Y", "RI_%d" % h, slice(0, W), "ex", h, True, CFG["LD"][2 * h + 1])
+        for h in range(2):
+            load("S", "LI", IN[h], "l0", h, False, 2200)
+            load("Y", "XW_%d" % h, full, "xt", h, True, CFG["LD"][2 * h])
+            load("S", "ZI", IN[h], "z0", h, False, 2500)
+            load("Y", "RI_%d" % h, full, "ex", h, True, CFG["LD"][2 * h + 1])
+        dma("S", v("THI")["ap"], T["th"][:], writes=[v("THI")])
 
     def hc(name, h, lo=0, hi=None, st=1):
-        n = "%s_%d" % (name, h if GS or name not in ("XW", "RI", "RW", "THM") else 0)
+        n = "%s_%d" % (name, h if GS or name not in ("XW", "RI", "RW") else 0)
         return cols(n, lo, hi if hi else WHAT[n][1][1], st)
+
+    def cn(t, h, j):
+        x = 4 * t + 2 * h * GS + j
+        return cols("CN", x, x + 1)
 
     def lf(t, h, lo=0, hi=HM):
         return cols("LF%d" % t, LW * h + lo, LW * h + hi)
@@ -291,33 +305,34 @@ def rank_program(g, core, T, topo):
         cp(lf(0, h), v("LI", full, IN[h]))
         ts(hc("LC", h), v("LI", full, IN[h]), -CEN, OP.add)
     ts(v("Ib"), v("IC"), 0, OP.is_equal)
-    for n, x in (("NIb", -1.0), ("PI", GATE), ("NI", -GATE), ("HIb", 0.5), ("Ih", 1.0)):
+    for n, x in (("NIb", -1.0), ("NI", -GATE), ("HIb", 0.5), ("AI", APART)):
+        either(v(n), v("Ib"), 0.0, x)
+    for n, x in (("Ih", 1.0), ("NIh", -1.0)):
         ts(v(n), v("Ib"), x, OP.mult)
     ts(v("IA"), v("IA"), 15, OP.bitwise_and)
     ts(v("DELTA"), v("IA"), 0, OP.is_equal)
     ts(col(CP0), cols("IA", 0, 1), 0, OP.is_equal)
     ts(v("IB"), v("IB"), 4, OP.arith_shift_right)
     ts(v("BOb"), v("IB"), 0, OP.is_equal)
-    for n, x in (("BOh", 1.0), ("NBOh", -1.0), ("NBOb", -1.0), ("NBR", -RIV / 2)):
+    for n, x in (("BOh", 1.0), ("NBOh", -1.0)):
         ts(v(n), v("BOb"), x, OP.mult)
+    for n, x in (("NBOb", -1.0), ("BO2", 2.0)):
+        either(v(n), v("BOb"), 0.0, x)
     ts(v("SEL0"), v("BOb"), col(CP0), OP.mult)
-    ts(v("BLK"), cols("BOb", 0, 128, 16), 16.0, OP.mult)
-    ts(v("BLKC"), cols("BOb", 0, 128, 16), CONF, OP.mult)
-    if any(CFG["VSUB"].values()):
-        ts(cols("BLK2", 0, 8), cols("BOb", 0, 128, 16), 32.0, OP.mult)
-        ts(cols("BLK2", 8, 16), cols("BOb", 0, 128, 16), -16.0, OP.mult)
+    for o, x in ((v("BLK"), 16.0), (v("BLKC"), CONF), (cols("BLK2", 0, 8), 32.0), (cols("BLK2", 8, 16), -16.0)):
+        either(o, cols("BOb", 0, 128, 16), 0.0, x)
     fill(v("SELA"), 0.0)
     cp(cols("SELA", 15, 143, 16), cols("BOb", 0, 128, 16))
     fill(v("ONb"), 1.0)
     for h in range(2):
         acc((cols("U_0", HM * h, HM * h + HM), v("SEL0"), hc("LC", h)), new=True)
     act(v("L0B0"), cols("U_0", 0, M), AF.Copy, bias=CEN)
-    send([(v("L0B0"), v("L0B%d" % t), 2) for t in range(1, TV)], ["l0%d" % t for t in range(1, TV)],
-         [T.cores[(rank + STEP * t) % N] for t in range(1, TV)])
+    send([(v("L0B0"), v("L0B%d" % t), 4 if t == 1 else 2) for t in range(1, TV)], ["l0%d" % t for t in range(1, TV)],
+         [T.cores[(rank + STEP * t) % N] for t in range(1, TV)], 7000.0)
     for h in range(2):
         for k in range(16):
-            (gcopy if k < CFG["G0"][h] else either)(cols("L0R0", 2048 * h + k, 2048 * h + 2048, 16), cols("L0B0", HM * h, HM * h + HM))
-    gcopy(cols("L0R1", 0, 4096, 16), v("L0B0"))
+            anyone(cols("L0R0", 2048 * h + k, 2048 * h + 2048, 16), cols("L0B0", HM * h, HM * h + HM), "GSV")
+    anyone(cols("L0R1", 0, 4096, 16), v("L0B0"), "GSV")
     iota(v("GI"), [[-32768, 8], [0, 16]], 0, 0, True)
     iota(v("KI"), [[0, 8], [1, 16]], 65536, 0, True)
     fill(v("CK", slice(0, 64)), 0.0)
@@ -328,406 +343,325 @@ def rank_program(g, core, T, topo):
     fill(v("CK", one, slice(256, 384)), -0.25)
     fill(v("CK", one, slice(384, 385)), -31.5)
     ts(v("CK", row, slice(0, 128)), v("GI", row), 4.0, OP.mult)
+    ts(v("CK", row, slice(128, 256)), v("GI", row), -4.0, OP.mult)
     ts(v("GI"), v("GI"), 4.0, OP.mult)
     tt(v("CC1"), v("GI"), v("KI"), OP.add)
     ts(cols("CC1", 0, 128, 16), cols("CC1", 0, 128, 16), 65536.0, OP.add)
-    cp(v("CC2"), v("CC1"))
-    ts(cols("CC2", 1, 128, 16), cols("CC2", 1, 128, 16), 65536.0, OP.add)
     iota(v("IQ"), [[16, 16]], 15, 0, True)
     cp(v("BC"), v("IQ"))
     ts(v("BS"), v("IQ"), -15.0, OP.add, 1.0 / 16, OP.mult)
     for h in range(2):
-        fill(hc("LOSE", h, 0, 1), BIG)
-        fill(hc("LS", h, 0, 1), 0.0)
+        fill(hc("M2", h, 0, 1), BIG)
+        fill(hc("MG", h, 0, 1), 0.0)
         fill(hc("QE", h, 0, 1), 1.0)
     fill(v("EO", one), 0.0)
     fill(v("EO", one, slice(0, 128, 16)), 1.0)
     iota(v("CKE", one), [[0, 16], [1, 16]], 0, 0, True)
     fill(v("RMAX"), 1.0)
-    fill(cols("RMAX", 0, 128, 16), 0.0)
-    iota(v("LOW"), [[0, 512]], -int(BIG), 0, True)
-    select(v("RMIN"), cols("LOW", 0, 256), [[0, 16], [1, 16]], OP.not_equal, BIG, 0, 0)
-    select(v("R4"), v("LOW"), [[0, 128], [1, 4]], OP.not_equal, BIG, 0, 0)
-    fill(v("RP", one), 0.0)
-    fill(v("RP", one, slice(0, 512, 4)), GATE)
-    fill(v("RP", one, slice(1, 512, 4)), GATE)
+    fill(v("RMIN"), -BIG)
+    fill(cols("RMIN", 0, 256, 16), BIG)
+    for h in range(2):
+        if CFG["HORN"][h]:
+            fill(dict(hc("MK", h, 0, 512, 4), lane=0), 0.0)
+    if not all(CFG["HORN"]):
+        iota(v("LO4"), [[0, 512]], -int(BIG), 0, True)
+        select(v("R4"), v("LO4"), [[0, 128], [1, 4]], OP.not_equal, BIG, 0, 0)
+        fill(v("RP", one), 0.0)
+        fill(v("RP", one, slice(0, 512, 4)), GATE)
+        fill(v("RP", one, slice(1, 512, 4)), GATE)
+        ts(v("PI"), v("Ib"), GATE, OP.mult)
     iota(v("IP"), [[0, 1]], 0, 1)
     ts(v("IP"), v("IP"), 15, OP.bitwise_and)
-    ts(col(CDUM), v("IP"), float(W), OP.add)
-    if CFG["WT"] < 2:
-        ts(col(CRN), v("IP"), 65536.0, OP.add)
-    if CFG["WT"] >= 2:
-        ts(col(CDUM + 1), v("IP"), W + 16.0, OP.add)
-        cp(col(CRN), v("IP"))
-        iota(v("J2"), [[-16, 2], [0, 4], [1, 32]], 0, 0, True)
-        ts(v("TR2"), v("J2"), col(CRN), OP.is_gt, RIV, OP.mult)
-        ts(v("TR3"), v("J2"), col(CRN), OP.is_equal, -RIV if CFG["WT"] == 2 else -2.0, OP.mult)
-        iota(v("J3"), [[0, 256]], -1, 0, True)
-        select(v("NB2"), v("J3"), [[-16, 2], [-32, 4], [0, 32]], OP.is_ge, 0.0, 0, 1)
-        select(v("NB2"), v("NB2"), [[16, 2], [32, 4], [0, 32]], OP.is_ge, 0.0, 15, -1)
-        ts(col(CP1), v("IP"), 1, OP.is_equal)
-        if CFG["WT"] == 2:
-            ts(col(CDUM + 2), v("IP"), 1, OP.is_le)
-            ts(v("ROW1"), v("BOb"), col(CDUM + 2), OP.mult, -RIV / 2, OP.mult)
-        ts(v("O32"), v("ONb"), col(CP1), OP.mult, 0.5, OP.mult)
-        if CFG["WT"] == 2:
-            fill(v("R32"), 1.0)
-        else:
-            ts(v("R32"), v("TR3"), 1.0, OP.add)
-            fill(v("CK", one, slice(392, 520)), 2048.0)
-        fill(cols("R32", 0, 256, 32), 0.0)
-    else:
-        fill(v("O32"), 1.0 / 32)
-        ts(v("TRF"), v("KI"), col(CRN), OP.is_ge, -7 * RIV, OP.mult)
-        ts(v("TRI"), v("DELTA"), -RIV, OP.mult)
-        tt(v("TRI"), v("TRI"), v("TRF"), OP.add)
+    for r in range(2):
+        ts(col(CDUM + r), v("IP"), W + 16.0 * r, OP.add)
+        x = 4096.0 if GS else 1.0
+        ts(col(CWIN + r), v("IP"), 2.0 * x, OP.mult, (32.0 * r - 30.0 + CEN / 4096) * x, OP.add)
+    cp(col(CRN), v("IP"))
+    iota(v("J2"), [[-16, 2], [0, 4], [1, 32]], 0, 0, True)
+    ts(v("TR2"), v("J2"), col(CRN), OP.is_gt, RIV, OP.mult)
+    ts(v("R32"), v("J2"), col(CRN), OP.is_equal, -2.0, OP.mult)
+    ts(v("R32"), v("R32"), 1.0, OP.add)
+    fill(cols("R32", 0, 256, 32), 0.0)
+    iota(v("J3"), [[0, 256]], -1, 0, True)
+    select(v("NB2"), v("J3"), [[-16, 2], [-32, 4], [0, 32]], OP.is_ge, 0.0, 0, 1)
+    select(v("NB2"), v("NB2"), [[16, 2], [32, 4], [0, 32]], OP.is_ge, 0.0, 15, -1)
+    ts(col(CP1), v("IP"), 1, OP.is_equal)
+    ts(v("O32"), v("ONb"), col(CP1), OP.mult, 0.5, OP.mult)
     iota(v("ID"), [[-1, 132]], 512, 1)
     ts(v("ID"), v("ID"), 15, OP.bitwise_and)
     ts(v("SB"), v("ID"), 0, OP.is_equal)
     ts(v("NSB"), v("ID"), 0, OP.not_equal)
-    fill(cols("CN", 0, 1), TCEN - 0.5 + (2048.0 if CFG["WT"] == 3 else 0.0))
     iota(v("IG"), [[0, 2], [1, 4], [0, 16]] if GS else [[1, 8], [0, 16]], 0, -1)
-    ts(v("THF"), v("THI"), -1.0, OP.mult, TCEN, OP.add)
-    cp(v("THH"), v("THF"))
-    if CFG["WT"] < 2:
-        fill(v("ONh", slice(0, 8)), 1.0)
-        ts(v("TMK"), v("DELTA"), -60000.0, OP.mult, 30000.0, OP.add)
-    ts(col(CTM), col(CP0), 60000.0, OP.mult, -30000.0, OP.add)
+    ts(v("THH"), v("THI"), -TCEN, OP.add)
+    ts(col(CTM), col(CP0), -60000.0, OP.mult, 30000.0, OP.add)
     for h in range(1 + GS):
-        gb, tg = v("GB8_%d" % h), v("THG_%d" % h)
-        ts(gb, v("IG"), -4 * h, OP.is_equal)
-        if CFG["WT"] < 2:
-            ts(tg, gb, v("THF"), OP.mult)
-            acc((hc("U", 1, 0, 128), v("ONh", slice(0, 8)), tg), new=True)
-        acc((hc("U", 1, 128, 129), gb, v("THH")), new=True)
-        ts(hc("THM", h, 0, 128), v("ONb"), hc("U", 1, 128, 129), OP.mult, col(CTM), OP.max)
-        if CFG["WT"] == 3:
-            ts(hc("THM", h, 128, 256), v("ONb"), hc("U", 1, 128, 129), OP.mult)
-        if CFG["WT"] < 2:
-            tt(hc("THM", h, 128, 256), hc("U", 1, 0, 128), v("TMK"), OP.max)
-        for n, x in (("DUP", "Ih"), ("SD", "SEL0")):
-            for s in range(2 * GS):
-                cp(v(n + str(h), full, SIDE[s]), v(x, full, SIDE[h]))
-    if any(CFG["TL"]):
-        cp(cols("DEL2", 0, 128), v("DELTA"))
-        cp(cols("DEL2", 128, 256), v("DELTA"))
+        ts(v("GB8_%d" % h), v("IG"), -4 * h, OP.is_equal)
+        acc((hc("W", 1, h, h + 1), v("GB8_%d" % h), v("THH")), new=not h)
+    for h in range(1 + GS):
+        ts(col(CTH + 2 * h), hc("W", 1, h, h + 1), TCEN + 31.0, OP.add)
+        ts(col(CTH + 2 * h + 1), hc("W", 1, h, h + 1), TCEN + 31.0, OP.add, col(CTM), OP.min)
+    ts(cols("CN", 0, 2 + 2 * GS), cols("COLS", CTH, CTH + 2 + 2 * GS), -31.5, OP.add)
+    if GS:
+        iota(v("ONN"), [[0, 128]], -4096, 0, True)
+        for s in range(2):
+            select(hc("DUP", s), v("ONb"), [[0, 2], [-1, 64]], OP.is_equal, 0.0, -64 * s, 1)
+            select(hc("DUN", s), v("ONN"), [[0, 2], [-1, 64]], OP.is_equal, 0.0, -64 * s, 1)
+            select(hc("SD", s), v("ONb"), [[0, 2], [-16, 4], [0, 16]], OP.is_equal, 0.0, -64 * s, 1)
     for h in range(1 + GS):
         stage[0] = "rw%d" % h
         for q in range(4):
-            {"V": cp, "G": gcopy}[CFG["RWBY"][q]](hc("RW", h, 640 * q, 640 * q + 640), hc("RI", h, 640 * q, 640 * q + 640))
+            anyone(hc("RW", h, 640 * q, 640 * q + 640), hc("RI", h, 640 * q, 640 * q + 640), "GV")
 
     def table(t, h):
         return hc("RW", h, 0, W) if t else hc("RI", h)
 
+    def pieces(n):
+        return [(HM * q // n, HM * (q + 1) // n) for q in range(n)]
+
     def reps(t):
         for k in range(1, 16):
-            gcopy(cols("L0R%d" % (t % 2), k, 4096, 16), v("L0B%d" % t))
+            anyone(cols("L0R%d" % (t % 2), k, 4096, 16), v("L0B%d" % t), CFG["ZBY"][2])
 
     def gather(h, off, G):
-        for q in range(CFG["XP"]):
-            a, b = HM * q // CFG["XP"], HM * (q + 1) // CFG["XP"]
+        for a, b in pieces(CFG["XP"]):
             either(hc(G, h, 16 * a, 16 * b), ind(hc("XW", h), off(a, b)))
 
-    def sizes(t, h, G, D, k0, out, blk):
-        for c in range(4):
-            bank = ("D0", "D1", "U_%d" % h if CFG["OWN"] & 1 else "D0", "D0" if CFG["OWN"] & 1 else "D1")[c]
-            ks = [k for k in range(4 * c, 4 * c + 4) if k >= k0]
-            for k in ks:
-                o = cols(bank, 128 * (k % 4), 128 * (k % 4) + 128)
-                acc((o, v("Ib"), hc(G, h, k, 2048, 16)), (o, v("NIb"), zb(t, h)), new=True)
-            lo, hi = ks[0], ks[-1] + 1
-            act(hc(D, h, 128 * lo, 128 * hi), cols(bank, 128 * (lo % 4), 128 * (hi - 4 * c)), AF.Abs)
-            for j in range(len(out(0))):
-                acc(*[(out(k)[j], hc(D, h, 128 * k, 128 * k + 128), blk) for k in ks])
+    def banks(h, which):
+        return [{"o": "D%d" % h, "x": "D%d" % (1 - h), "0": "D0", "1": "D1"}.get(c, "%s_%d" % (c, h)) for c in which]
+
+    def sizes(h, which, four):
+        for c, bank in enumerate(banks(h, which)):
+            if four:
+                acc(*[(cols(bank, r, 512, 4), v("NIb"), hc("Z4", h, 128 * c, 128 * c + 128)) for r in range(4)], new=True)
+            else:
+                acc((v(bank), v("NIb"), hc("ZR", h, 512 * c, 512 * c + 512)), new=True)
+            acc((v(bank), v("Ib"), hc("GA", h, 512 * c, 512 * c + 512)))
+            act(hc("DA", h, 512 * c, 512 * c + 512), v(bank), AF.Abs)
 
     def phase1x(t, h):
         if t:
             ts(hc("LC", h), lf(t, h), -CEN, OP.add)
-        acc((hc("W", h, 256, 384), v("ONb", one), v("CK", one, slice(128, 256))), new=True)
-        if h in CFG["XSUB"] and t:
-            for q in range(CFG["VP"]):
-                a, b = HM * q // CFG["VP"], HM * (q + 1) // CFG["VP"]
-                x, y = hc("GA", h, 16 * a, 16 * b), hc("DA", h, 16 * a, 16 * b)
-                tt(x, ind(hc("XW", h), lf(t, h, a, b)), hc("ZR", h, 16 * a, 16 * b), OP.subtract)
-                act(y, x, AF.Abs)
+        acc((hc("W", h, 256, 384), v("ONb", two), v("CK", two, slice(128, 256))), new=True)
+        gather(h, lambda a, b: lf(t, h, a, b), "GA")
+        if CFG["P1"][h]:
+            sizes(h, CFG["B1"], True)
             for o, at in (("K", 0), ("W", 256)):
                 acc(*[(hc(o, h, at + k, at + 128, 16), hc("DA", h, k, 2048, 16), v("BLK")) for k in range(1, 16)])
             return
-        gather(h, lambda a, b: lf(t, h, a, b), "GA")
-        sizes(t, h, "GA", "DA", 1, lambda k: [hc("K", h, k, 128, 16), hc("W", h, 256 + k, 384, 16)], v("BLK"))
+        for c in range(4):
+            bank = banks(h, CFG["B1"])[c]
+            ks = [k for k in range(4 * c, 4 * c + 4) if k]
+            for k in ks:
+                o = cols(bank, 128 * (k % 4), 128 * (k % 4) + 128)
+                acc((o, v("Ib"), hc("GA", h, k, 2048, 16)), (o, v("NIb"), zb(t, h)), new=True)
+            lo, hi = ks[0], ks[-1] + 1
+            act(hc("DA", h, 128 * lo, 128 * hi), cols(bank, 128 * (lo % 4), 128 * (hi - 4 * c)), AF.Abs)
+            for o, at in (("K", 0), ("W", 256)):
+                acc(*[(hc(o, h, at + k, at + 128, 16), hc("DA", h, 128 * k, 128 * k + 128), v("BLK")) for k in ks])
 
     def phase1r(t, h):
-        for q in range(CFG["RP"]):
-            a, b = HM * q // CFG["RP"], HM * (q + 1) // CFG["RP"]
+        for a, b in pieces(CFG["RP"]):
             tt(hc("CF", h, 16 * a, 16 * b), ind(table(t, h), lf(t, h, a, b)),
                cols("L0R%d" % (t % 2), 2048 * h + 16 * a, 2048 * h + 16 * b), OP.is_equal)
         acc(*[(hc("K", h, k, 128, 16), hc("CF", h, k, 2048, 16), v("BLKC")) for k in range(1, 16)])
 
-    def last(h, name):
-        return ind(hc(name, h), cols("BC", 0, 8))
+    def last(h, name, n=8):
+        return ind(hc(name, h), cols("BC", 0, n))
 
-    def step(h, Q, l, Mn, n, bc):
-        either(hc("ML", h), hc(Mn, h, 15, n, 16))
-        tt(hc(Q, h, 1 + 128 * l, 1 + 128 * l + n), ind(hc("ML", h), cols(bc, 0, n // 16)), hc(Mn, h, 0, n), OP.is_equal)
-
-    def qq(h, Q, l):
-        return hc(Q, h, 1 + 128 * l, 129 + 128 * l), hc(Q, h, 128 * l, 128 + 128 * l)
-
-    def turn(h, Q, l):
-        o, (q, s) = hc("U", h, 128 * l, 128 * l + 128), qq(h, Q, l)
-        acc((o, v("EO", one), v("ONb", one)), (o, q, v("Ib")), (o, s, v("NIb")), new=True)
-        return o
-
-    def lists(o, src, a0, a1, new=False):
-        acc(*[(o, cols("SELA", 15 - a, 143 - a), cols(src, a0 + a, a1, 16)) for a in range(16)], new=new)
-
-    def tlists(h, bank, src, mid):
-        for l in range(2):
-            acc((hc(bank, h, 128 * l, 128 * l + 128), hc(src, h, 128 * l, 128 * l + 128), v("BOh")), new=True)
-        tt(hc(mid, h), hc(bank, h, 0, 256), v("DEL2"), OP.mult)
-        for l in range(2):
-            acc((hc(bank, h, 256 + 8 * l, 264 + 8 * l), hc(mid, h, 128 * l, 128 * l + 128), cols("BOh", 0, 128, 16)), new=True)
+    def lists(o, src):
+        acc(*[(o, cols("SELA", 15 - a, 143 - a), cols(src, a, 256, 16)) for a in range(16)], new=True)
 
     def near(t, h):
         key = hc("K", h, 0, 128)
         scan(hc("M1", h), v("CC1"), key, OP.min, OP.min, BIG)
-        tt(hc("LOSE", h, 1, 128), hc("K", h, 1, 128), hc("M1", h, 0, 127), OP.max)
         tt(hc("KEY", h), key, v("CC1"), OP.min)
-        scan(hc("M2", h), v("CC2"), hc("LOSE", h), OP.min, OP.min, BIG)
+        scan(hc("M2", h, 1, 128), hc("KEY", h, 1, 128), hc("M1", h, 0, 127), OP.min, OP.max, BIG)
         for l in range(2):
-            o, u = hc("OAB", h, 128 * l, 128 * l + 128), hc("U", h, 128 * l, 128 * l + 128)
+            o = hc("OAB", h, 128 * l, 128 * l + 128)
             tt(o, last(h, "M%d" % (l + 1)), hc("KEY", h), OP.is_equal)
-            acc((u, o, v("Ib")), new=True)
-            tt(hc("OL", h, 128 * l, 128 * l + 128), u, hc("LC", h), OP.mult)
-        if CFG["TL"][0]:
-            tlists(h, "K", "OL", "LTD")
-        else:
-            lists(hc("K", h, 256, 272), "OL_%d" % h, 0, 256, True)
+            acc((hc("U", h, 128 * l, 128 * l + 128), o, v("Ib")), new=not l)
+        for l in range(2):
+            tt(hc("OL", h, 128 * l, 128 * l + 128), hc("U", h, 128 * l, 128 * l + 128), hc("LC", h), OP.mult)
+        lists(hc("K", h, 256, 272), "OL_%d" % h)
         ts(hc("LOF", h), hc("K", h, 256, 272), CEN, OP.add)
-        cp(hc("EU", h), ind(table(t, h), hc("LOF", h)))
+        for a, b in ((0, 8), (8, 16)) if CFG["EU2"] else ((0, 16),):
+            cp(hc("EU", h, 16 * a, 16 * b), ind(table(t, h), hc("LOF", h, a, b)))
         ts(hc("EC", h), hc("EU", h), -CEN, OP.add)
-        if not CFG["WT"]:
-            ts(hc("LAC", h), hc("LOF", h, 0, 8), -CEN, OP.add)
 
     def far(t, h):
         key = hc("W", h, 256, 384)
         acc(*[(key, v("NI"), hc("OAB", h, 128 * l, 128 * l + 128)) for l in range(2)])
-        scan(hc("MF", h), v("RMAX"), key, OP.mult, OP.max)
-        tt(hc("LS", h, 1, 128), hc("W", h, 257, 384), hc("MF", h, 0, 127), OP.min)
         either(hc("KF", h), key)
+        scan(hc("MF", h), v("RMAX"), hc("KF", h), OP.mult, OP.max)
         tt(hc("FF", h, 0, 128), last(h, "MF"), hc("KF", h), OP.is_equal)
-        scan(hc("MG", h), v("RMAX"), hc("LS", h), OP.mult, OP.max)
+        scan(hc("MG", h, 1, 128), hc("KF", h, 1, 128), hc("MF", h, 0, 127), OP.max, OP.min, -BIG)
         tt(hc("FF", h, 128, 256), last(h, "MG"), hc("KF", h), OP.is_equal)
 
     def rivals(t, h):
-        ola, o, d = hc("OL", h, 0, 128), hc("U", h, 256, 384), hc("K", h, 272, 400)
-        if not CFG["TL"][0]:
-            acc((o, ola, v("BOh")), new=True)
-            tt(hc("LTD", h, 0, 128), o, v("DELTA"), OP.mult)
-        if CFG["WT"] == 3:
-            for r in range(2):
-                ts(hc("LAF", h, 4 * r, 4 * r + 4), hc("LOF", h, r, 8, 2), 1.0 / 4096, OP.mult, 1.0, OP.add)
-            d = hc("K", h, 0, 256)
-            acc((d, v("Ib"), v("TR2")), (d, hc("LTD", h, 0, 128), v("NB2")),
-                *[(hc("K", h, 128 * r, 128 * r + 128), v("BOh"), ola) for r in range(2)], new=True)
-            if t and not h:
-                ts(cols("CN", t, t + 1), cols("ZB%d" % t, LW + HM, LW + HM + 1), TCEN + 31.0 + 2048.0, OP.add)
-            ts(hc("LIM", h), d, 0.0, OP.is_equal, cols("CN", t, t + 1), OP.mult)
-        elif CFG["WT"] == 2:
-            for r in range(2):
-                cp(hc("LAF", h, 4 * r, 4 * r + 4), hc("LOF", h, r, 8, 2))
-            d = hc("K", h, 0, 256)
-            acc((d, v("Ib"), v("TR2")), (d, v("Ib"), v("TR3")), (d, hc("LTD", h, 0, 128), v("NB2")),
-                *[(hc("K", h, 128 * r, 128 * r + 128), v("BOh"), ola) for r in range(2)], new=True)
-        else:
-            acc((d, v("Ib"), v("TRI")), (d, v("NBOh"), ola), (d, hc("LTD", h, 0, 128), v("BOh")), new=True)
-        if not GS:
-            acc((o, v("Ih"), hc("EC", h, 0, 128)), (o, v("NI"), cols("SB", t, t + 128)), new=True)
-            o = hc("U", h, 384, 512)
-            acc((o, v("SEL0"), hc("LC", h)), (o, v("NI"), cols("NSB", t, t + 128)), new=True)
-            either(hc("NW", h, 0, 256), hc("U", h, 256, 512), CEN)
+        ola, o, d = hc("OL", h, 0, 128), hc("U", h, 256, 384), hc("K", h, 0, 256)
+        for r in range(2 - 2 * GS):
+            either(hc("LAF", h, 4 * r, 4 * r + 4), hc("K", h, 256 + r, 264, 2), col(CWIN + r), 1.0 / 4096)
+        if GS:
+            ts(hc("LAH", h), hc("LOF", h, 0, 8), -CEN, OP.add)
+        acc((o, ola, v("BOh")), new=True)
+        tt(hc("LTD", h), o, v("DELTA"), OP.mult)
+        acc((d, v("Ib"), v("TR2")), (d, hc("LTD", h), v("NB2")),
+            *[(hc("K", h, 128 * r, 128 * r + 128), v("BOh"), ola) for r in range(2)], new=True)
+        act(hc("AD", h), d, AF.Abs)
+        acc((hc("K", h, 256, 512), v("AI"), hc("AD", h)), new=True)
+        if t and (GS or not h):
+            for j in range(2):
+                either(cn(t, h, j), cols("CNi", 4 * t, 4 * t + 1), col(CTH + 2 * h + j))
+        if GS:
+            mm = []
+            for s in range(2):
+                for at, x, y, z in ((0, "DUP", hc("EC", h, 0, 128), "SB"), (256, "SD", hc("LC", h), "NSB")):
+                    o = hc("U", h, at + 128 * s, at + 128 * s + 128)
+                    mm += [(o, hc(x, s), y), (o, v("NI"), cols(z, t, t + 128))]
+            acc(*mm, new=True)
+            either(hc("NW", h), hc("U", h), CEN)
             return
-        for s in range(2):
-            o = hc("U", h, 128 * s, 128 * s + 128)
-            acc((o, v("DUP%d" % s), hc("EC", h, 0, 128)), (o, v("NI"), cols("SB", t, t + 128)), new=True)
-            o = hc("U", h, 256 + 128 * s, 384 + 128 * s)
-            acc((o, v("SD%d" % s), hc("LC", h)), (o, v("NI"), cols("NSB", t, t + 128)), new=True)
-        either(hc("NW", h), hc("U", h), CEN)
+        acc((o, v("Ih"), hc("EC", h, 0, 128)), (o, v("NI"), cols("SB", t, t + 128)), new=True)
+        o = hc("U", h, 384, 512)
+        acc((o, v("SEL0"), hc("LC", h)), (o, v("NI"), cols("NSB", t, t + 128)))
+        either(hc("NW", h, 0, 256), hc("U", h, 256, 512), CEN)
 
     def phase2g(t, h):
-        for l, G in enumerate(("GA", "GB")):
-            if (h, l) not in CFG["VSUB"]:
-                gather(h, lambda a, b: hc("EU", h, 128 * l + a, 128 * l + b), G)
+        gather(h, lambda a, b: hc("EU", h, a, b), "GA")
 
     def spread(t, h):
-        if not any(x[0] == h for x in CFG["VSUB"]):
-            return
-        how = {"G": gcopy, "V": cp, "E": either}
-        by = CFG["ZBY"][h]
-        for k, e in enumerate(by[:4]):
-            how[e](dict(hc("Z4", h, k, 512, 4), lane=k), zb(t, h))
-        for k, e in enumerate(by[4:]):
-            how[e](dict(hc("ZR", h, k, 2048, 4), lane=k), hc("Z4", h))
+        for k in range(4):
+            anyone(dict(hc("Z4", h, k, 512, 4), lane=k), zb(t, h), CFG["ZBY"][0])
+        for k in range(4):
+            anyone(dict(hc("ZR", h, k, 2048, 4), lane=k), hc("Z4", h), CFG["ZBY"][1])
 
     def phase2(t, h):
         acc((hc("W", h, 0, 256), v("ONb", one), v("CKE", one)), new=True)
-        for l, (G, D) in enumerate((("GA", "DA"), ("GB", "DB"))):
-            out = lambda k: hc("W", h, 128 * l + k, 128 * l + 128, 16)
-            if (h, l) not in CFG["VSUB"]:
-                if not CFG["WIDE"]:
-                    sizes(t, h, G, D, 0, lambda k: [out(k)], v("BLK"))
-                    continue
-                for c in range(4):
-                    o = v(("D0", "D1", "U_%d" % h if CFG["OWN"] & 2 else "D0", "D0" if CFG["OWN"] & 2 else "D1")[c])
-                    acc((o, v("NIb"), hc("ZR", h, 512 * c, 512 * c + 512)), new=True)
-                    acc((o, v("Ib"), hc(G, h, 512 * c, 512 * c + 512)))
-                    act(hc(D, h, 512 * c, 512 * c + 512), o, AF.Abs)
-                acc(*[(out(k), hc(D, h, k, 2048, 16), v("BLK")) for k in range(16)])
-                continue
-            relu = CFG["VSUB"][(h, l)]
-            for q in range(CFG["VP"]):
-                a, b = HM * q // CFG["VP"], HM * (q + 1) // CFG["VP"]
-                x, y = hc(G, h, 16 * a, 16 * b), hc(D, h, 16 * a, 16 * b)
-                tt(x, ind(hc("XW", h), hc("EU", h, 128 * l + a, 128 * l + b)), hc("ZR", h, 16 * a, 16 * b), OP.subtract)
-                if relu:
-                    op("VS", cyc(x["n"], True), [x], [y], [lambda x=x, y=y: S.activation(y["ap"], x["ap"], AF.Relu)],
-                       costs={"V": cyc(x["n"], True), "S": x["n"] * CYC + CFG["SO"]}, alt=[tsf(y, x, 0.0, OP.max)])
-                else:
-                    act(y, x, AF.Abs)
-            if relu:
-                acc(*[(out(k), hc(G, h, k, 2048, 16), cols("BLK2", 8, 16)) for k in range(16)])
-            acc(*[(out(k), hc(D, h, k, 2048, 16), cols("BLK2" if relu else "BLK", 0, 8)) for k in range(16)])
+        sizes(h, CFG["B2"], False)
+        acc(*[(hc("W", h, k, 128, 16), hc("DA", h, k, 2048, 16), v("BLK")) for k in range(16)])
+        for a, b in pieces(CFG["VP"]):
+            x = hc("GB", h, 16 * a, 16 * b)
+            tt(x, ind(hc("XW", h), hc("EU", h, 128 + a, 128 + b)), hc("ZR", h, 16 * a, 16 * b), OP.subtract)
+            either(hc("DB", h, 16 * a, 16 * b), x, relu=True)
+        for G, at in (("GB", 8), ("DB", 0)):
+            acc(*[(hc("W", h, 128 + k, 256, 16), hc(G, h, k, 2048, 16), cols("BLK2", at, at + 8)) for k in range(16)])
 
     def pick(t, h):
+        u = [hc("U", h, 128 * l, 128 * l + 128) for l in range(2)]
+        acc(*[(o, v("EO", one), v("ONb", one)) for o in u], new=True)
         scan(hc("ME", h), v("RMIN"), hc("W", h, 0, 256), OP.max, OP.min)
-        if CFG["KE"][h]:
-            (cp if CFG["KE"][h] == 2 else either)(hc("KE", h), hc("W", h, 0, 256))
-            tt(hc("QE", h, 0, 256), ind(hc("ME", h), v("BC")), hc("KE", h), OP.is_equal)
-            for l in range(2):
-                acc((hc("U", h, 128 * l, 128 * l + 128), hc("QE", h, 128 * l, 128 * l + 128), v("Ib")), new=True)
-        else:
-            step(h, "QE", 0, "ME", 256, "BS")
-            for l in range(2):
-                turn(h, "QE", l)
+        cp(hc("ML", h), hc("ME", h, 15, 256, 16))
+        tt(hc("QE", h, 1, 257), ind(hc("ML", h), v("BS")), hc("ME", h), OP.is_equal)
+        for l, o in enumerate(u):
+            acc((o, hc("QE", h, 128 * l + 1, 128 * l + 129), v("Ib")), (o, hc("QE", h, 128 * l, 128 * l + 128), v("NIb")))
         tt(hc("OEE", h), hc("U", h, 0, 256), hc("EC", h), OP.mult)
-        if CFG["TL"][1]:
-            tlists(h, "U", "OEE", "ETD")
-        else:
-            lists(hc("U", h, 256, 272), "OEE_%d" % h, 0, 256, True)
+        lists(hc("U", h, 256, 272), "OEE_%d" % h)
         ts(hc("LEF", h), hc("U", h, 256, 272), CEN, OP.add)
-        xa, xb = hc("XE", h, 0, 128), hc("XE", h, 128, 256)
-        nat, tr = hc("W", h, 128, 256), hc("W", h, 256, 384)
-        if CFG["XD"][h]:
-            cp(xb, ind(hc("XW", h), hc("LEF", h, 8, 16)))
-            tt(xa, ind(hc("XW", h), hc("LEF", h, 0, 8)), xb, OP.subtract)
-            ts(hc("AE", h), xa, 0.0, OP.max, 2.0, OP.mult)
-            if CFG["WT"] == 3:
-                both = ((hc("K", h, 256, 384), 128), (nat, 0))
-                for o, at in both:
-                    acc((o, v("Ih"), hc("THM", h, at, at + 128)), (o, v("ONb", one), v("CK", one, slice(392, 520))), new=True)
-                for x, y in (("NBOb", xa), ("BOb", hc("AE", h))):
-                    for o, at in both:
-                        acc((o, v(x), y))
-            elif CFG["WT"] == 2:
-                acc((nat, v("Ih"), hc("THM", h, 0, 128)), new=True)
-                acc((nat, v("NBOb"), xa))
-                acc((nat, v("BOb"), hc("AE", h)))
-            else:
-                acc((hc("W", h, 128, 384), v("Ih"), hc("THM", h)), new=True)
-                acc((nat, v("NBOb"), xa), (tr, xa, v("NBOb")))
-                acc((nat, v("BOb"), hc("AE", h)), (tr, hc("AE", h), v("BOb")))
+        xa, xb, ae = hc("XE", h, 0, 128), hc("XE", h, 128, 256), hc("AE", h)
+        nat, o = hc("W", h, 128, 256), cols(banks(h, CFG["BZ"])[0], 384, 512)
+        riv = [hc("K", h, 256, 384), hc("K", h, 384, 512)]
+        cp(xb, ind(hc("XW", h), hc("LEF", h, 8, 16)))
+        if CFG["XD"][h] == 2:
+            either(xa, ind(hc("XW", h), hc("LEF", h, 0, 8)))
+            tt(ae, ind(hc("XW", h), hc("LEF", h, 0, 8)), xb, OP.max)
+            acc((nat, v("NBOb"), xb), new=True)
+            acc(*[(x, v("NBOb"), xb) for x in riv])
+            acc(*[(x, v("NBOb"), xa) for x in riv + [nat]])
         else:
-            either(hc("XE", h), ind(hc("XW", h), hc("LEF", h)))
-            o = hc("W", h, 0, 128)
-            acc((o, v("Ib"), xa), (o, v("NIb"), xb), new=True)
-            act(hc("AE", h), o, AF.Abs)
-            if CFG["WT"] == 2:
-                acc((nat, v("Ih"), hc("THM", h, 0, 128)), (nat, v("BOb"), hc("AE", h)), new=True)
-            else:
-                acc((hc("W", h, 128, 384), v("Ih"), hc("THM", h)), (nat, v("BOb"), hc("AE", h)), (tr, hc("AE", h), v("BOb")), new=True)
-        if t and not h and CFG["WT"] < 3:
-            ts(cols("CN", t, t + 1), cols("ZB%d" % t, LW + HM, LW + HM + 1), TCEN + 31.0, OP.add)
-        wide = 128 if CFG["WT"] >= 2 else 256
-        act(hc("SG", h, 0, wide), hc("W", h, 128, 128 + wide), AF.Sign, scale=-1.0, bias=cols("CN", t, t + 1), accum_out=cols("AC", h, h + 1))
-        o = hc("W", h, 384, 512)
-        acc((o, v("ONb", one), v("CK", one, slice(256, 384))), (o, v("HIb"), xa), (o, v("Ib" if CFG["XD"][h] else "HIb"), xb), new=True)
-        zo = cols("ZBo%d" % t, LW * (1 - h), LW * (1 - h) + HM) if t < TV - 1 else v("ZY", full, IN[h])
-        ts(zo, o, MAGIC, OP.add, -MAGIC, OP.add)
+            tt(xa, ind(hc("XW", h), hc("LEF", h, 0, 8)), xb, OP.subtract)
+            ts(ae, xa, 0.0, OP.max)
+            acc((nat, v("NBOb"), xa), new=True)
+            acc(*[(x, v("NBOb"), xa) for x in riv])
+        acc((o, v("ONb", one), v("CK", one, slice(256, 384))), (o, v("HIb" if CFG["XD"][h] == 2 else "Ib"), xb), new=CFG["BZ"] != "W")
+        acc((o, v("HIb"), xa))
+        acc((nat, v("BO2"), ae))
+        acc(*[(x, v("BO2"), ae) for x in riv])
+        if CFG["HORN"][h]:
+            ts(dict(hc("MK", h, 3, 512, 4), lane=3), nat, cn(t, h, 1), OP.is_ge)
+        else:
+            act(hc("SG", h), nat, AF.Sign, scale=-1.0, bias=cn(t, h, 1), accum_out=cols("AC", h, h + 1))
+        act(hc("SN", h), hc("K", h, 256, 512), AF.Sign, scale=-1.0, bias=cn(t, h, 0))
+        zo = cols("ZBo%d" % t, LW * h, LW * h + HM) if t < TV - 1 else v("ZY", full, IN[h])
+        if CFG["ZS"][h]:
+            ts(zo, o, MAGIC, OP.add, -MAGIC, OP.add)
+        else:
+            act(hc("ZT", h), o, AF.Copy, bias=MAGIC)
+            act(zo, hc("ZT", h), AF.Copy, bias=-MAGIC)
+        if t < TV - 1 and CFG["HORN"][h]:
+            act(hc("SG", h), nat, AF.Sign, scale=-1.0, bias=cn(t, h, 1), accum_out=cols("AC", h, h + 1))
+
+    def marks(t, h):
+        if not CFG["HORN"][h]:
+            return
+        o = [cols(banks(h, CFG["BF"])[0], 128 * l, 128 * l + 128) for l in range(2)]
+        f = [hc("FF", h, 128 * l, 128 * l + 128) for l in range(2)]
+        acc((o[0], f[0], v("Ib")), (o[1], f[0], v("Ib")), (o[1], f[1], v("Ib")), new=True)
+        for l in range(2):
+            either(dict(hc("MK", h, 1 + l, 512, 4), lane=1 + l), o[l])
 
     def rows(t, h):
         c = [hc("U", h, j, 512, 4) for j in range(4)]
-        mm = [(hc("U", h), v("ONb", one), v("RP", one)), (c[2], v("Ih"), hc("LC", h)), (c[3], v("Ih"), hc("EC", h, 128, 256))]
-        for l in range(2):
-            q = hc("FF", h, 128 * l, 128 * l + 128)
-            mm += [(c[l], q, v("NI")), (c[2], q, v("PI")), (c[l], v("BOh"), hc("OEE", h, 128 * l, 128 * l + 128))]
-        acc(*mm, new=True)
-        acc(*[(c[j], v("NI" if j == 3 else "PI"), hc("SG", h, 0, 128)) for j in range(4)])
-        scan(hc("NL", h), v("R4"), hc("U", h), OP.max, OP.min)
-        lo = cols("LFo%d" % t, HM * (1 - h), HM * (2 - h)) if t < TV - 1 else v("LY", full, IN[h])
-        ts(lo, hc("NL", h, 3, 512, 4), GATE + CEN, OP.add)
+        if not CFG["HORN"][h]:
+            mm = [(hc("U", h), v("ONb", one), v("RP", one)), (c[2], v("Ih"), hc("LC", h)), (c[3], v("Ih"), hc("EC", h, 128, 256))]
+            for l in range(2):
+                q = hc("FF", h, 128 * l, 128 * l + 128)
+                mm += [(c[l], q, v("NI")), (c[2], q, v("PI")), (c[l], v("BOh"), hc("OEE", h, 128 * l, 128 * l + 128))]
+            acc(*mm, new=True)
+            acc(*[(c[j], v("NI" if j == 3 else "PI"), hc("SG", h)) for j in range(4)])
+            scan(hc("NL", h), v("R4"), hc("U", h), OP.max, OP.min)
+            lo = cols("LFo%d" % t, LW * h, LW * h + HM) if t < TV - 1 else v("LY", full, IN[h])
+            (ts if t < TV - 1 else lambda o, a, x, _: either(o, a, x))(lo, hc("NL", h, 3, 512, 4), GATE + CEN, OP.add)
+            return
+        ea, eb, lc, ec = hc("OEE", h, 0, 128), hc("OEE", h, 128, 256), hc("LC", h), hc("EC", h, 128, 256)
+        acc((c[0], v("BOh"), ea), (c[0], v("NBOh"), eb), (c[1], v("BOh"), eb), (c[1], v("NIh"), lc), (c[2], v("Ih"), lc),
+            (c[2], v("NIh"), ec), (c[3], v("Ih"), ec), new=True)
+        scan(hc("NL", h), hc("MK", h), hc("U", h), OP.mult, OP.add)
+        lo = cols("LFo%d" % t, LW * h, LW * h + HM) if t < TV - 1 else v("LY", full, IN[h])
+        (ts(lo, hc("NL", h, 3, 512, 4), CEN, OP.add) if t < TV - 1 else either(lo, hc("NL", h, 3, 512, 4), CEN))
 
     def leave(t, h):
-        wide = HM + h
+        ls = (cols("LFo%d" % t, LW * h, LW * h + HM), lf(t + 1, h))
+        zs = (cols("ZBo%d" % t, LW * h, LW * h + HM), cols("ZB%d" % (t + 1), LW * h, LW * h + HM))
+        if CFG["ZSEP"][h]:
+            send([zs + (8,)], ["z%d_%d" % (t + 1, h)])
+            send([ls + (8,)], ["l%d_%d" % (t + 1, h)])
+        else:
+            send([ls + (4,), zs + (4,)], ["l%d_%d" % (t + 1, h)])
         if h:
+            stage[0] = "count"
             p = cols("W_1", 0, 1)
             acc((p, v("ONb", one), v("CK", one, slice(384, 385))), *[(p, v("O32"), cols("AC", j, j + 1)) for j in range(2)], new=True)
             ts(col(CRN), p, 64 * MAGIC, OP.add, -64 * MAGIC, OP.add)
-            tt(cols("ZBo%d" % t, HM, HM + 1), p, col(CRN), OP.subtract)
-        send([(cols("LFo%d" % t, HM * (1 - h), HM * (1 - h) + wide), lf(t + 1, h, 0, wide), 4),
-              (cols("ZBo%d" % t, LW * (1 - h), LW * (1 - h) + wide), cols("ZB%d" % (t + 1), LW * h, LW * h + wide), 4)], ["l%d_%d" % (t + 1, h)])
+            tt(cols("CNo", 4 * t, 4 * t + 1), p, col(CRN), OP.subtract)
+            send([(cols("CNo", 4 * t, 4 * t + 1), cols("CNi", 4 * t + 4, 4 * t + 5), 8)], ["n%d" % (t + 1)])
 
     def winners(t, h):
-        if CFG["WT"] == 3:
-            for r in range(2):
-                tt(dict(hc("EQ", h, 128 * r, 128 * r + 128)), hc("K", h, 256, 384), hc("LIM", h, 128 * r, 128 * r + 128), OP.is_lt)
-            scan(hc("CNT", h), v("R32"), hc("EQ", h), OP.mult, OP.add)
-            tt(hc("SCF", h), hc("LAF", h), hc("CNT", h, 31, 256, 32), OP.subtract)
-            for r in range(2):
-                ts(dict(hc("SCU", h, r, 8, 2), lane=r), hc("SCF", h, 4 * r, 4 * r + 4), 4096.0, OP.mult, col(CDUM + r), OP.min)
-            return
-        if CFG["WT"] == 2:
-            acc(*[(hc("K", h, 128 * r, 128 * r + 128), v("ROW1"), hc("SG", h, 0, 128)) for r in range(2)])
-            ts(hc("EQ", h), hc("K", h, 0, 256), 0.0, OP.is_equal, RIV, OP.mult)
-            scan(hc("CNT", h), v("R32"), hc("EQ", h), OP.mult, OP.add)
-            tt(hc("SCF", h), hc("CNT", h, 31, 256, 32), hc("LAF", h), OP.add)
-            for r in range(2):
-                ts(dict(hc("SCU", h, r, 8, 2), lane=r), hc("SCF", h, 4 * r, 4 * r + 4), col(CDUM + r), OP.min)
-            return
-        d = hc("K", h, 272, 400)
-        acc((d, hc("SG", h, 128, 256), v("NBR")))
-        ts(hc("EQ", h), d, 0.0, OP.is_equal, RIV, OP.mult)
-        if not CFG["WT"]:
-            acc((hc("K", h, 128, 136), v("Ih"), hc("LAC", h)), new=True)
-            lists(hc("K", h, 128, 136), "EQ_%d" % h, 0, 128)
-            ts(hc("SCU", h, 0, 16, 2), hc("K", h, 128, 136), CEN, OP.add, col(CDUM), OP.min)
-            return
-        o = hc("K", h, 0, 128)
-        acc((o, hc("OL", h, 0, 128), v("BOh")), (o, hc("EQ", h), v("BOh")), new=True)
-        tt(hc("SCT", h), o, v("DELTA"), OP.mult)
         if GS:
-            for s in range(2):
-                for r in range(2):
-                    acc((v("K_%d" % h, SIDE[r], slice(128 + 8 * s, 136 + 8 * s)), hc("SCT", h, 64 * s, 64 * s + 64), cols("BOh", 0, 128, 16)), new=True)
-        else:
-            acc((hc("K", h, 128, 136), hc("SCT", h), cols("BOh", 0, 128, 16)), new=True)
-        n = 8 + 8 * GS
-        ts(hc("SCU", h, 0, 2 * n, 2), hc("K", h, 128, 128 + n), CEN, OP.add, col(CDUM), OP.min)
+            o = [(s, r, hc("K", h, 8 * r + 4 * s, 8 * r + 4 * s + 4)) for s in range(2) for r in range(2)]
+            acc(*[(x, hc("DUP", s), hc("LAH", h, r, 8, 2)) for s, r, x in o], new=True)
+            scan(hc("CNB", h), v("R32"), hc("SN", h), OP.mult, OP.add)
+            acc(*[(x, hc("DUN", s), hc("CNB", h, 128 * r + 31, 128 * r + 128, 32)) for s, r, x in o])
+            for r in range(2):
+                ts(dict(hc("SCU", h, r, 16, 2), lane=r), hc("K", h, 8 * r, 8 * r + 8), col(CWIN + r), OP.add, col(CDUM + r), OP.min)
+            return
+        scan(hc("CNT", h), v("R32"), hc("SN", h), OP.mult, OP.add)
+        tt(hc("SCF", h), hc("LAF", h), hc("CNT", h, 31, 256, 32), OP.subtract)
+        for r in range(2):
+            ts(dict(hc("SCU", h, r, 8, 2), lane=r), hc("SCF", h, 4 * r, 4 * r + 4), 4096.0, OP.mult, col(CDUM + r), OP.min)
 
     def write(t, h):
         n = 128 + 128 * GS
-        for q in range(3, -1, -1) if CFG["WT"] >= 2 else ():
+        for q in range(n // 32 - 1, -1, -1):
             tt(ind(hc("RW", h), hc("SCU", h, 2 * q, 2 * q + 2)), hc("NW", h, 32 * q, 32 * q + 32), hc("NW", h, n + 32 * q, n + 32 + 32 * q), OP.max)
-        for b in range(n // 16 - 1, -1, -1) if CFG["WT"] < 2 else ():
-            tt(ind(hc("RW", h), hc("SCU", h, 2 * b, 2 * b + 1)), hc("NW", h, 16 * b, 16 * b + 16), hc("NW", h, n + 16 * b, n + 16 + 16 * b), OP.max)
         if t == TV - 1 and h and not GS:
             dma("S", T["yl"][:], v("LY")["ap"], reads=[v("LY")])
             dma("S", T["yz"][:], v("ZY")["ap"], reads=[v("ZY")])
             dma("Y", T["yr"][:], hc("RW", h, 0, W)["ap"], reads=[hc("RW", h, 0, W)], cost=6000)
         if t == TV - 1 and GS:
             for s in range(2):
-                for n, x in (("yl", "LY"), ("yz", "ZY")):
-                    dma("Y", T[n][SIDE[h], IN[s]], v(x, SIDE[s], IN[h])["ap"], reads=[v(x, full, IN[h])])
-            dma("Y", T["yr"][SIDE[h], full], v("RW_%d" % h, SIDE[0], slice(0, W))["ap"], reads=[hc("RW", h, 0, W)], cost=4500)
+                for x, y in (("yl", "LY"), ("yz", "ZY")):
+                    dma("Y", T[x][SIDE[h], IN[s]], v(y, SIDE[s], IN[h])["ap"], reads=[v(y, full, IN[h])])
+            dma("Y", T["yr"][SIDE[h], full], v("RW_%d" % h, SIDE[0], slice(0, W))["ap"], reads=[hc("RW", h, 0, W)], cost=4000)
 
     def do(t, h, *parts):
         for name, part in parts:
@@ -746,7 +680,7 @@ def rank_program(g, core, T, topo):
         do(t, h, ("near", near), ("phase2g", phase2g), ("far", far), ("rivals", rivals))
 
     def third(t, h):
-        do(t, h, ("phase2", phase2), ("pick", pick), ("winners", winners), ("rows", rows))
+        do(t, h, ("phase2", phase2), ("marks", marks), ("pick", pick), ("winners", winners), ("rows", rows))
         if t + 1 < TV:
             do(t, h, ("leave", leave))
         do(t, h, ("write", write))
@@ -758,8 +692,17 @@ def rank_program(g, core, T, topo):
             part(t, h)
 
     if "order" not in ORDER:
+        for a, b in CFG["AFTER"]:
+            for t in range(TV):
+                x = max(o["i"] for o in ops if (o["stage"], o["t"]) == (a, t))
+                for o in ops[x:]:
+                    if (o["stage"], o["t"]) == (b, t):
+                        o["order"].add(x)
         ORDER.update(_plan(ops))
     order, who = ORDER["order"], ORDER["who"]
+    closes = dict.fromkeys(BANK, True)
+    for m in [m for i in order for m in ops[i].get("mms", ())][::-1]:
+        m[4], closes[m[0]["name"]] = closes[m[0]["name"]], m[3]
 
     que = {"V": V, "S": S, "P": P, "G": g, "Y": g.sync}
     count_, known, clock, place = {}, {}, {}, {}
@@ -767,8 +710,8 @@ def rank_program(g, core, T, topo):
     for pos, i in enumerate(order):
         o = ops[i]
         e = who[i]
-        if o["eng"] == "VS" and e == "V":
-            o["fns"] = o["alt"]
+        if "alt" in o:
+            o["fns"] = [o["alt"][e]]
         place[i] = pos
         if e == "R":
             clock[i] = (o["arr"][0], o["arr"][1], {})
@@ -829,7 +772,7 @@ def _lay(ops, nxt, need, key, who):
                 while q < len(a) and a[q] < at + c:
                     at = max(at, b[q])
                     q += 1
-            late = at + c + (CFG["HELP"] if "costs" in o and e == "V" else 0)
+            late = at + c + (CFG["HELP"] * "GSV".index(e) if "costs" in o else 0)
             if best is None or late < best[0]:
                 best = (late, e, at, c, q)
         _, e, at, c, q = best
@@ -852,27 +795,39 @@ def _relay(prv, turn, key, who, cost, lat):
         for j, _, _ in prv[i]:
             if key[j] >= key[i]:
                 key[i] = key[j] + 0.001
-    slots = {e: ([], []) for e in "VSPGYR"}
+    slots, by = {e: ([], [], []) for e in "VSPGYR"}, [None] * len(key)
     for i in sorted(turn, key=lambda i: key[i]):
-        e, at = who[i], 0.0
+        e, at, w = who[i], 0.0, None
         c = cost[i][e]
         for j, lag, near in prv[i]:
             x = fin[j] + (near if who[j] == e else lag)
             if x > at:
-                at = x
+                at, w = x, j
         if e != "R":
-            a, b = slots[e]
+            a, b, ids = slots[e]
             q = m = len(b)
             while q and b[q - 1] > at:
                 q -= 1
             while q < m and a[q] < at + c:
                 if b[q] > at:
-                    at = b[q]
+                    at, w = b[q], ~ids[q]
                 q += 1
             a.insert(q, at)
             b.insert(q, at + c)
-        start[i], fin[i] = at, at + c
-    return max(x + y for x, y in zip(fin, lat)), start, fin, who
+            ids.insert(q, i)
+        start[i], fin[i], by[i] = at, at + c, w
+    return max(x + y for x, y in zip(fin, lat)), start, fin, who, by
+
+
+def _held(r, lat):
+    i, out = max(range(len(lat)), key=lambda j: r[2][j] + lat[j]), []
+    while r[4][i] is not None:
+        j = r[4][i]
+        if j < 0:
+            j = ~j
+            out.append((i, j))
+        i = j
+    return out
 
 
 def _plan(ops):
@@ -880,7 +835,7 @@ def _plan(ops):
     fw, bw = [[] for _ in range(n)], [[] for _ in range(n)]
     for j, o in enumerate(ops):
         for i in sorted(o["deps"] | o["order"]):
-            lag = [ops[i].get("lat", 0) + o.get("pre", 0) + (CFG[x] if i in o["deps"] else 0.0) for x in ("HOP", "SELF")]
+            lag = [o.get("pre", 0) + (ops[i].get("lat", 0) + CFG[x] if i in o["deps"] else 0.0) for x in ("HOP", "SELF")]
             fw[i].append((j, *lag))
             bw[j].append((i, *lag))
     nf, nb = [len(x) for x in bw], [len(x) for x in fw]
@@ -913,15 +868,39 @@ def _plan(ops):
     both = [x for x in like.values() if all("costs" in ops[i] for i in x)]
     cur, up, lat = best, list(range(n)), [o.get("lat", 0) for o in ops]
     cost = [o.get("costs") or {o["eng"]: o["cost"]} for o in ops]
+    kin = {i: x for x in like.values() for i in x}
+
+    def other(i, who):
+        x = ops[i]["eng"].replace(who[i], "")
+        return x[int(draw() * len(x))]
+    cur = best = _relay(bw, up, cur[1], cur[3], cost, lat)
+    held = _held(cur, lat)
     for it in range(CFG["FINE"]):
         key, who, u = list(cur[1]), cur[3], draw()
         if it % 50 == 49:
             key = [-x for x in _relay(fw, up[::-1], [-x - y for x, y in zip(cur[2], lat)], who, cost, lat)[2]]
-        elif u < 0.2:
+        elif u > 1 - CFG["CRIT"] and held:
+            i, j = held[int(draw() * len(held))]
+            how, same = draw(), draw() < CFG["SAME"]
+            far = (0, 0, 300, 1000)[int(draw() * 4)]
+            if how < 0.25 and ("costs" in ops[i] or "costs" in ops[j]):
+                x = i if "costs" in ops[i] and ("costs" not in ops[j] or draw() < 0.5) else j
+                who, e = list(who), other(x, who)
+                for y in (kin[x] if same else [x]):
+                    if e in ops[y].get("costs", ""):
+                        who[y] = e
+            elif how < 0.6:
+                for y in (kin[i] if same else [i]):
+                    key[y] -= cur[1][i] - cur[1][j] + 1 + far
+            else:
+                for y in (kin[j] if same else [j]):
+                    key[y] += cur[1][i] - cur[1][j] + 1 + far
+        elif u < 0.2 * (1 - CFG["CRIT"]):
             x = both[int(draw() * len(both))]
-            who, e = list(who), "V" if who[x[-1]] == "S" else "S"
+            who, e = list(who), other(x[-1], who)
             for i in (x if draw() < 0.7 else [x[int(draw() * len(x))]]):
-                who[i] = e
+                if e in ops[i]["costs"]:
+                    who[i] = e
         else:
             run = runs[parts[int(draw() * len(parts))]]
             a = int(draw() * len(run)) if draw() < 0.7 else 0
@@ -932,60 +911,9 @@ def _plan(ops):
                     if t is None or ops[i]["t"] == t:
                         key[i] += d
         r = _relay(bw, up, key, who, cost, lat)
-        if r[0] < cur[0] + CFG["TEMP"] * (1 - it / CFG["FINE"]) * draw() ** 2:
-            cur = r
+        if r[0] - cur[0] + CFG["MEAN"] * (sum(r[2]) - sum(cur[2])) / n < CFG["TEMP"] * (1 - it / CFG["FINE"]) * draw() ** 2:
+            cur, held = r, _held(r, lat)
             best = min(best, r, key=lambda x: x[0])
-    end, start, fin, who = best
+    end, start, fin, who, _ = best
     order = sorted(range(n), key=lambda i: (start[i], i))
     return {"order": order, "who": who, "plan": [(start[i], fin[i], who[i], i) for i in order], "ops": ops, "end": end}
-
-
-def _plan0(ops):
-    n, HOP = len(ops), CFG["HOP"]
-    succ, need, tail, ready = [[] for _ in range(n)], [0] * n, [0.0] * n, [0.0] * n
-    for o in ops:
-        pre = o["deps"] | o["order"]
-        need[o["i"]] = len(pre)
-        for d in pre:
-            succ[d].append(o["i"])
-    for i in range(n - 1, -1, -1):
-        o = ops[i]
-        tail[i] = o["cost"] + o.get("lat", 0) + o.get("pre", 0) + HOP + max([tail[j] for j in succ[i]] + [0.0])
-    pri = [tail[o["i"]] + CFG["EARLY"].get(o["stage"], 0) for o in ops]
-    avail = {e: [] for o in ops for e in o["eng"]}
-    free = {e: 0.0 for e in avail}
-
-    def put(i):
-        for e in ops[i]["eng"]:
-            avail[e].append(i)
-    for o in ops:
-        if not need[o["i"]]:
-            put(o["i"])
-    order, plan, who = [], [], {}
-    while len(order) < n:
-        best = None
-        for e, lst in avail.items():
-            if e == "V":
-                lst = [j for j in lst if "costs" not in ops[j] or free["S"] > max(ready[j], free["V"]) + CFG["HELP"]]
-            if lst:
-                first = min(ready[j] for j in lst)
-                est = first if e == "R" else max(free[e], first)
-                if best is None or est < best[0]:
-                    best = (est, e, lst)
-        est, e, lst = best
-        i = max((j for j in lst if ready[j] <= est), key=lambda j: (pri[j], -j))
-        order.append(i)
-        o = ops[i]
-        for x in o["eng"]:
-            avail[x].remove(i)
-        who[i] = e
-        fin = est + (o["costs"][e] if "costs" in o else o["cost"]) + o.get("pre", 0)
-        if e != "R":
-            free[e] = fin
-        plan.append((est, fin, e, i))
-        for j in succ[i]:
-            ready[j] = max(ready[j], fin + o.get("lat", 0) + (HOP if i in ops[j]["deps"] or e == "R" else 0.0))
-            need[j] -= 1
-            if not need[j]:
-                put(j)
-    return {"order": order, "plan": plan, "who": who, "ops": ops}

import numpy as np
from concourse.bass import DstId, RemoteDMATransfer
from concourse.mybir import dt, AluOpType, AxisListType, ActivationFunctionType

OP = AluOpType
AF = ActivationFunctionType
W, M, HM, TV, STEP = 2560, 256, 128, 4, 3
BIG, GATE, CONF = 4194304.0, 262144.0, 131072.0
CEN, TCEN = 1280.0, 2041.0
MAGIC = 12582912.0
RIV, APART = 3840.0, 8192.0
CFG = {"GC": 1.4, "SC": 3.8, "PE": 0.42, "PO": 2.0, "VO": 20.0, "SO": 40.0, "LD": (3600, 6200, 7600, 10400), "GS": 0, "MEAN": 0.0, "SAME": 0.5, "XD": (2, 2), "ZS": (0, 0), "P1": (1, 1),
       "B1": "oUoU", "B2": "oUoU", "BZ": "o", "BF": "o", "EU2": 1, "HORN": (1, 1), "AFTER": (("phase2g0", "near1"),), "ZSEP": (0, 0), "G0": (2, 2), "SELF": 150.0, "MM": 8, "RFIRST": (0, 1), "HOP": 260.0, "HELP": 1500.0, "XP": 4, "RP": 4,
       "SEND": 600.0, "LAT": 1800.0, "PASS": 20, "FINE": 7000, "TEMP": 500.0, "CRIT": 0.6, "SEED": 3, "AMP": 4800.0, "VP": 4,
       "ZBY": ("GSV", "GSV", "GSV")}
CYC = 0.83
LW = 136

SCRATCH, BANK, ORDER = {}, {}, {}
WHAT, AT = {}, {}


def _buf(name, shape, dtype, where="sbuf"):
    WHAT[name] = (where, shape, dtype)
    if where == "psum" or shape[1] > 2048:
        SCRATCH[name] = WHAT[name]
        return
    host = "all_" + dtype
    at = SCRATCH[host][1][1] if host in SCRATCH else 0
    AT[name] = (host, at)
    SCRATCH[host] = ("sbuf", [128, at + -(-shape[1] // 64) * 64], dtype)


def _declare():
    B, F, H, I, U = "bfloat16", "float32", "float16", "int32", "uint16"
    sq, dq, wide = [128, 128], [128, 256], [128, 2048]
    for h in range(2):
        for n, s, d in (("XW", [128, W], B), ("RI", [128, W], I), ("RW", [128, W + 32], F)):
            _buf("%s_%d" % (n, h), s, d)
        for n, s, d in (("DUP", sq, H), ("SD", sq, H), ("DUN", sq, B), ("GB8", [8, 128], H), ("LAH", [128, 8], H), ("CNB", dq, B)):
            _buf("%s_%d" % (n, h), s, d)
    for n, s, d in (("LI", dq, I), ("ZI", dq, B),
                    ("L0R0", [128, 4096], F), ("L0R1", [128, 4096], F), ("LY", dq, F), ("ZY", dq, B)):
        _buf(n, s, d)
    for t in range(TV):
        for n, d in (("LF", U), ("ZB", B), ("LFo", U), ("ZBo", B)):
            _buf("%s%d" % (n, t), [128, 2 * LW], d)
        _buf("L0B%d" % t, dq, F)
    for h in range(2):
        for n, s, d in (("GA", wide, B), ("GB", wide, B), ("DA", wide, B), ("DB", wide, B), ("CF", wide, B), ("ZR", wide, B), ("Z4", [128, 512], B),
                        ("LC", sq, H), ("M1", sq, F), ("M2", sq, F), ("KEY", sq, F), ("OAB", dq, B), ("MF", sq, F), ("MG", sq, F), ("KF", sq, F),
                        ("FF", dq, B), ("ME", dq, F), ("QE", [128, 257], B), ("OL", dq, H), ("LOF", [128, 16], U), ("EU", dq, U), ("EC", dq, H),
                        ("LTD", sq, H), ("NW", [128, 512], F), ("OEE", dq, H), ("LEF", [128, 16], U), ("XE", dq, B), ("AE", sq, B), ("SG", sq, B),
                        ("NL", [128, 512], F), ("AD", dq, B), ("SN", dq, B), ("CNT", dq, F), ("SCF", [128, 8], F), ("LAF", [128, 8], F),
                        ("SCU", [128, 16], U), ("ZT", sq, F), ("MK", [128, 512], B)):
            _buf("%s_%d" % (n, h), s, d)
    for n, s, d in (("COLS", [128, 16], F), ("AC", [128, 2], F), ("IA", sq, I), ("IB", sq, I), ("IC", sq, I), ("ID", [128, 132], I),
                    ("IQ", [128, 16], F), ("IP", [128, 1], I), ("IG", [8, 128], I), ("GI", sq, F), ("KI", sq, F),
                    ("DELTA", sq, B), ("BOb", sq, B), ("BOh", sq, H), ("NBOb", sq, B), ("J2", dq, B), ("J3", dq, B),
                    ("LOW", dq, B), ("TR2", dq, B), ("NB2", dq, H), ("R32", dq, B), ("Ib", sq, B), ("NIb", sq, B), ("NBOh", sq, H), ("BO2", sq, B),
                    ("HIb", sq, B), ("Ih", sq, H), ("NIh", sq, H), ("NI", sq, B), ("AI", sq, B), ("ONb", sq, B),
                    ("LO4", [128, 512], B), ("R4", [128, 512], B), ("RP", [128, 512], B), ("PI", sq, B), ("CNo", [128, 16], F), ("CNi", [128, 16], F),
                    ("SB", [128, 132], B), ("NSB", [128, 132], B), ("SEL0", sq, H), ("SELA", [128, 144], H), ("BLK", [128, 8], B),
                    ("CN", [128, 16], F), ("BLK2", [128, 16], B), ("BLKC", [128, 8], B), ("CK", [128, 392], B), ("CKE", dq, B), ("EO", sq, B),
                    ("BC", [128, 16], U), ("BS", [128, 16], U), ("ML_0", [128, 16], F), ("ML_1", [128, 16], F), ("CC1", sq, F), ("RMIN", dq, B), ("RMAX", sq, B),
                    ("O32", sq, F), ("THI", [8, 1], I), ("THH", [8, 1], H), ("ONN", sq, B)):
        _buf(n, s, d)
    for k, n in enumerate(("D0", "D1", "K_0", "K_1", "U_0", "U_1", "W_0", "W_1")):
        _buf(n, [128, 512], F, "psum")
        BANK[n] = k


_declare()
SEMAPHORES = ["sV", "sS", "sP", "sG", "snt"] + ["ld%d" % i for i in range(28)]
for _t in range(1, TV):
    SEMAPHORES += ["l0%d" % _t, "n%d" % _t] + ["%s%d_%d" % (x, _t, h) for x in "lz" for h in range(2)]
CP0, CP1, CTM, CRN, CDUM, CWIN, CTH = 0, 1, 2, 3, 4, 6, 8


def rank_program(g, core, T, topo):
    rank = T.rank_of(core)
    if rank is None:
        return
    N = len(T.cores)
    V, S, P = g.vector, g.scalar, g.tensor
    ops, hist, ndma, stage, latest = [], {}, [0], ["start", 0], {}
    full = slice(None)
    GC = CFG["GC"]

    def v(name, *idx):
        where, shape, dtype = WHAT[name]
        sl = list(idx) + [full] * (len(shape) - len(idx))
        a, b, st = sl[1].indices(shape[1])
        n = (b - a + st - 1) // st
        p0, p1, _ = sl[0].indices(shape[0])
        host, at = AT.get(name, (name, 0))
        return {"ap": T[host][p0:p1, at + a:at + b:st], "name": name, "lo": a, "hi": a + (n - 1) * st + 1, "lane": a % 16 if st == 16 else None,
                "n": n, "psum": where == "psum", "two": dtype in ("bfloat16", "float16", "uint16")}

    def cols(name, lo, hi, st=1):
        return v(name, full, slice(lo, hi, st))

    def col(j):
        return cols("COLS", j, j + 1)

    def ind(win, off):
        return {"ap": win["ap"].indirect(off["ap"]), "parts": [win, off], "n": 16 * off["n"], "psum": False, "two": False, "ind": True}

    def flat(aps):
        out = []
        for a in aps:
            if isinstance(a, dict):
                out += a["parts"] if "parts" in a else [a]
        return out

    def hit(a, b):
        return a[5] == b[5] and a[2] < b[3] and b[2] < a[3] and (a[4] is None or b[4] is None or a[4] == b[4])

    def op(eng, cost, reads, writes, fns, **kw):
        i = len(ops)
        o = {"i": i, "eng": eng, "cost": cost, "stage": stage[0], "t": stage[1], "fns": fns, "deps": set(), "order": set(kw.pop("after", ()))}
        o.update(kw)
        writes = [a for w in writes for a in (w["parts"][:1] if "parts" in w else [w])]
        for a, wr in [(a, 0) for a in flat(reads)] + [(a, 1) for a in writes]:
            key = BANK.get(a["name"], a["name"])
            me = (i, wr, a["lo"], a["hi"], a["lane"], a["name"])
            old = hist.setdefault(key, [])
            if a["psum"] and eng == "P":
                if key in o["opens"]:
                    for e in old:
                        if e[0] != i:
                            o["order" if ops[e[0]]["eng"] == "P" else "deps"].add(e[0])
                    hist[key] = [me]
                else:
                    o["order"].add(old[0][0])
                    assert all(ops[e[0]]["eng"] == "P" for e in old if e[0] != i)
                    old.append(me)
                continue
            keep = []
            for e in old:
                if e[0] != i:
                    if a["psum"] and (ops[e[0]]["eng"] != eng or len(eng) > 1):
                        o["deps"].add(e[0])
                    elif (wr or e[1]) and hit(me, e):
                        o["deps"].add(e[0])
                        if wr and a["lane"] is None and not a["psum"] and a["lo"] <= e[2] and e[3] <= a["hi"]:
                            continue
                keep.append(e)
            keep.append(me)
            hist[key] = keep
        ops.append(o)
        return i

    def cyc(n, half):
        return max(64, n * (0.5 if half else 1)) * CYC + CFG["VO"]

    def tt(out, a, b, o):
        rd = [a, b]
        if "ind" in out:
            c = 50 + out["n"] * CFG["SC"] * CYC
            rd.append(out["parts"][1])
        elif "ind" in a:
            c = 50 + a["n"] * GC * CYC
        else:
            c = cyc(a["n"], False) if (a["psum"] or b["psum"]) else cyc(2 * a["n"], False)
        return op("V", c, rd, [out], [lambda: V.tensor_tensor(out["ap"], a["ap"], b["ap"], o)])

    def raw(x):
        return x["ap"] if isinstance(x, dict) else x

    def tsf(out, a, s1, o1, s2=None, o2=None):
        def f():
            if o2 is None:
                return V.tensor_scalar(out["ap"], a["ap"], raw(s1), None, o1)
            return V.tensor_scalar(out["ap"], a["ap"], raw(s1), raw(s2), o1, o2)
        return f

    def ts(out, a, s1, o1, s2=None, o2=None):
        return op("V", cyc(a["n"], a["two"] and out["two"]), [a, s1, s2], [out], [tsf(out, a, s1, o1, s2, o2)])

    def cp(out, a):
        c = 50 + a["n"] * GC * CYC if "ind" in a else cyc(a["n"], a["two"] and out["two"])
        return op("V", c, [a], [out], [lambda: V.tensor_copy(out["ap"], a["ap"])])

    def fill(out, x):
        return op("V", cyc(out["n"], out["two"]), [], [out], [lambda: V.memset(out["ap"], x)])

    def scan(out, d0, d1, o0, o1, first=0.0):
        return op("V", cyc(d0["n"], False), [d0, d1], [out], [lambda: V.tensor_tensor_scan(out["ap"], d0["ap"], d1["ap"], first, o0, o1)])

    def act(out, a, f, **kw):
        c = (65 + a["n"] * GC * CYC) if "ind" in a else a["n"] * CYC + CFG["SO"]
        wr = [out] + ([kw["accum_out"]] if "accum_out" in kw else [])
        return op("S", c, [a] + [x for k, x in kw.items() if k != "accum_out"], wr,
                  [lambda: S.activation(out["ap"], a["ap"], f, **{k: raw(x) for k, x in kw.items()})])

    def either(out, a, add=None, mul=None, relu=False):
        k = "ind" in a
        cv = 50 + a["n"] * GC * CYC if k else cyc(a["n"], a["two"] and out["two"])
        cs = 65 + a["n"] * GC * CYC if k else a["n"] * CYC + CFG["SO"]
        if relu:
            fs, fv = (lambda: S.activation(out["ap"], a["ap"], AF.Relu)), tsf(out, a, 0.0, OP.max)
        elif mul is not None:
            fs, fv = (lambda: S.activation(out["ap"], a["ap"], AF.Identity, bias=raw(add), scale=mul)), tsf(out, a, mul, OP.mult, add, OP.add)
        elif add is not None:
            fs = lambda: S.activation(out["ap"], a["ap"], AF.Identity if isinstance(add, dict) else AF.Copy, bias=raw(add))
            fv = tsf(out, a, add, OP.add)
        else:
            fs, fv = (lambda: S.activation(out["ap"], a["ap"], AF.Copy)), (lambda: V.tensor_copy(out["ap"], a["ap"]))
        return op("VS", cv, [a, add], [out], [fs], costs={"V": cv, "S": cs}, alt={"V": fv, "S": fs})

    def anyone(out, a, by):
        n = a["n"]
        fn = {"G": lambda: g.affine_select(out["ap"], a["ap"], [[0, n]], OP.is_ge, 0.0, 0, 0),
              "V": lambda: V.tensor_copy(out["ap"], a["ap"]), "S": lambda: S.activation(out["ap"], a["ap"], AF.Copy)}
        c = {"G": 170 + 2 * n * CYC, "V": cyc(n, a["two"] and out["two"]), "S": n * CYC + CFG["SO"]}
        if len(by) == 1:
            return op(by, c[by], [a], [out], [fn[by]])
        return op(by, c[by[0]], [a], [out], [fn[by[0]]], costs={e: c[e] for e in by}, alt=fn)

    def pe(*mms):
        c = sum(max(64, m[2]["n"]) * CFG["PE"] * (1 if m[1]["two"] else 4) + CFG["PO"] for m in mms)
        return op("P", c, [x for m in mms for x in (m[1], m[2])], [m[0] for m in mms],
                  [(lambda m=m: P.matmul(m[0]["ap"], m[1]["ap"], m[2]["ap"], m[3], m[4])) for m in mms],
                  opens={BANK[m[0]["name"]] for m in mms if m[3]}, mms=mms)

    def acc(*mms, new=False):
        mms = [list(m) + [new and j == 0, False] for j, m in enumerate(mms)]
        for j in range(0, len(mms), CFG["MM"]):
            pe(*mms[j:j + CFG["MM"]])

    def iota(out, pat, base, cm, small=False):
        def f():
            if small:
                return g.iota(out["ap"], pat, base, cm, allow_small_or_imprecise_dtypes=True)
            return g.iota(out["ap"], pat, base, cm)
        return op("G", 130 + 2 * out["n"] * CYC, [], [out], [f])

    def select(out, a, pat, o, x, base, cm):
        return op("G", 170 + 2 * out["n"] * CYC, [a], [out], [lambda: g.affine_select(out["ap"], a["ap"], pat, o, x, base, cm)])

    def gcopy(out, a):
        return select(out, a, [[0, out["n"]]], OP.is_ge, 0.0, 0, 0)

    def dma(q, out, a, reads=(), writes=(), cost=2500):
        k = ndma[0]
        ndma[0] += 1
        f = {"Y": lambda: g.sync.dma_start(out, a), "S": lambda: S.dma_start(out, a)}[q]
        latest[q] = [op(q, 60, list(reads), list(writes), [f], dmasem="ld%d" % k, lat=cost, after=latest.get(q, ()))]

    def send(items, sem, dsts=None, more=0.0):
        dsts = dsts or [T.cores[(rank + STEP) % N]] * len(items)
        at, tr = 0, []
        for it, d in zip(items, dsts):
            tr.append((it, topo.addr(d), sum(1 << e for e in topo.engines(core, d)[at:at + it[2]])))
            at += it[2]

        def f():
            g.remote_dma_fused([RemoteDMATransfer(dst_ids=[DstId(rid=ad[0], pnc=ad[1])], dma_engine_mask=mk, remote_sem=T.sem[sem[j % len(sem)]],
                                                  src=it[0]["ap"], dst=it[1]["ap"]) for j, (it, ad, mk) in enumerate(tr)], local_sem=T.sem["snt"])
        s = op("G", CFG["SEND"], [it[0] for it in items], [], [f], remote=at)
        for j, sm in enumerate(sem):
            mine = [it for q, it in enumerate(items) if q % len(sem) == j]
            op("R", 0, [], [it[1] for it in mine], [], arr=(sm, sum(it[2] for it in mine)), after=[s], pre=CFG["LAT"] + more)

    IN = [slice(HM, M), slice(0, HM)]
    GS = CFG["GS"]
    SIDE = [slice(0, 64), slice(64, 128)]
    for q, name, src, c in (("Y", "LI", "l0", 2200), ("Y", "XW_0", "xt", CFG["LD"][0]), ("S", "ZI", "z0", 2500), ("S", "THI", "th", 9000),
                            ("Y", "RI_0", "ex", CFG["LD"][1])) if not GS else ():
        dma(q, v(name)["ap"], T[src][:], writes=[v(name)], cost=c)

    def load(q, name, cs, src, h, both, cost):
        for s in range(2):
            x = dict(v(name, SIDE[s], cs), lane=s)
            dma(q, x["ap"], T[src][SIDE[h], full if both else IN[s]], writes=[x], cost=cost)
    if GS:
        IN = IN[::-1]
        for h in range(2):
            load("S", "LI", IN[h], "l0", h, False, 2200)
            load("Y", "XW_%d" % h, full, "xt", h, True, CFG["LD"][2 * h])
            load("S", "ZI", IN[h], "z0", h, False, 2500)
            load("Y", "RI_%d" % h, full, "ex", h, True, CFG["LD"][2 * h + 1])
        dma("S", v("THI")["ap"], T["th"][:], writes=[v("THI")])

    def hc(name, h, lo=0, hi=None, st=1):
        n = "%s_%d" % (name, h if GS or name not in ("XW", "RI", "RW") else 0)
        return cols(n, lo, hi if hi else WHAT[n][1][1], st)

    def cn(t, h, j):
        x = 4 * t + 2 * h * GS + j
        return cols("CN", x, x + 1)

    def lf(t, h, lo=0, hi=HM):
        return cols("LF%d" % t, LW * h + lo, LW * h + hi)

    def zb(t, h):
        return cols("ZB%d" % t, LW * h, LW * h + HM) if t else v("ZI", full, IN[h])

    one, two, row = slice(0, 1), slice(0, 33), slice(32, 33)
    iota(v("IC"), [[-1, 128]], 0, 1)
    iota(v("IB"), [[-16, 8], [0, 16]], 0, 1)
    iota(v("IA"), [[0, 8], [-1, 16]], 16, 1)
    for h in range(2):
        cp(lf(0, h), v("LI", full, IN[h]))
        ts(hc("LC", h), v("LI", full, IN[h]), -CEN, OP.add)
    ts(v("Ib"), v("IC"), 0, OP.is_equal)
    for n, x in (("NIb", -1.0), ("NI", -GATE), ("HIb", 0.5), ("AI", APART)):
        either(v(n), v("Ib"), 0.0, x)
    for n, x in (("Ih", 1.0), ("NIh", -1.0)):
        ts(v(n), v("Ib"), x, OP.mult)
    ts(v("IA"), v("IA"), 15, OP.bitwise_and)
    ts(v("DELTA"), v("IA"), 0, OP.is_equal)
    ts(col(CP0), cols("IA", 0, 1), 0, OP.is_equal)
    ts(v("IB"), v("IB"), 4, OP.arith_shift_right)
    ts(v("BOb"), v("IB"), 0, OP.is_equal)
    for n, x in (("BOh", 1.0), ("NBOh", -1.0)):
        ts(v(n), v("BOb"), x, OP.mult)
    for n, x in (("NBOb", -1.0), ("BO2", 2.0)):
        either(v(n), v("BOb"), 0.0, x)
    ts(v("SEL0"), v("BOb"), col(CP0), OP.mult)
    for o, x in ((v("BLK"), 16.0), (v("BLKC"), CONF), (cols("BLK2", 0, 8), 32.0), (cols("BLK2", 8, 16), -16.0)):
        either(o, cols("BOb", 0, 128, 16), 0.0, x)
    fill(v("SELA"), 0.0)
    cp(cols("SELA", 15, 143, 16), cols("BOb", 0, 128, 16))
    fill(v("ONb"), 1.0)
    for h in range(2):
        acc((cols("U_0", HM * h, HM * h + HM), v("SEL0"), hc("LC", h)), new=True)
    act(v("L0B0"), cols("U_0", 0, M), AF.Copy, bias=CEN)
    send([(v("L0B0"), v("L0B%d" % t), 4 if t == 1 else 2) for t in range(1, TV)], ["l0%d" % t for t in range(1, TV)],
         [T.cores[(rank + STEP * t) % N] for t in range(1, TV)], 7000.0)
    for h in range(2):
        for k in range(16):
            anyone(cols("L0R0", 2048 * h + k, 2048 * h + 2048, 16), cols("L0B0", HM * h, HM * h + HM), "GSV")
    anyone(cols("L0R1", 0, 4096, 16), v("L0B0"), "GSV")
    iota(v("GI"), [[-32768, 8], [0, 16]], 0, 0, True)
    iota(v("KI"), [[0, 8], [1, 16]], 65536, 0, True)
    fill(v("CK", slice(0, 64)), 0.0)
    ts(v("CK", one, slice(0, 128)), v("KI", one), -65536.0, OP.add)
    ts(v("CK", one, slice(128, 256)), v("KI", one), -1.0, OP.mult, 65552.0, OP.add)
    fill(v("CK", one, slice(0, 128, 16)), GATE)
    fill(v("CK", one, slice(128, 256, 16)), 0.0)
    fill(v("CK", one, slice(256, 384)), -0.25)
    fill(v("CK", one, slice(384, 385)), -31.5)
    ts(v("CK", row, slice(0, 128)), v("GI", row), 4.0, OP.mult)
    ts(v("CK", row, slice(128, 256)), v("GI", row), -4.0, OP.mult)
    ts(v("GI"), v("GI"), 4.0, OP.mult)
    tt(v("CC1"), v("GI"), v("KI"), OP.add)
    ts(cols("CC1", 0, 128, 16), cols("CC1", 0, 128, 16), 65536.0, OP.add)
    iota(v("IQ"), [[16, 16]], 15, 0, True)
    cp(v("BC"), v("IQ"))
    ts(v("BS"), v("IQ"), -15.0, OP.add, 1.0 / 16, OP.mult)
    for h in range(2):
        fill(hc("M2", h, 0, 1), BIG)
        fill(hc("MG", h, 0, 1), 0.0)
        fill(hc("QE", h, 0, 1), 1.0)
    fill(v("EO", one), 0.0)
    fill(v("EO", one, slice(0, 128, 16)), 1.0)
    iota(v("CKE", one), [[0, 16], [1, 16]], 0, 0, True)
    fill(v("RMAX"), 1.0)
    fill(v("RMIN"), -BIG)
    fill(cols("RMIN", 0, 256, 16), BIG)
    for h in range(2):
        if CFG["HORN"][h]:
            fill(dict(hc("MK", h, 0, 512, 4), lane=0), 0.0)
    if not all(CFG["HORN"]):
        iota(v("LO4"), [[0, 512]], -int(BIG), 0, True)
        select(v("R4"), v("LO4"), [[0, 128], [1, 4]], OP.not_equal, BIG, 0, 0)
        fill(v("RP", one), 0.0)
        fill(v("RP", one, slice(0, 512, 4)), GATE)
        fill(v("RP", one, slice(1, 512, 4)), GATE)
        ts(v("PI"), v("Ib"), GATE, OP.mult)
    iota(v("IP"), [[0, 1]], 0, 1)
    ts(v("IP"), v("IP"), 15, OP.bitwise_and)
    for r in range(2):
        ts(col(CDUM + r), v("IP"), W + 16.0 * r, OP.add)
        x = 4096.0 if GS else 1.0
        ts(col(CWIN + r), v("IP"), 2.0 * x, OP.mult, (32.0 * r - 30.0 + CEN / 4096) * x, OP.add)
    cp(col(CRN), v("IP"))
    iota(v("J2"), [[-16, 2], [0, 4], [1, 32]], 0, 0, True)
    ts(v("TR2"), v("J2"), col(CRN), OP.is_gt, RIV, OP.mult)
    ts(v("R32"), v("J2"), col(CRN), OP.is_equal, -2.0, OP.mult)
    ts(v("R32"), v("R32"), 1.0, OP.add)
    fill(cols("R32", 0, 256, 32), 0.0)
    iota(v("J3"), [[0, 256]], -1, 0, True)
    select(v("NB2"), v("J3"), [[-16, 2], [-32, 4], [0, 32]], OP.is_ge, 0.0, 0, 1)
    select(v("NB2"), v("NB2"), [[16, 2], [32, 4], [0, 32]], OP.is_ge, 0.0, 15, -1)
    ts(col(CP1), v("IP"), 1, OP.is_equal)
    ts(v("O32"), v("ONb"), col(CP1), OP.mult, 0.5, OP.mult)
    iota(v("ID"), [[-1, 132]], 512, 1)
    ts(v("ID"), v("ID"), 15, OP.bitwise_and)
    ts(v("SB"), v("ID"), 0, OP.is_equal)
    ts(v("NSB"), v("ID"), 0, OP.not_equal)
    iota(v("IG"), [[0, 2], [1, 4], [0, 16]] if GS else [[1, 8], [0, 16]], 0, -1)
    ts(v("THH"), v("THI"), -TCEN, OP.add)
    ts(col(CTM), col(CP0), -60000.0, OP.mult, 30000.0, OP.add)
    for h in range(1 + GS):
        ts(v("GB8_%d" % h), v("IG"), -4 * h, OP.is_equal)
        acc((hc("W", 1, h, h + 1), v("GB8_%d" % h), v("THH")), new=not h)
    for h in range(1 + GS):
        ts(col(CTH + 2 * h), hc("W", 1, h, h + 1), TCEN + 31.0, OP.add)
        ts(col(CTH + 2 * h + 1), hc("W", 1, h, h + 1), TCEN + 31.0, OP.add, col(CTM), OP.min)
    ts(cols("CN", 0, 2 + 2 * GS), cols("COLS", CTH, CTH + 2 + 2 * GS), -31.5, OP.add)
    if GS:
        iota(v("ONN"), [[0, 128]], -4096, 0, True)
        for s in range(2):
            select(hc("DUP", s), v("ONb"), [[0, 2], [-1, 64]], OP.is_equal, 0.0, -64 * s, 1)
            select(hc("DUN", s), v("ONN"), [[0, 2], [-1, 64]], OP.is_equal, 0.0, -64 * s, 1)
            select(hc("SD", s), v("ONb"), [[0, 2], [-16, 4], [0, 16]], OP.is_equal, 0.0, -64 * s, 1)
    for h in range(1 + GS):
        stage[0] = "rw%d" % h
        for q in range(4):
            anyone(hc("RW", h, 640 * q, 640 * q + 640), hc("RI", h, 640 * q, 640 * q + 640), "GV")

    def table(t, h):
        return hc("RW", h, 0, W) if t else hc("RI", h)

    def pieces(n):
        return [(HM * q // n, HM * (q + 1) // n) for q in range(n)]

    def reps(t):
        for k in range(1, 16):
            anyone(cols("L0R%d" % (t % 2), k, 4096, 16), v("L0B%d" % t), CFG["ZBY"][2])

    def gather(h, off, G):
        for a, b in pieces(CFG["XP"]):
            either(hc(G, h, 16 * a, 16 * b), ind(hc("XW", h), off(a, b)))

    def banks(h, which):
        return [{"o": "D%d" % h, "x": "D%d" % (1 - h), "0": "D0", "1": "D1"}.get(c, "%s_%d" % (c, h)) for c in which]

    def sizes(h, which, four):
        for c, bank in enumerate(banks(h, which)):
            if four:
                acc(*[(cols(bank, r, 512, 4), v("NIb"), hc("Z4", h, 128 * c, 128 * c + 128)) for r in range(4)], new=True)
            else:
                acc((v(bank), v("NIb"), hc("ZR", h, 512 * c, 512 * c + 512)), new=True)
            acc((v(bank), v("Ib"), hc("GA", h, 512 * c, 512 * c + 512)))
            act(hc("DA", h, 512 * c, 512 * c + 512), v(bank), AF.Abs)

    def phase1x(t, h):
        if t:
            ts(hc("LC", h), lf(t, h), -CEN, OP.add)
        acc((hc("W", h, 256, 384), v("ONb", two), v("CK", two, slice(128, 256))), new=True)
        gather(h, lambda a, b: lf(t, h, a, b), "GA")
        if CFG["P1"][h]:
            sizes(h, CFG["B1"], True)
            for o, at in (("K", 0), ("W", 256)):
                acc(*[(hc(o, h, at + k, at + 128, 16), hc("DA", h, k, 2048, 16), v("BLK")) for k in range(1, 16)])
            return
        for c in range(4):
            bank = banks(h, CFG["B1"])[c]
            ks = [k for k in range(4 * c, 4 * c + 4) if k]
            for k in ks:
                o = cols(bank, 128 * (k % 4), 128 * (k % 4) + 128)
                acc((o, v("Ib"), hc("GA", h, k, 2048, 16)), (o, v("NIb"), zb(t, h)), new=True)
            lo, hi = ks[0], ks[-1] + 1
            act(hc("DA", h, 128 * lo, 128 * hi), cols(bank, 128 * (lo % 4), 128 * (hi - 4 * c)), AF.Abs)
            for o, at in (("K", 0), ("W", 256)):
                acc(*[(hc(o, h, at + k, at + 128, 16), hc("DA", h, 128 * k, 128 * k + 128), v("BLK")) for k in ks])

    def phase1r(t, h):
        for a, b in pieces(CFG["RP"]):
            tt(hc("CF", h, 16 * a, 16 * b), ind(table(t, h), lf(t, h, a, b)),
               cols("L0R%d" % (t % 2), 2048 * h + 16 * a, 2048 * h + 16 * b), OP.is_equal)
        acc(*[(hc("K", h, k, 128, 16), hc("CF", h, k, 2048, 16), v("BLKC")) for k in range(1, 16)])

    def last(h, name, n=8):
        return ind(hc(name, h), cols("BC", 0, n))

    def lists(o, src):
        acc(*[(o, cols("SELA", 15 - a, 143 - a), cols(src, a, 256, 16)) for a in range(16)], new=True)

    def near(t, h):
        key = hc("K", h, 0, 128)
        scan(hc("M1", h), v("CC1"), key, OP.min, OP.min, BIG)
        tt(hc("KEY", h), key, v("CC1"), OP.min)
        scan(hc("M2", h, 1, 128), hc("KEY", h, 1, 128), hc("M1", h, 0, 127), OP.min, OP.max, BIG)
        for l in range(2):
            o = hc("OAB", h, 128 * l, 128 * l + 128)
            tt(o, last(h, "M%d" % (l + 1)), hc("KEY", h), OP.is_equal)
            acc((hc("U", h, 128 * l, 128 * l + 128), o, v("Ib")), new=not l)
        for l in range(2):
            tt(hc("OL", h, 128 * l, 128 * l + 128), hc("U", h, 128 * l, 128 * l + 128), hc("LC", h), OP.mult)
        lists(hc("K", h, 256, 272), "OL_%d" % h)
        ts(hc("LOF", h), hc("K", h, 256, 272), CEN, OP.add)
        for a, b in ((0, 8), (8, 16)) if CFG["EU2"] else ((0, 16),):
            cp(hc("EU", h, 16 * a, 16 * b), ind(table(t, h), hc("LOF", h, a, b)))
        ts(hc("EC", h), hc("EU", h), -CEN, OP.add)

    def far(t, h):
        key = hc("W", h, 256, 384)
        acc(*[(key, v("NI"), hc("OAB", h, 128 * l, 128 * l + 128)) for l in range(2)])
        either(hc("KF", h), key)
        scan(hc("MF", h), v("RMAX"), hc("KF", h), OP.mult, OP.max)
        tt(hc("FF", h, 0, 128), last(h, "MF"), hc("KF", h), OP.is_equal)
        scan(hc("MG", h, 1, 128), hc("KF", h, 1, 128), hc("MF", h, 0, 127), OP.max, OP.min, -BIG)
        tt(hc("FF", h, 128, 256), last(h, "MG"), hc("KF", h), OP.is_equal)

    def rivals(t, h):
        ola, o, d = hc("OL", h, 0, 128), hc("U", h, 256, 384), hc("K", h, 0, 256)
        for r in range(2 - 2 * GS):
            either(hc("LAF", h, 4 * r, 4 * r + 4), hc("K", h, 256 + r, 264, 2), col(CWIN + r), 1.0 / 4096)
        if GS:
            ts(hc("LAH", h), hc("LOF", h, 0, 8), -CEN, OP.add)
        acc((o, ola, v("BOh")), new=True)
        tt(hc("LTD", h), o, v("DELTA"), OP.mult)
        acc((d, v("Ib"), v("TR2")), (d, hc("LTD", h), v("NB2")),
            *[(hc("K", h, 128 * r, 128 * r + 128), v("BOh"), ola) for r in range(2)], new=True)
        act(hc("AD", h), d, AF.Abs)
        acc((hc("K", h, 256, 512), v("AI"), hc("AD", h)), new=True)
        if t and (GS or not h):
            for j in range(2):
                either(cn(t, h, j), cols("CNi", 4 * t, 4 * t + 1), col(CTH + 2 * h + j))
        if GS:
            mm = []
            for s in range(2):
                for at, x, y, z in ((0, "DUP", hc("EC", h, 0, 128), "SB"), (256, "SD", hc("LC", h), "NSB")):
                    o = hc("U", h, at + 128 * s, at + 128 * s + 128)
                    mm += [(o, hc(x, s), y), (o, v("NI"), cols(z, t, t + 128))]
            acc(*mm, new=True)
            either(hc("NW", h), hc("U", h), CEN)
            return
        acc((o, v("Ih"), hc("EC", h, 0, 128)), (o, v("NI"), cols("SB", t, t + 128)), new=True)
        o = hc("U", h, 384, 512)
        acc((o, v("SEL0"), hc("LC", h)), (o, v("NI"), cols("NSB", t, t + 128)))
        either(hc("NW", h, 0, 256), hc("U", h, 256, 512), CEN)

    def phase2g(t, h):
        gather(h, lambda a, b: hc("EU", h, a, b), "GA")

    def spread(t, h):
        for k in range(4):
            anyone(dict(hc("Z4", h, k, 512, 4), lane=k), zb(t, h), CFG["ZBY"][0])
        for k in range(4):
            anyone(dict(hc("ZR", h, k, 2048, 4), lane=k), hc("Z4", h), CFG["ZBY"][1])

    def phase2(t, h):
        acc((hc("W", h, 0, 256), v("ONb", one), v("CKE", one)), new=True)
        sizes(h, CFG["B2"], False)
        acc(*[(hc("W", h, k, 128, 16), hc("DA", h, k, 2048, 16), v("BLK")) for k in range(16)])
        for a, b in pieces(CFG["VP"]):
            x = hc("GB", h, 16 * a, 16 * b)
            tt(x, ind(hc("XW", h), hc("EU", h, 128 + a, 128 + b)), hc("ZR", h, 16 * a, 16 * b), OP.subtract)
            either(hc("DB", h, 16 * a, 16 * b), x, relu=True)
        for G, at in (("GB", 8), ("DB", 0)):
            acc(*[(hc("W", h, 128 + k, 256, 16), hc(G, h, k, 2048, 16), cols("BLK2", at, at + 8)) for k in range(16)])

    def pick(t, h):
        u = [hc("U", h, 128 * l, 128 * l + 128) for l in range(2)]
        acc(*[(o, v("EO", one), v("ONb", one)) for o in u], new=True)
        scan(hc("ME", h), v("RMIN"), hc("W", h, 0, 256), OP.max, OP.min)
        cp(hc("ML", h), hc("ME", h, 15, 256, 16))
        tt(hc("QE", h, 1, 257), ind(hc("ML", h), v("BS")), hc("ME", h), OP.is_equal)
        for l, o in enumerate(u):
            acc((o, hc("QE", h, 128 * l + 1, 128 * l + 129), v("Ib")), (o, hc("QE", h, 128 * l, 128 * l + 128), v("NIb")))
        tt(hc("OEE", h), hc("U", h, 0, 256), hc("EC", h), OP.mult)
        lists(hc("U", h, 256, 272), "OEE_%d" % h)
        ts(hc("LEF", h), hc("U", h, 256, 272), CEN, OP.add)
        xa, xb, ae = hc("XE", h, 0, 128), hc("XE", h, 128, 256), hc("AE", h)
        nat, o = hc("W", h, 128, 256), cols(banks(h, CFG["BZ"])[0], 384, 512)
        riv = [hc("K", h, 256, 384), hc("K", h, 384, 512)]
        cp(xb, ind(hc("XW", h), hc("LEF", h, 8, 16)))
        if CFG["XD"][h] == 2:
            either(xa, ind(hc("XW", h), hc("LEF", h, 0, 8)))
            tt(ae, ind(hc("XW", h), hc("LEF", h, 0, 8)), xb, OP.max)
            acc((nat, v("NBOb"), xb), new=True)
            acc(*[(x, v("NBOb"), xb) for x in riv])
            acc(*[(x, v("NBOb"), xa) for x in riv + [nat]])
        else:
            tt(xa, ind(hc("XW", h), hc("LEF", h, 0, 8)), xb, OP.subtract)
            ts(ae, xa, 0.0, OP.max)
            acc((nat, v("NBOb"), xa), new=True)
            acc(*[(x, v("NBOb"), xa) for x in riv])
        acc((o, v("ONb", one), v("CK", one, slice(256, 384))), (o, v("HIb" if CFG["XD"][h] == 2 else "Ib"), xb), new=CFG["BZ"] != "W")
        acc((o, v("HIb"), xa))
        acc((nat, v("BO2"), ae))
        acc(*[(x, v("BO2"), ae) for x in riv])
        if CFG["HORN"][h]:
            ts(dict(hc("MK", h, 3, 512, 4), lane=3), nat, cn(t, h, 1), OP.is_ge)
        else:
            act(hc("SG", h), nat, AF.Sign, scale=-1.0, bias=cn(t, h, 1), accum_out=cols("AC", h, h + 1))
        act(hc("SN", h), hc("K", h, 256, 512), AF.Sign, scale=-1.0, bias=cn(t, h, 0))
        zo = cols("ZBo%d" % t, LW * h, LW * h + HM) if t < TV - 1 else v("ZY", full, IN[h])
        if CFG["ZS"][h]:
            ts(zo, o, MAGIC, OP.add, -MAGIC, OP.add)
        else:
            act(hc("ZT", h), o, AF.Copy, bias=MAGIC)
            act(zo, hc("ZT", h), AF.Copy, bias=-MAGIC)
        if t < TV - 1 and CFG["HORN"][h]:
            act(hc("SG", h), nat, AF.Sign, scale=-1.0, bias=cn(t, h, 1), accum_out=cols("AC", h, h + 1))

    def marks(t, h):
        if not CFG["HORN"][h]:
            return
        o = [cols(banks(h, CFG["BF"])[0], 128 * l, 128 * l + 128) for l in range(2)]
        f = [hc("FF", h, 128 * l, 128 * l + 128) for l in range(2)]
        acc((o[0], f[0], v("Ib")), (o[1], f[0], v("Ib")), (o[1], f[1], v("Ib")), new=True)
        for l in range(2):
            either(dict(hc("MK", h, 1 + l, 512, 4), lane=1 + l), o[l])

    def rows(t, h):
        c = [hc("U", h, j, 512, 4) for j in range(4)]
        if not CFG["HORN"][h]:
            mm = [(hc("U", h), v("ONb", one), v("RP", one)), (c[2], v("Ih"), hc("LC", h)), (c[3], v("Ih"), hc("EC", h, 128, 256))]
            for l in range(2):
                q = hc("FF", h, 128 * l, 128 * l + 128)
                mm += [(c[l], q, v("NI")), (c[2], q, v("PI")), (c[l], v("BOh"), hc("OEE", h, 128 * l, 128 * l + 128))]
            acc(*mm, new=True)
            acc(*[(c[j], v("NI" if j == 3 else "PI"), hc("SG", h)) for j in range(4)])
            scan(hc("NL", h), v("R4"), hc("U", h), OP.max, OP.min)
            lo = cols("LFo%d" % t, LW * h, LW * h + HM) if t < TV - 1 else v("LY", full, IN[h])
            (ts if t < TV - 1 else lambda o, a, x, _: either(o, a, x))(lo, hc("NL", h, 3, 512, 4), GATE + CEN, OP.add)
            return
        ea, eb, lc, ec = hc("OEE", h, 0, 128), hc("OEE", h, 128, 256), hc("LC", h), hc("EC", h, 128, 256)
        acc((c[0], v("BOh"), ea), (c[0], v("NBOh"), eb), (c[1], v("BOh"), eb), (c[1], v("NIh"), lc), (c[2], v("Ih"), lc),
            (c[2], v("NIh"), ec), (c[3], v("Ih"), ec), new=True)
        scan(hc("NL", h), hc("MK", h), hc("U", h), OP.mult, OP.add)
        lo = cols("LFo%d" % t, LW * h, LW * h + HM) if t < TV - 1 else v("LY", full, IN[h])
        (ts(lo, hc("NL", h, 3, 512, 4), CEN, OP.add) if t < TV - 1 else either(lo, hc("NL", h, 3, 512, 4), CEN))

    def leave(t, h):
        ls = (cols("LFo%d" % t, LW * h, LW * h + HM), lf(t + 1, h))
        zs = (cols("ZBo%d" % t, LW * h, LW * h + HM), cols("ZB%d" % (t + 1), LW * h, LW * h + HM))
        if CFG["ZSEP"][h]:
            send([zs + (8,)], ["z%d_%d" % (t + 1, h)])
            send([ls + (8,)], ["l%d_%d" % (t + 1, h)])
        else:
            send([ls + (4,), zs + (4,)], ["l%d_%d" % (t + 1, h)])
        if h:
            stage[0] = "count"
            p = cols("W_1", 0, 1)
            acc((p, v("ONb", one), v("CK", one, slice(384, 385))), *[(p, v("O32"), cols("AC", j, j + 1)) for j in range(2)], new=True)
            ts(col(CRN), p, 64 * MAGIC, OP.add, -64 * MAGIC, OP.add)
            tt(cols("CNo", 4 * t, 4 * t + 1), p, col(CRN), OP.subtract)
            send([(cols("CNo", 4 * t, 4 * t + 1), cols("CNi", 4 * t + 4, 4 * t + 5), 8)], ["n%d" % (t + 1)])

    def winners(t, h):
        if GS:
            o = [(s, r, hc("K", h, 8 * r + 4 * s, 8 * r + 4 * s + 4)) for s in range(2) for r in range(2)]
            acc(*[(x, hc("DUP", s), hc("LAH", h, r, 8, 2)) for s, r, x in o], new=True)
            scan(hc("CNB", h), v("R32"), hc("SN", h), OP.mult, OP.add)
            acc(*[(x, hc("DUN", s), hc("CNB", h, 128 * r + 31, 128 * r + 128, 32)) for s, r, x in o])
            for r in range(2):
                ts(dict(hc("SCU", h, r, 16, 2), lane=r), hc("K", h, 8 * r, 8 * r + 8), col(CWIN + r), OP.add, col(CDUM + r), OP.min)
            return
        scan(hc("CNT", h), v("R32"), hc("SN", h), OP.mult, OP.add)
        tt(hc("SCF", h), hc("LAF", h), hc("CNT", h, 31, 256, 32), OP.subtract)
        for r in range(2):
            ts(dict(hc("SCU", h, r, 8, 2), lane=r), hc("SCF", h, 4 * r, 4 * r + 4), 4096.0, OP.mult, col(CDUM + r), OP.min)

    def write(t, h):
        n = 128 + 128 * GS
        for q in range(n // 32 - 1, -1, -1):
            tt(ind(hc("RW", h), hc("SCU", h, 2 * q, 2 * q + 2)), hc("NW", h, 32 * q, 32 * q + 32), hc("NW", h, n + 32 * q, n + 32 + 32 * q), OP.max)
        if t == TV - 1 and h and not GS:
            dma("S", T["yl"][:], v("LY")["ap"], reads=[v("LY")])
            dma("S", T["yz"][:], v("ZY")["ap"], reads=[v("ZY")])
            dma("Y", T["yr"][:], hc("RW", h, 0, W)["ap"], reads=[hc("RW", h, 0, W)], cost=6000)
        if t == TV - 1 and GS:
            for s in range(2):
                for x, y in (("yl", "LY"), ("yz", "ZY")):
                    dma("Y", T[x][SIDE[h], IN[s]], v(y, SIDE[s], IN[h])["ap"], reads=[v(y, full, IN[h])])
            dma("Y", T["yr"][SIDE[h], full], v("RW_%d" % h, SIDE[0], slice(0, W))["ap"], reads=[hc("RW", h, 0, W)], cost=4000)

    def do(t, h, *parts):
        for name, part in parts:
            stage[0] = name + str(h)
            part(t, h)

    def first(t, h):
        stage[0] = "phase1x%d" % h
        acc((hc("K", h, 0, 128), v("ONb", two), v("CK", two, slice(0, 128))), new=True)
        do(t, h, ("spread", spread), *[("phase1x", phase1x), ("phase1r", phase1r)][::-1 if CFG["RFIRST"][h] and t else 1])
        if t + 1 < TV and h == 0:
            stage[0] = "reps"
            reps(t + 1)

    def second(t, h):
        do(t, h, ("near", near), ("phase2g", phase2g), ("far", far), ("rivals", rivals))

    def third(t, h):
        do(t, h, ("phase2", phase2), ("marks", marks), ("pick", pick), ("winners", winners), ("rows", rows))
        if t + 1 < TV:
            do(t, h, ("leave", leave))
        do(t, h, ("write", write))

    for t in range(TV):
        for part, h in ([(p, h) for h in range(2) for p in (first, second, third)] if GS else
                        [(p, h) for p in (first, second, third) for h in range(2)]):
            stage[1] = t
            part(t, h)

    if "order" not in ORDER:
        for a, b in CFG["AFTER"]:
            for t in range(TV):
                x = max(o["i"] for o in ops if (o["stage"], o["t"]) == (a, t))
                for o in ops[x:]:
                    if (o["stage"], o["t"]) == (b, t):
                        o["order"].add(x)
        ORDER.update(_plan(ops))
    order, who = ORDER["order"], ORDER["who"]
    closes = dict.fromkeys(BANK, True)
    for m in [m for i in order for m in ops[i].get("mms", ())][::-1]:
        m[4], closes[m[0]["name"]] = closes[m[0]["name"]], m[3]

    que = {"V": V, "S": S, "P": P, "G": g, "Y": g.sync}
    count_, known, clock, place = {}, {}, {}, {}
    sent = 0
    for pos, i in enumerate(order):
        o = ops[i]
        e = who[i]
        if "alt" in o:
            o["fns"] = [o["alt"][e]]
        place[i] = pos
        if e == "R":
            clock[i] = (o["arr"][0], o["arr"][1], {})
            count_[o["arr"][0]] = o["arr"][1]
            continue
        kn = known.setdefault(e, {})
        for d in sorted(o["deps"], key=lambda j: -place[j]):
            sem, val, snap = clock[d]
            if kn.get(sem, 0) >= val:
                continue
            que[e].wait_ge(T.sem[sem], val)
            kn[sem] = val
            for s, x in snap.items():
                kn[s] = max(kn.get(s, 0), x)
        if "remote" in o:
            o["fns"][0]()
            sent += o["remote"]
        elif "dmasem" in o:
            o["fns"][0]().then_inc(T.sem[o["dmasem"]], 16)
            clock[i] = (o["dmasem"], 16, dict(kn))
            count_[o["dmasem"]] = 16
        else:
            s = "s" + e
            for f in o["fns"]:
                f().then_inc(T.sem[s], 1)
                count_[s] = count_.get(s, 0) + 1
            clock[i] = (s, count_[s], dict(kn))
    for s, x in count_.items():
        g.wait_ge(T.sem[s], x)
    g.wait_ge(T.sem["snt"], sent)


def _after(xs, x):
    lo, hi = 0, len(xs)
    while lo < hi:
        mid = (lo + hi) // 2
        if xs[mid] > x:
            hi = mid
        else:
            lo = mid + 1
    return lo


def _lay(ops, nxt, need, key, who):
    n, need = len(ops), list(need)
    ready, start, fin, new = [dict.fromkeys(o["eng"], 0.0) for o in ops], [0.0] * n, [0.0] * n, [None] * n
    slots = {e: ([], []) for e in "VSPGY"}
    free = sorted((-key[i], i) for i in range(n) if not need[i])
    while free:
        i = free.pop()[1]
        o, best = ops[i], None
        for e in (who[i] if who else o["eng"]):
            c = o["costs"][e] if "costs" in o else o["cost"]
            at, q = ready[i][e], 0
            if e != "R":
                a, b = slots[e]
                q = _after(b, at)
                while q < len(a) and a[q] < at + c:
                    at = max(at, b[q])
                    q += 1
            late = at + c + (CFG["HELP"] * "GSV".index(e) if "costs" in o else 0)
            if best is None or late < best[0]:
                best = (late, e, at, c, q)
        _, e, at, c, q = best
        if e != "R":
            slots[e][0].insert(q, at)
            slots[e][1].insert(q, at + c)
        new[i], start[i], fin[i] = e, at, at + c
        for j, lag, near in nxt[i]:
            for x in ready[j]:
                ready[j][x] = max(ready[j][x], fin[i] + (near if x == e else lag))
            need[j] -= 1
            if not need[j]:
                free.insert(_after(free, (-key[j], j)), (-key[j], j))
    return max(fin[i] + ops[i].get("lat", 0) for i in range(n)), start, fin, new


def _relay(prv, turn, key, who, cost, lat):
    key, start, fin = list(key), [0.0] * len(key), [0.0] * len(key)
    for i in turn:
        for j, _, _ in prv[i]:
            if key[j] >= key[i]:
                key[i] = key[j] + 0.001
    slots, by = {e: ([], [], []) for e in "VSPGYR"}, [None] * len(key)
    for i in sorted(turn, key=lambda i: key[i]):
        e, at, w = who[i], 0.0, None
        c = cost[i][e]
        for j, lag, near in prv[i]:
            x = fin[j] + (near if who[j] == e else lag)
            if x > at:
                at, w = x, j
        if e != "R":
            a, b, ids = slots[e]
            q = m = len(b)
            while q and b[q - 1] > at:
                q -= 1
            while q < m and a[q] < at + c:
                if b[q] > at:
                    at, w = b[q], ~ids[q]
                q += 1
            a.insert(q, at)
            b.insert(q, at + c)
            ids.insert(q, i)
        start[i], fin[i], by[i] = at, at + c, w
    return max(x + y for x, y in zip(fin, lat)), start, fin, who, by


def _held(r, lat):
    i, out = max(range(len(lat)), key=lambda j: r[2][j] + lat[j]), []
    while r[4][i] is not None:
        j = r[4][i]
        if j < 0:
            j = ~j
            out.append((i, j))
        i = j
    return out


def _plan(ops):
    n = len(ops)
    fw, bw = [[] for _ in range(n)], [[] for _ in range(n)]
    for j, o in enumerate(ops):
        for i in sorted(o["deps"] | o["order"]):
            lag = [o.get("pre", 0) + (ops[i].get("lat", 0) + CFG[x] if i in o["deps"] else 0.0) for x in ("HOP", "SELF")]
            fw[i].append((j, *lag))
            bw[j].append((i, *lag))
    nf, nb = [len(x) for x in bw], [len(x) for x in fw]
    tail = [0.0] * n
    for i in range(n - 1, -1, -1):
        tail[i] = ops[i]["cost"] + max([tail[j] + lag for j, lag, _ in fw[i]] + [ops[i].get("lat", 0)])
    key, best, cur, seed = [-x for x in tail], None, None, [CFG["SEED"]]
    parts = sorted({o["stage"] for o in ops})

    def draw():
        seed[0] = (seed[0] * 6364136223846793005 + 1442695040888963407) % 2 ** 64
        return (seed[0] >> 11) / 2.0 ** 53
    for _ in range(CFG["PASS"]):
        r = _lay(ops, fw, nf, key, None)
        back = _lay(ops, bw, nb, [-r[2][i] - ops[i].get("lat", 0) for i in range(n)], r[3])[2]
        r = min(r, _lay(ops, fw, nf, [-x for x in back], None), key=lambda x: x[0])
        if cur is None or r[0] < cur[0] + 300:
            cur = r
        if best is None or r[0] < best[0]:
            best = r
        move = {parts[int(draw() * len(parts))]: (draw() + draw() + draw() - 1.5) * CFG["AMP"] for _ in range(1 + int(draw() * 3))}
        key = [cur[1][i] + move.get(ops[i]["stage"], 0.0) + (draw() - 0.5) * CFG["AMP"] / 20 for i in range(n)]
    like, seen, runs = {}, {}, {}
    for i, o in enumerate(ops):
        x = (o["stage"], o["t"])
        seen[x] = seen.get(x, 0) + 1
        like.setdefault((o["stage"], seen[x]), []).append(i)
    for x in like:
        runs.setdefault(x[0], []).append(like[x])
    both = [x for x in like.values() if all("costs" in ops[i] for i in x)]
    cur, up, lat = best, list(range(n)), [o.get("lat", 0) for o in ops]
    cost = [o.get("costs") or {o["eng"]: o["cost"]} for o in ops]
    kin = {i: x for x in like.values() for i in x}

    def other(i, who):
        x = ops[i]["eng"].replace(who[i], "")
        return x[int(draw() * len(x))]
    cur = best = _relay(bw, up, cur[1], cur[3], cost, lat)
    held = _held(cur, lat)
    for it in range(CFG["FINE"]):
        key, who, u = list(cur[1]), cur[3], draw()
        if it % 50 == 49:
            key = [-x for x in _relay(fw, up[::-1], [-x - y for x, y in zip(cur[2], lat)], who, cost, lat)[2]]
        elif u > 1 - CFG["CRIT"] and held:
            i, j = held[int(draw() * len(held))]
            how, same = draw(), draw() < CFG["SAME"]
            far = (0, 0, 300, 1000)[int(draw() * 4)]
            if how < 0.25 and ("costs" in ops[i] or "costs" in ops[j]):
                x = i if "costs" in ops[i] and ("costs" not in ops[j] or draw() < 0.5) else j
                who, e = list(who), other(x, who)
                for y in (kin[x] if same else [x]):
                    if e in ops[y].get("costs", ""):
                        who[y] = e
            elif how < 0.6:
                for y in (kin[i] if same else [i]):
                    key[y] -= cur[1][i] - cur[1][j] + 1 + far
            else:
                for y in (kin[j] if same else [j]):
                    key[y] += cur[1][i] - cur[1][j] + 1 + far
        elif u < 0.2 * (1 - CFG["CRIT"]):
            x = both[int(draw() * len(both))]
            who, e = list(who), other(x[-1], who)
            for i in (x if draw() < 0.7 else [x[int(draw() * len(x))]]):
                if e in ops[i]["costs"]:
                    who[i] = e
        else:
            run = runs[parts[int(draw() * len(parts))]]
            a = int(draw() * len(run)) if draw() < 0.7 else 0
            d = (draw() + draw() + draw() - 1.5) * (600, 2000, 6000)[int(draw() * 3)]
            t = int(draw() * TV) if draw() < 0.4 else None
            for x in run[a:a + (1, 2, 4, 8, 99)[int(draw() * 5)]]:
                for i in x:
                    if t is None or ops[i]["t"] == t:
                        key[i] += d
        r = _relay(bw, up, key, who, cost, lat)
        if r[0] - cur[0] + CFG["MEAN"] * (sum(r[2]) - sum(cur[2])) / n < CFG["TEMP"] * (1 - it / CFG["FINE"]) * draw() ** 2:
            cur, held = r, _held(r, lat)
            best = min(best, r, key=lambda x: x[0])
    end, start, fin, who, _ = best
    order = sorted(range(n), key=lambda i: (start[i], i))
    return {"order": order, "who": who, "plan": [(start[i], fin[i], who[i], i) for i in order], "ops": ops, "end": end}
